import numpy as np, ml_dtypes
CORES = [83,85,87,115,117,119]
N = 6
BF = ml_dtypes.bfloat16
C, V, VX, STEPS = 512, 2048, 4096, 4
def parts(rng):
    x = rng.integers(0, 32, (N, 8, 16, VX), dtype=np.int32); rb = rng.integers(0, V, (N, 8, 16, V), dtype=np.int32)
    a = rng.integers(0, V, (N, 8, 16, C), dtype=np.int32); h = rng.integers(0, 32, (N, 8, 16, C), dtype=np.int32)
    th = rng.integers(80, 135, (N, 8, 16, 1)) + rng.integers(-12, 13, (N, 8, 1, 1)); w = rng.integers(0, 256, (N, 8, 16, 1))
    return x, rb, a, h, th, w
def pack(x, rb, a, h, th, w):
    return {"cues": x.reshape(N, 128, VX).astype(np.float32).astype(BF), "spare": rb.reshape(N, 128, V).astype(np.int32), "scroll": a.reshape(N, 128, C).astype(np.int32),
            "heard": h.reshape(N, 128, C).astype(np.float32).astype(BF), "th": th.reshape(N, 128, 1).astype(np.int32), "w": w.reshape(N, 128, 1).astype(np.int32)}
def setup_inputs(rng):
    return pack(*parts(rng))
def setup_inputs_corners(rng):
    x, rb, a, h, th, w = parts(rng); lane = np.arange(16).reshape(1, 1, 16, 1); n = np.arange(V); c = np.arange(C)
    u = rng.random((N, 8, 1, VX)); x = np.where(u < 0.1, 0, np.where(u < 0.2, 31, x)); u = rng.random((N, 8, 1, C)); h = np.where(u < 0.1, 0, np.where(u < 0.2, 31, h))
    rb = np.choose(rng.integers(0, 5, rb.shape), [0, V - 1, n, (n + 1) % V, rb]); a = np.choose(rng.integers(0, 5, a.shape), [0, V - 1, c, V - C + c, a])
    kd = np.argsort(rng.random((N, 8)), axis=1).reshape(N, 8, 1, 1); j = rng.integers(0, 16, (N, 8, 1, 1)); mid = rng.integers(80, 135, (N, 8, 16, 1))
    th = np.choose(kd, [496, 496 * (lane == 15), 0, 496 * (lane == j), mid, 496 * (lane % 2), mid, mid]); w = np.where(kd == 6, 255, np.where(kd == 7, 0, w))
    q = rng.permutation(N); th[q[0]] = 496; th[q[1]] = 0
    return pack(x, rb, a, h, th, w)
def setup_inputs_ends(rng):
    def two(hi, *shape): return np.where(rng.random(shape) < 0.5, hi, 0)
    lane = np.arange(16).reshape(1, 1, 16, 1)
    u = rng.random((N, 8, 1, VX)); u[..., 1] = 1.0; u[..., V - 2] = 1.0; x = np.where(u < 0.3, 0, np.where(u < 0.6, 31, two(31, N, 8, 16, VX)))
    u = rng.random((N, 8, 1, C)); h = np.where(u < 0.25, 0, np.where(u < 0.5, 31, two(31, N, 8, 16, C)))
    rb = two(V - 1, N, 8, 16, V); u = rng.random((N, 8, 1, V)); rb = np.where(u < 0.1, 0, np.where(u < 0.2, V - 1, rb)); a = two(V - 1, N, 8, 16, C)
    w = two(255, N, 8, 16, 1); w[:, 0, 0] = 0; w[:, 0, 1] = 255; w[:, 7] = 255
    j = rng.integers(0, 16, (N, 8, 1, 1)); only = rng.random((N, 8, 1, 1)) < 0.3; none = rng.random((N, 8, 1, 1)) < 0.4; none[0] = False; none[:, 0] = False; none[N - 1, 7] = True
    th = np.where(lane == j, 496, two(496, N, 8, 16, 1)); th = np.where(only, 496 * (lane == 15), th); th = np.where(none, 0, th); th[:, 0, 0] = 0; th[:, 0, 15] = 496
    s = (16 * 255 * 31) & (VX - 1); x[:, 7, :, s] = 0; x[:, 7, :, (s + V - 1) & (VX - 1)] = 0; x[:, 7, :, V - 2] = 31
    m = rng.random((N, 1, C)) < 0.2; m[..., [0, 1, C - 2, C - 1]] = True; h[:, 7] = np.where(m, 31, h[:, 7])
    return pack(x, rb, a, h, th, w)
def setup_inputs_far(rng):
    x, rb, a, h, th, w = parts(rng); x = rng.integers(20, 32, x.shape); h = rng.integers(0, 4, h.shape)
    half = np.argsort(rng.random((N, 8)), axis=1).reshape(N, 8, 1, 1) & 1
    th = np.where(half == 1, rng.integers(345, 396, (N, 8, 16, 1)), 0)
    q = int(rng.integers(0, N)); p = (q + 1) % N; b = (q - 1) % N; g0 = int(rng.integers(0, 8)); rest = [g for g in range(8) if g != g0]
    x[b] = rng.integers(0, 4, x[b].shape)
    for r, count in ((q, 3 * C + int(rng.integers(8, 16))), (p, 7 * C)):
        th[r] = rng.integers(40, 65, (8, 16, 1)); hit = np.zeros(7 * C, bool); hit[rng.permutation(7 * C)[:count]] = True; hit = hit.reshape(7, C)
        for i, g in enumerate(rest):
            to = (np.arange(VX) - np.add.reduce(w[r, g] * x[r, g], axis=0)) & (VX - 1); can = np.nonzero(to < V)[0]
            c = np.nonzero(hit[i])[0]; n = can[rng.integers(0, len(can), len(c))]
            h[r, g][:, c] = x[r, g][:, n]; a[r, g, rng.integers(0, 16, len(c)), c] = to[n]
    e = rng.integers(-1, 2, (N, 8, C)); h[:, g0, 0::2] = 30 + e; h[:, g0, 1::2] = 30 - e
    x[:, g0, :, :V] = 31; x[:, g0, :, V:] = 0; w[:, g0] = V // 16
    th[:, g0] = rng.choice(np.array([0, 15, 16, 479, 480]), (N, 16, 1)); th[np.arange(N), g0, rng.integers(0, 15, N)] = 480
    return pack(x, rb, a, h, th, w)
def setup_inputs_spread(rng):
    x, rb, a, h, th, w = parts(rng)
    x = np.minimum((np.exp2(5 * rng.random((N, 8, 1, VX))) * rng.random(x.shape) + 0.5).astype(np.int64), 31); h = np.minimum((np.exp2(5 * rng.random((N, 8, 1, C))) * rng.random(h.shape) + 0.5).astype(np.int64), 31)
    def uneven(top, shape, flip):
        v = np.minimum(np.power(float(top), rng.random(shape)).astype(np.int64), top) - 1
        return np.where(rng.random(flip) < 0.3, top - 1 - v, v)
    rb = uneven(V, rb.shape, (N, 8, 1, V)); a = uneven(V, a.shape, (N, 8, 1, C)); w = uneven(256, w.shape, (N, 8, 1, 1))
    th = np.minimum(uneven(497, th.shape, (N, 8, 16, 1)), rng.choice(np.array([20, 60, 110, 496]), (N, 8, 1, 1)))
    return pack(x, rb, a, h, th, w)
def setup_inputs_ties(rng):
    x, rb, a, h, th, w = parts(rng)
    o = rng.integers(6, 26, (N, 8, 16, 2)); e = rng.integers(-6, 7, (N, 8, 16)); pool = rng.integers(0, 32, (N, 8, 16, 4)); pool[..., 0] = o[..., 0] + e; pool[..., 1] = o[..., 0] - e
    x = np.take_along_axis(pool, rng.integers(0, 4, (N, 8, 1, VX)), 3); h = np.take_along_axis(o, (rng.random((N, 8, 1, C)) < 0.3).astype(np.int64), 3)
    less = np.stack([rng.permutation(8) % 2 for q in range(N)])
    th = np.broadcast_to(np.maximum(np.add.reduce(np.abs(e), axis=2) - less, 0)[:, :, None, None], (N, 8, 16, 1))
    a = np.where(rng.random((N, 8, 1, C)) < 0.25, a[:, :, 3:4], a)
    return pack(x, rb, a, h, th, w)
def check_inputs(d):
    bad = []
    for k, hi in (("cues", 31), ("spare", V - 1), ("scroll", V - 1), ("heard", 31), ("th", 496), ("w", 255)):
        v = np.asarray(d[k]).astype(np.float64)
        if not (np.all(v >= 0) and np.all(v <= hi)): bad.append("range of " + k)
        elif np.any(v != np.floor(v)): bad.append("whole numbers in " + k)
    return bad
def reference(cues, spare, scroll, heard, th, w):
    x = cues.astype(np.float32).astype(np.int32).reshape(N, 8, 16, VX); rb = spare.astype(np.int32).reshape(N, 8, 16, V); gb = np.array(rb)
    a = scroll.astype(np.int32).reshape(N, 8, 16, C); h = heard.astype(np.float32).astype(np.int32).reshape(N, 8, 16, C)
    limit = th.astype(np.int32).reshape(N, 8, 16, 1); weight = w.astype(np.int32).reshape(N, 8, 16, 1)
    head = np.zeros((N, 8, C), np.int32); wait = np.zeros((N, 8, C), np.int32); m = [0] * N; place = np.arange(16, dtype=np.int32)[None, :, None]
    for t in range(STEPS):
        say = []
        for r in range(N):
            old = a[r]; hr = h[r]
            shift = np.add.reduce(weight[r] * hr, axis=1) & (VX - 1)
            at = (old + shift[:, None, :]) & (VX - 1)
            px = np.take_along_axis(x[r], at.reshape(8, 1, 16 * C), 2).reshape(8, 16, 16, C)
            d = np.add.reduce(np.abs(px - hr[:, :, None, :]), axis=1)
            o = (place - head[r][:, None, :]) & 15
            near = d <= limit[r] + (m[r] & 15); got = np.any(near, axis=1)
            k = np.argmin(np.where(near, o, 16 + 16 * d + o), axis=1)
            upto = (k - head[r]) & 15
            ak = np.take_along_axis(old, k[:, None, :], 1)[:, 0]
            xk = np.take_along_axis(px, k[:, None, None, :], 2)[:, :, 0]
            rk = np.take_along_axis(rb[r], ak[:, None, :], 2); gk = np.take_along_axis(gb[r], ak[:, None, :], 2)
            sk = np.take_along_axis(x[r], (ak ^ 1)[:, None, :], 2)
            say.append(np.where(got[:, None, :], sk, np.abs(hr - xk)))
            more = np.where(got, 0, wait[r] + 1); full = more == 2
            new = np.where(got[:, None, :] & (o <= upto[:, None, :]), rk, np.where(full[:, None, :], gk, old))
            gi, ci = np.nonzero(got); gb[r][gi, :, (ak - (ak & (C - 1)))[gi, ci] + ci] = old[gi, :, ci]
            head[r] = np.where(got, (k + 1) & 15, np.where(full, 0, head[r])); wait[r] = np.where(full, 0, more)
            m[r] = int(np.count_nonzero(got)); a[r] = new
        h = np.stack([say[(r - 1 - t % (N - 1)) % N] for r in range(N)])
    return {"ys": a.reshape(N, 128, C).astype(np.float32), "yg": gb.reshape(N, 128, V).astype(np.float32), "yh": h.reshape(N, 128, C).astype(np.float32).astype(BF)}

@@ -1,0 +1,552 @@
+import numpy as np
+import comms_topo
+from concourse.mybir import dt, AluOpType, AxisListType, ActivationFunctionType
+
+ALU = AluOpType
+ACT = ActivationFunctionType
+C, V, VX, STEPS = 512, 2048, 4096, 4
+NCH = 2
+CW = C // NCH
+NS = CW // 128
+NC = CW // 16
+NA = 8
+MW = 128
+NE = 8
+GP = 64
+LAM = 5000.0
+ROUNDS = 220
+BIAS = 9.0e9
+SEED = 2
+SLACK = 1000.0
+YB = 4
+
+SCRATCH = {
+    "tab": ("sbuf", [128, 8192], "bfloat16"),
+    "book": ("sbuf", [128, 6144], "float32"),
+    "spi": ("sbuf", [128, 2048], "int32"),
+    "g2": ("sbuf", [128, 2048], "float32"),
+    "ai": ("sbuf", [128, 512], "int32"),
+    "thi": ("sbuf", [128, 8], "int32"), "wi": ("sbuf", [128, 8], "int32"),
+    "af": ("sbuf", [128, 512], "float32"),
+    "tt": ("sbuf", [128, 512], "float16"), "mm": ("sbuf", [128, 512], "float16"),
+    "yr": ("sbuf", [128, 512], "bfloat16"), "off": ("sbuf", [128, 512], "uint16"),
+    "hz": ("sbuf", [128, 512], "bfloat16"), "yy": ("sbuf", [128, 512], "bfloat16"),
+    "gg": ("sbuf", [128, 512], "bfloat16"),
+    "scp": ("sbuf", [128, 512], "float32"), "sck": ("sbuf", [128, 512], "float32"), "ll": ("sbuf", [128, 512], "float32"),
+    "km": ("sbuf", [128, 32], "float32"),
+    "ki": ("sbuf", [128, 32], "int32"), "nm": ("sbuf", [128, 32], "bfloat16"),
+    "s0": ("sbuf", [128, 32], "int32"), "s1": ("sbuf", [128, 32], "int32"), "t1": ("sbuf", [128, 32], "int32"),
+    "zz": ("sbuf", [128, 32], "int32"), "i9": ("sbuf", [128, 32], "int32"), "wv": ("sbuf", [128, 32], "int32"),
+    "lst": ("sbuf", [128, 96], "int32"), "lu": ("sbuf", [128, 96], "uint16"),
+    "gw0": ("sbuf", [128, 32], "int32"), "gw1": ("sbuf", [128, 32], "int32"), "gwu": ("sbuf", [128, 32], "uint16"),
+    "cc": ("sbuf", [128, 32], "int32"), "cl": ("sbuf", [128, 16], "int32"), "c16": ("sbuf", [128, 32], "int32"),
+    "mc": ("sbuf", [128, 8], "float32"), "mi": ("sbuf", [128, 8], "int32"),
+    "pi": ("sbuf", [128, 8], "int32"), "pj": ("sbuf", [128, 8], "int32"), "col": ("sbuf", [128, 16], "float32"),
+    "jj": ("sbuf", [128, 144], "float32"), "jl": ("sbuf", [128, 256], "float32"), "jh": ("sbuf", [128, 128], "float32"),
+    "jm": ("sbuf", [128, 128], "float32"), "bi": ("sbuf", [128, 16], "int32"), "bl": ("sbuf", [128, 16], "uint16"),
+    "kk": ("sbuf", [128, 512], "float32"), "vv": ("sbuf", [128, 512], "int32"), "vw": ("sbuf", [128, 512], "int32"),
+    "okn": ("sbuf", [128, 512], "int32"),
+    "ih": ("sbuf", [128, 128], "float16"), "ib": ("sbuf", [128, 128], "bfloat16"), "ineg": ("sbuf", [128, 128], "bfloat16"),
+    "ibig": ("sbuf", [128, 128], "bfloat16"), "wblk": ("sbuf", [128, 128], "bfloat16"), "wide": ("sbuf", [128, 144], "bfloat16"),
+    "hb": ("sbuf", [128, 256], "bfloat16"), "dmx": ("sbuf", [128, 16], "bfloat16"), "dab": ("sbuf", [128, 16], "bfloat16"),
+    "dx": ("sbuf", [128, 16], "bfloat16"),
+    "bs": ("sbuf", [128, 8], "float32"), "r0": ("sbuf", [128, 128], "float32"), "r1": ("sbuf", [128, 128], "float32"),
+    "rsp": ("sbuf", [128, 128], "bfloat16"), "rsk": ("sbuf", [128, 128], "bfloat16"),
+    "cep": ("sbuf", [128, 512], "float16"), "ck": ("sbuf", [128, 256], "float16"),
+    "o2k": ("sbuf", [128, 128], "float16"), "one": ("sbuf", [128, 128], "bfloat16"),
+    "rst": ("sbuf", [128, 256], "float32"), "dm": ("sbuf", [128, 256], "float32"),
+    "ut": ("sbuf", [128, 1024], "bfloat16"), "nt": ("sbuf", [128, 1024], "bfloat16"),
+    "st0": ("sbuf", [128, 1024], "bfloat16"), "st1": ("sbuf", [128, 1024], "bfloat16"),
+}
+for _i in range(2):
+    SCRATCH["xg%d" % _i] = ("sbuf", [128, 16 * CW], "bfloat16")
+    SCRATCH["mx%d" % _i] = ("sbuf", [128, 16 * CW], "bfloat16")
+for _i in range(STEPS):
+    SCRATCH["a%d" % _i] = ("sbuf", [128, 512], "float16")
+    SCRATCH["say%d" % _i] = ("sbuf", [128, 512], "bfloat16")
+for _i in range(STEPS + 1):
+    SCRATCH["h%d" % _i] = ("sbuf", [128, 512], "bfloat16")
+for _n in ("ha0", "ha1", "sb", "ep0", "ep1", "kb", "yb0", "yb1"):
+    SCRATCH[_n] = ("psum", [128, 512], "float32")
+
+NDMA = 40
+SEMAPHORES = ["cv", "cs", "cp", "cg", "sent"] + ["d%d" % _i for _i in range(NDMA)] + \
+             ["arr%d_%d" % (_t, _c) for _t in range(STEPS) for _c in range(NCH)]
+
+CY, PCY, GA, SC, HOP = 1.04, 0.52, 1.56, 3.8, 120.0
+
+
+def build(g, core, T, topo):
+    ops = []
+    cores = list(T.cores)
+    n = len(cores)
+    rank = T.rank_of(core)
+    v, s, p, y = g.vector, g.scalar, g.tensor, g.sync
+
+    now = [0]
+
+    def op(eng, fn, rd, wr, cost, banks=(), lat=0.0, sem=None, alt=None):
+        ops.append({"ord": [], "alt": alt, "c": now[0], "eng": eng, "fn": fn, "rd": list(rd), "wr": list(wr), "bk": list(banks), "cost": cost, "lat": lat, "sem": sem})
+
+    def vc(k, f=1.0):
+        return max(64.0, k * f) * CY + 30.0
+
+    def ts(out, in0, s1, s2, o0, o1, rd, wr, k, f=1.0, banks=()):
+        if o1 is None:
+            op("v", lambda: v.tensor_scalar(out, in0, s1, None, o0), rd, wr, vc(k, f), banks)
+        else:
+            op("v", lambda: v.tensor_scalar(out, in0, s1, s2, o0, o1), rd, wr, vc(k, f), banks)
+
+    def tt(out, in0, in1, o, rd, wr, k, f=2.0, banks=()):
+        op("v", lambda: v.tensor_tensor(out, in0, in1, o), rd, wr, vc(k, f), banks)
+
+    def cp(out, in_, rd, wr, k, f=1.0, banks=()):
+        op("v", lambda: v.tensor_copy(out, in_), rd, wr, vc(k, f), banks)
+
+    def ms(ap, val, wr, k, f=1.0):
+        op("v", lambda: v.memset(ap, val), [], wr, vc(k, f))
+
+    def act(out, in_, fn, rd, wr, cost, banks=(), bias=None):
+        if bias is None:
+            op("s", lambda: s.activation(out, in_, fn), rd, wr, cost, banks)
+        else:
+            op("s", lambda: s.activation(out, in_, fn, bias=bias), rd, wr, cost, banks)
+
+    def either(out, in_, rd, wr, cost_s, cost_v):
+        op("s", lambda: s.activation(out, in_, ACT.Copy), rd, wr, cost_s, alt=(lambda: v.tensor_copy(out, in_), cost_v))
+
+    def mm(out, lhs, rhs, st, sp, rd, bank, k, f=1.0):
+        op("p", lambda: p.matmul(out, lhs, rhs, st, sp), rd, [bank], max(64.0, k) * f * PCY)
+
+    def mid(out, lhs, rhs, rd, bank, k):
+        op("p", lambda: p.matmul(out, lhs, rhs, False, False), rd, [], max(64.0, k) * PCY, [bank])
+
+    def io(out, pat, base, cm, wr, k, flt):
+        if flt:
+            op("g", lambda: g.iota(out, pat, base, cm, allow_small_or_imprecise_dtypes=True), [], wr, 130.0 + 2 * k * CY)
+        else:
+            op("g", lambda: g.iota(out, pat, base, cm), [], wr, 130.0 + 2 * k * CY)
+
+    nd = [0]
+
+    def dma(q, out, in_, rd, wr, nbytes):
+        sem = "d%d" % nd[0]
+        nd[0] += 1
+        e = y if q == "y" else s
+        op(q, lambda: e.dma_start(out, in_), rd, wr, 60.0, lat=1800.0 + nbytes / 150.0, sem=(sem, 16))
+
+    def gat(k):
+        return 60.0 + k * GA * CY
+
+    dma("y", T.h0[:], T.heard[:], [], ["h0_%d" % c for c in range(NCH)], 1 << 17)
+    dma("s", T.wi[:, 0:1], T.w[:], [], ["wi"], 1 << 12)
+    dma("s", T.ai[:], T.scroll[:], [], ["ai"], 3 << 17)
+    dma("y", T.tab[:, 6144:8192], T.cues[:, 2048:4096], [], ["tab1"], 7 << 17)
+    dma("y", T.tab[:, 4096:6144], T.cues[:, 0:2048], [], ["tab0"], 11 << 17)
+    dma("s", T.thi[:, 0:1], T.th[:], [], ["thi"], 1 << 12)
+    dma("y", T.spi[:], T.spare[:], ["tab0", "tab1"], ["spi"], 1 << 20)
+    for i, j in ((3, 0), (4, 3), (2, 1), (5, 2)):
+        ops[i]["ord"].append(j)
+
+    io(T.pi[:, 0:1], [[0, 1]], 0, 1, ["pi"], 1, False)
+    io(T.jj[:], [[1, 144]], 0, 0, ["jj"], 144, True)
+    io(T.jh[:], [[1, 8], [0, 16]], 0, 0, ["jh"], 128, True)
+    io(T.jl[:], [[0, 16], [1, 16]], 0, 0, ["jl"], 256, True)
+    op("g", lambda: g.affine_select(T.jm[:], T.jh[:], [[0, 8], [-1, 16]], ALU.is_ge, -1.0, 15 - NA, 0), ["jh"], ["jm"], 170.0 + 256 * CY)
+    io(T.bi[:], [[1, 16]], 0, 0, ["bi"], 16, False)
+    io(T.c16[:], [[16, 32]], 512, 0, ["c16"], 32, False)
+    io(T.nt[:, 0:512], [[0, 256], [1, 2]], 0, 0, ["nt0"], 512, True)
+    io(T.vv[:], [[0, 16], [1, 16], [0, 2]], 0, -1, ["vv"], 512, False)
+    io(T.okn[:], [[1, 16], [0, 16], [64, 2]], 0, 0, ["okn"], 512, False)
+    io(T.kk[:], [[0, 16], [1, 16], [64, 2]], 0, 0, ["kk"], 512, True)
+    col = lambda j: T.col[:, j:j + 1]
+    PF, LANE, GRP, WF, THN, L2, L34, G15 = 0, 1, 2, 3, 4, 5, 6, 7
+    cp(T.pj[:, 0:1], T.pi[:, 0:1], ["pi"], ["pj0"], 1)
+    ts(T.pj[:, 1:2], T.pi[:, 0:1], 15, None, ALU.bitwise_and, None, ["pi"], ["pj1"], 1)
+    ts(T.pj[:, 2:3], T.pi[:, 0:1], 4, None, ALU.arith_shift_right, None, ["pi"], ["pj2"], 1)
+    cp(T.col[:, 0:3], T.pj[:, 0:3], ["pj0", "pj1", "pj2"], ["col"], 3)
+    cp(col(WF), T.wi[:, 0:1], ["wi"], ["wf"], 1)
+    ts(T.wblk[:], T.jh[:], col(GRP), col(WF), ALU.is_equal, ALU.mult, ["jh", "col", "wf"], ["wblk"], 128)
+    ts(T.ih[:], T.jj[:, 0:128], col(PF), None, ALU.is_equal, None, ["jj", "col"], ["ih"], 128)
+    ts(T.ib[:], T.jj[:, 0:128], col(PF), None, ALU.is_equal, None, ["jj", "col"], ["ib"], 128)
+    ts(T.ineg[:], T.jj[:, 0:128], col(PF), -1.0, ALU.is_equal, ALU.mult, ["jj", "col"], ["ineg"], 128)
+    for c in range(NCH):
+        cp(T.a0[:, c * CW:(c + 1) * CW], T.ai[:, c * CW:(c + 1) * CW], ["ai"], ["a0_%d" % c], CW)
+    ts(T.ibig[:], T.ib[:], float(1 << 24), None, ALU.mult, None, ["ib"], ["ibig"], 128, 0.5)
+    ts(col(G15), col(GRP), 16.0, 15.0, ALU.mult, ALU.add, ["col"], ["g15"], 1)
+    ts(T.wide[:], T.jj[:], col(G15), col(WF), ALU.is_equal, ALU.mult, ["jj", "g15", "wf"], ["wide"], 144)
+    ts(T.hb[:, 0:128], T.jm[:], col(GRP), -2048.0, ALU.is_equal, ALU.mult, ["jm", "col"], ["hb0"], 128)
+    ts(T.hb[:, 128:256], T.jm[:], col(GRP), -65536.0, ALU.is_equal, ALU.mult, ["jm", "col"], ["hb1"], 128)
+    cp(T.dx[:], T.hb[:, 0::16], ["hb0", "hb1"], ["dx"], 16)
+    ts(T.dmx[:], T.hb[:, 0::16], -2.0, None, ALU.mult, None, ["hb0", "hb1"], ["dmx"], 16)
+    ts(T.dab[:], T.hb[:, 0::16], -1.0, None, ALU.mult, None, ["hb0", "hb1"], ["dab"], 16)
+    ts(T.bs[:], T.jj[:, 0:8], col(GRP), None, ALU.is_equal, None, ["jj", "col"], ["bs"], 8)
+    ts(col(THN), T.thi[:, 0:1], -1.0, None, ALU.mult, None, ["thi"], ["thn"], 1)
+    ts(col(L2), col(LANE), 2.0, 1.0, ALU.mult, ALU.add, ["col"], ["l2"], 1)
+    ts(col(L34), col(LANE), 34.0, None, ALU.mult, None, ["col"], ["l34"], 1)
+    ts(T.cep[:, 0:128], T.ih[:], col(THN), None, ALU.mult, None, ["ih", "thn"], ["cep0"], 128, 0.5)
+    ts(T.cep[:, 128:256], T.ih[:], col(L2), -60.25, ALU.mult, ALU.add, ["ih", "l2"], ["cep1"], 128, 0.5)
+    for b in range(NS):
+        ts(T.ck[:, b * 128:(b + 1) * 128], T.ih[:], col(L34), None, ALU.mult, None, ["ih", "l34"], ["ck%d" % b], 128, 0.5)
+    cks = ["ck%d" % j for j in range(NS)]
+    ms(T.o2k[:], 2048.0, ["o2k"], 128, 0.5)
+    ms(T.one[:], 1.0, ["one"], 128, 0.5)
+    ms(T.mc[:, 2:3], -1024.0, ["mb"], 1)
+    ts(T.r0[:], T.jh[:], col(GRP), None, ALU.is_equal, None, ["jh", "col"], ["r0"], 128)
+    ts(T.r1[:], T.ib[:], -16.0, None, ALU.mult, None, ["ib"], ["r1"], 128)
+    tt(T.r0[:], T.r0[:], T.r1[:], ALU.add, ["r0", "r1"], ["r0"], 128)
+    ts(T.rsp[:], T.r0[:], 4096.0, None, ALU.mult, None, ["r0"], ["rsp"], 128)
+    ts(T.rsk[:], T.r0[:], 65536.0, None, ALU.mult, None, ["r0"], ["rsk"], 128)
+    ts(T.rst[:, 0:CW], T.jl[:, 0:CW], 0.0, 1.0e9, ALU.is_equal, ALU.mult, ["jl"], ["rst"], CW)
+    ts(T.dm[:, 0:CW], T.jl[:, 0:CW], col(LANE), None, ALU.is_equal, None, ["jl", "col"], ["dm"], CW)
+    cp(T.bl[:], T.bi[:], ["bi"], ["bl"], 16)
+    ts(T.cc[:], T.c16[:], col(LANE), None, ALU.add, None, ["c16", "col"], ["cc"], 32)
+    ts(T.cl[:], T.cc[:, 0:16], -512.0, 2.0, ALU.add, ALU.mult, ["cc"], ["cl"], 16)
+    ms(T.nt[:, 512:1024], 1.0, ["nt1"], 512, 0.5)
+    ms(T.ut[:, 512:1024], 0.0, ["ut1"], 512, 0.5)
+    ms(T.st0[:, 512:1024], 0.0, ["st0_%d" % c for c in range(NCH)], 512, 0.5)
+    ts(T.vw[:], T.vv[:], 15, None, ALU.bitwise_and, None, ["vv"], ["vw"], 512)
+    tt(T.ut[:, 0:512], T.vw[:], T.okn[:], ALU.is_le, ["vw", "okn"], ["ut0"], 512)
+    ts(T.st0[:, 0:512], T.kk[:], col(LANE), None, ALU.is_lt, None, ["kk", "col"], ["stt0"], 512)
+    either(T.st1[:, 0:512], T.st0[:, 0:512], ["stt0"], ["stt1"], vc(512), vc(512, 0.5))
+    for e in range(2):
+        either(T.tab[:, e:2048:2], T.tab[:, 4097 - e:6144:2], ["tab0"], ["sw%d" % e], vc(1024), vc(1024, 0.5))
+    for e in range(2):
+        either(T.tab[:, 2048 + e * 1024:3072 + e * 1024], T.tab[:, 6144 + e * 1024:7168 + e * 1024], ["tab1"], ["tab%d" % (2 + e)], vc(1024), vc(1024, 0.5))
+    for e in range(4):
+        cp(T.book[:, e * 512:(e + 1) * 512], T.spi[:, e * 512:(e + 1) * 512], ["spi"], ["sp%d" % e], 512)
+    sps = ["sp%d" % e for e in range(4)]
+    dma("y", T.book[:, 2048:4096], T.book[:, 0:2048], sps, ["gap"], 1 << 20)
+
+    tabs = ["tab0", "tab1", "tab2", "tab3"]
+    k = 0
+    ny = [0]
+    for t in range(STEPS):
+        last = t == STEPS - 1
+        H, A = T["h%d" % t], T["a%d" % t]
+        STo, STn = T["st%d" % (t % 2)], T["st%d" % ((t + 1) % 2)]
+        dst = cores[(rank + 1 + t % (n - 1)) % n]
+        src = cores[(rank - 1 - t % (n - 1)) % n]
+        for c in range(NCH):
+            q = k % 2
+            now[0] = c
+            k += 1
+            c0 = c * CW
+            cs = slice(c0, c0 + CW)
+            ws = slice(c * NC, (c + 1) * NC)
+            h, a = "h%d_%d" % (t, c), "a%d_%d" % (t, c)
+            sto = "st%d_%d" % (t % 2, c)
+            ha = "ha%d" % q
+            HA, X, MX = T[ha], T["xg%d" % q], T["mx%d" % q]
+            r = lambda name: "%s_%d" % (name, c)
+            mm(T.sb[:, 0:CW], T.wblk[:], H[:, cs], True, True, ["wblk", h], "sb", CW)
+            act(T.yr[:, cs], T.sb[:, 0:CW], ACT.Identity, [], [r("yr")], vc(CW), ["sb"], bias=524288.0)
+            mm(HA[:, 0:CW], T.wblk[:], H[:, cs], True, False, ["wblk", h], ha, CW)
+            mm(HA[:, 0:CW], T.ih[:], A[:, cs], False, False, ["ih", a], ha, CW)
+            mm(HA[:, 0:CW], T.ineg[:], T.yr[:, cs], False, True, ["ineg", r("yr")], ha, CW)
+            mm(HA[:, 256:256 + CW], T.ib[:], H[:, cs], True, True, ["ib", h], ha, CW)
+            ts(T.off[:, cs], HA[:, 0:CW], 526336.0, None, ALU.add, None, [], [r("off")], CW, 1.0, [ha])
+            for m in range(16):
+                mm(T.sb[:, 256:256 + NC], T.wide[:, 15 - m:143 - m], H[:, c0 + m:c0 + CW:16], m == 0, m == 15, ["wide", h], "sb", NC)
+            ts(T.s0[:, ws], T.sb[:, 256:256 + NC], 2048.0, None, ALU.add, None, [], [r("s0")], NC, 1.0, ["sb"])
+            ts(T.s1[:, ws], T.s0[:, ws], 4095, None, ALU.bitwise_and, None, [r("s0")], [r("s1")], NC)
+            xs = [["x%d_%d" % (q, e) for e in range(b * 128 // GP, (b + 1) * 128 // GP)] for b in range(NS)]
+            for e in range(CW // GP):
+                either(X[:, e * GP * 16:(e + 1) * GP * 16], T.tab[:, 2048:8192].indirect(T.off[:, c0 + e * GP:c0 + (e + 1) * GP]),
+                       tabs + [r("off")], ["x%d_%d" % (q, e)], gat(GP * 16), gat(GP * 16))
+            eps = ["ep%d" % ((k * NS + b) % 2) for b in range(NS)]
+            for b in range(NS):
+                ep = eps[b]
+                EP = T[ep]
+                bs_ = slice(c0 + b * 128, c0 + (b + 1) * 128)
+                mm(EP[:, 0:256], T.o2k[:], T.cep[:, 0:256], True, False, ["o2k", "cep0", "cep1"], ep, 256)
+                mid(EP[:, 0:256], H[:, bs_], T.hb[:], [h, "hb0", "hb1"], ep, 256)
+                if t > 0:
+                    mid(EP[:, 128:256], STo[:, 512 + c0 + b * 128:512 + c0 + (b + 1) * 128], T.rsp[:], [sto, "rsp"], ep, 128)
+                for i in range(16 - NA):
+                    mid(EP[:, i:256:16], X[:, b * 2048 + i:(b + 1) * 2048:16], T.dx[:], xs[b] + ["dx"], ep, 16)
+                for i in range(16 - NA):
+                    mxr = "mx%d_%d_%d" % (q, i, b)
+                    o_ = MX[:, i * CW + b * 128:i * CW + (b + 1) * 128]
+                    tt(o_, X[:, b * 2048 + i:(b + 1) * 2048:16], HA[:, 256 + b * 128:256 + (b + 1) * 128], ALU.max, xs[b], [mxr], 128, 1.0, [ha])
+                    mid(EP[:, i:256:16], o_, T.dmx[:], [mxr, "dmx"], ep, 16)
+                for j0 in range(0, NA, YB):
+                    yb = "yb%d" % (ny[0] % 2)
+                    ny[0] += 1
+                    js = list(range(j0, min(NA, j0 + YB)))
+                    for j in js:
+                        o_ = T[yb][:, (j - j0) * 128:(j - j0 + 1) * 128]
+                        mm(o_, T.ineg[:], H[:, c0 + b * 128:c0 + (b + 1) * 128], True, False, ["ineg", h], yb, 128)
+                        mm(o_, T.ib[:], X[:, b * 2048 + 16 - NA + j:(b + 1) * 2048:16], False, True, ["ib"] + xs[b], yb, 128)
+                    m0 = (16 - NA) * CW + b * NA * 128
+                    mxr = "ab%d_%d_%d" % (q, b, j0)
+                    act(MX[:, m0 + j0 * 128:m0 + (j0 + len(js)) * 128], T[yb][:, 0:len(js) * 128], ACT.Abs, [], [mxr], vc(len(js) * 128), [yb])
+                    for j in js:
+                        mid(EP[:, 16 - NA + j:256:16], MX[:, m0 + j * 128:m0 + (j + 1) * 128], T.dab[:], [mxr, "dab"], ep, 16)
+                mm(EP[:, 128:256], A[:, bs_], T.ih[:], False, True, [a, "ih"], ep, 128)
+                act(T.gg[:, bs_], EP[:, 0:128], ACT.Sign, ["mb"], [r("gg%d" % b)], vc(128), [ep], bias=T.mc[:, 2:3])
+                op("v", lambda o_=T.scp[:, bs_], i_=EP[:, 128:256]: v.tensor_tensor_scan(o_, T.rst[:, 0:128], i_, 0.0, ALU.add, ALU.min),
+                   ["rst"], [r("scp%d" % b)], vc(128), [ep])
+            mm(T.kb[:, 0:CW], T.o2k[:], T.ck[:, 0:CW], True, False, ["o2k"] + cks, "kb", CW)
+            for b in range(NS):
+                if t > 0:
+                    mm(T.kb[:, b * 128:(b + 1) * 128], STo[:, 512 + c0 + b * 128:512 + c0 + (b + 1) * 128], T.rsk[:], False, False, [sto, "rsk"], "kb", 128)
+                mm(T.kb[:, b * 128:(b + 1) * 128], A[:, c0 + b * 128:c0 + (b + 1) * 128], T.ih[:], False, False, [a, "ih"], "kb", 128)
+            mm(T.kb[:, 0:CW], T.ibig[:], T.gg[:, cs], False, True, ["ibig"] + [r("gg%d" % b) for b in range(NS)], "kb", CW)
+            op("v", lambda o_=T.sck[:, cs]: v.tensor_tensor_scan(o_, T.rst[:, 0:CW], T.kb[:, 0:CW], 0.0, ALU.add, ALU.min),
+               ["rst"], [r("sck")], vc(CW), ["kb"])
+            tt(T.km[:, ws], T.scp[:, c0 + 15:c0 + CW:16], T.sck[:, c0 + 15:c0 + CW:16], ALU.min, [r("sck")] + [r("scp%d" % b) for b in range(NS)], [r("km")], NC)
+            op("v", lambda o_=T.ll[:, cs], w_=T.km[:, ws]: v.tensor_tensor(o_, w_.indirect(T.bl[:, 0:NC]), T.dm[:, 0:CW], ALU.mult),
+               [r("km"), "bl", "dm"], [r("ll")], gat(CW))
+            for b in range(NS):
+                mm(T.kb[:, 256 + b * 8:256 + (b + 1) * 8], T.ll[:, c0 + b * 128:c0 + (b + 1) * 128], T.bs[:], True, True, [r("ll"), "bs"], "kb", 8, 4.0)
+            kw = T.kb[:, 256:256 + NC]
+            l0 = c * 3 * NC
+            cp(T.ki[:, ws], kw, [], [r("ki")], NC, 1.0, ["kb"])
+            ts(T.nm[:, ws], kw, -240.0 * 65536.0, None, ALU.is_ge, None, [], [r("nm")], NC, 1.0, ["kb"])
+            ts(T.lst[:, l0 + NC:l0 + 2 * NC], T.ki[:, ws], 4095, None, ALU.bitwise_and, None, [r("ki")], [r("bk")], NC)
+            ts(T.i9[:, ws], T.ki[:, ws], 11, 511, ALU.arith_shift_right, ALU.bitwise_and, [r("ki")], [r("i9")], NC)
+            tt(T.t1[:, ws], T.nm[:, ws], T.s1[:, ws], ALU.mult, [r("nm"), r("s1")], [r("t1")], NC)
+            WV, wv = (T.cc, "cc") if t == 0 else (T.wv, r("wv"))
+            tt(T.zz[:, ws], T.nm[:, ws], WV[:, ws], ALU.mult, [r("nm"), wv], [r("zz")], NC)
+            tt(T.lst[:, l0:l0 + NC], T.t1[:, ws], T.lst[:, l0 + NC:l0 + 2 * NC], ALU.add, [r("t1"), r("bk")], [r("spx")], NC)
+            tt(T.lst[:, l0 + 2 * NC:l0 + 3 * NC], T.i9[:, ws], T.zz[:, ws], ALU.max, [r("i9"), r("zz")], [r("iu")], NC)
+            cp(T.lu[:, l0:l0 + 3 * NC], T.lst[:, l0:l0 + 3 * NC], [r("spx"), r("bk"), r("iu")], [r("lu")], 3 * NC)
+            if not last:
+                tt(T.wv[:, ws], T.cc[:, ws], T.zz[:, ws], ALU.subtract, ["cc", r("zz")], [r("wv")], NC)
+            lsp, lbk, liu = T.lu[:, l0:l0 + NC], T.lu[:, l0 + NC:l0 + 2 * NC], T.lu[:, l0 + 2 * NC:l0 + 3 * NC]
+            op("v", lambda o_=T.hz[:, cs], l_=liu, h_=H[:, cs]: v.tensor_tensor(o_, T.nt[:, 0:1024].indirect(l_), h_, ALU.mult),
+               ["nt0", "nt1", r("lu"), h], [r("hz")], gat(CW))
+            op("v", lambda o_=T.yy[:, cs], l_=lsp, h_=T.hz[:, cs]: v.tensor_tensor(o_, T.tab[:, 0:8192].indirect(l_), h_, ALU.subtract),
+               tabs + ["sw0", "sw1", r("lu"), r("hz")], [r("yy")], gat(CW))
+            say = "say%d_%d" % (t, c)
+            act(T["say%d" % t][:, cs], T.yy[:, cs], ACT.Abs, [r("yy")], [say], vc(CW))
+            rid, pid, _ = topo.addr(dst)
+            msk = 0
+            for e in topo.engines(core, dst)[:NE]:
+                msk |= 1 << e
+            got = len(topo.engines(src, core)[:NE])
+            arr = "arr%d_%d" % (t, c)
+            op("g", lambda o_=T["h%d" % (t + 1)][:, cs], i_=T["say%d" % t][:, cs], a_=arr, pid=pid, rid=rid, msk=msk:
+               g.remote_dma(o_, i_, T.sem[a_], T.sem["sent"], pid, rid, msk),
+               [say], ["h%d_%d" % (t + 1, c)], 300.0, lat=2500.0, sem=(arr, got, len(topo.engines(core, dst)[:NE])))
+            if t == 0:
+                ts(T.gw0[:, ws], T.ki[:, ws], 2047, None, ALU.bitwise_and, None, [r("ki")], [r("n0")], NC)
+                cp(T.gwu[:, ws], T.gw0[:, ws], [r("n0")], [r("n1")], NC)
+                op("v", lambda o_=T.tt[:, cs], l_=T.gwu[:, ws], a_=A[:, cs]: v.tensor_tensor(o_, T.spi[:, 0:2048].indirect(l_), a_, ALU.subtract),
+                   ["spi", r("n1"), a], [r("tt")], gat(CW))
+            else:
+                op("v", lambda o_=T.tt[:, cs], l_=lbk, a_=A[:, cs]: v.tensor_tensor(o_, T.book[:, 0:4096].indirect(l_), a_, ALU.subtract),
+                   sps + ["gap", r("lu"), a], [r("tt")], gat(CW))
+            op("v", lambda o_=T.mm[:, cs], l_=liu, t_=T.tt[:, cs]: v.tensor_tensor(o_, T.ut[:, 0:1024].indirect(l_), t_, ALU.mult),
+               ["ut0", "ut1", r("lu"), r("tt")], [r("mm")], gat(CW))
+            if last:
+                tt(T.af[:, cs], A[:, cs], T.mm[:, cs], ALU.add, [a, r("mm")], [r("af")], CW)
+                dma("y", T.ys[:, cs], T.af[:, cs], [r("af")], [r("ys")], CW * 512)
+                dma("y", T.yh[:, cs], T["h%d" % STEPS][:, cs], ["h%d_%d" % (STEPS, c)], [r("yh")], CW * 256)
+            else:
+                tt(T["a%d" % (t + 1)][:, cs], A[:, cs], T.mm[:, cs], ALU.add, [a, r("mm")], ["a%d_%d" % (t + 1, c)], CW)
+                either(STn[:, 512 + c0:512 + c0 + CW], STo[:, 0:1024].indirect(liu),
+                       ["stt%d" % (t % 2), r("lu")] + ["st%d_%d" % (t % 2, e) for e in range(NCH)], ["st%d_%d" % ((t + 1) % 2, c)], gat(CW), gat(CW))
+            if last and (c + 1) * CW == 256:
+                kis = ["ki_%d" % e for e in range(c + 1)]
+                ts(T.gw0[:, 0:16], T.ki[:, 0:16], 3584, None, ALU.bitwise_and, None, kis, ["gw0a"], 16)
+                tt(T.gw1[:, 0:16], T.gw0[:, 0:16], T.cl[:], ALU.add, ["gw0a", "cl"], ["gw1a"], 16)
+                ts(T.gwu[:, 0:16], T.gw1[:, 0:16], 0.5, None, ALU.mult, None, ["gw1a"], ["gwua"], 16)
+                op("v", lambda a_=A[:, 0:256]: v.tensor_copy(T.g2[:, 0:2048].indirect(T.gwu[:, 0:16]), a_),
+                   ["gwua"] + ["a%d_%d" % (t, e) for e in range(c + 1)], ["g2_%d" % e for e in range(4)], 60.0 + 256 * SC * CY)
+                for e in range(4):
+                    dma("y", T.yg[:, e * 512:e * 512 + 256], T.g2[:, e * 256:(e + 1) * 256], ["g2_%d" % e], ["yga%d" % e], 1 << 17)
+        w0 = 16 if last else 0
+        kis = ["ki_%d" % e for e in range(NCH)]
+        ts(T.gw0[:, w0:32], T.ki[:, w0:32], 3584, None, ALU.bitwise_and, None, kis, ["gw0"] + ([] if last else ["gw0a"]) + ["n0_%d" % e for e in range(NCH)], 32)
+        tt(T.gw1[:, w0:32], T.gw0[:, w0:32], T.cc[:, w0:32], ALU.add, ["gw0", "cc"], ["gw1"] + ([] if last else ["gw1a"]), 32)
+        cp(T.gwu[:, w0:32], T.gw1[:, w0:32], ["gw1"], ["gwu"] + ([] if last else ["gwua"]) + ["n1_%d" % e for e in range(NCH)], 32)
+        op("v", lambda a_=A[:, 16 * w0:512], w0=w0: v.tensor_copy(T.book[:, 1536:6144].indirect(T.gwu[:, w0:32]), a_),
+           ["gwu"] + ([] if last else ["gwua"]) + ["a%d_%d" % (t, e) for e in range(NCH)], ["gap", "sp3"], 60.0 + (512 - 16 * w0) * SC * CY)
+        if last:
+            for e in range(4):
+                dma("y" if e % 2 == 0 else "s", T.yg[:, e * 512 + 256:(e + 1) * 512], T.book[:, 2048 + e * 512 + 256:2048 + (e + 1) * 512], ["gap"], ["ygb%d" % e], 1 << 18)
+        else:
+            if t == STEPS - 2:
+                for e in range(4):
+                    dma("y", T.g2[:, e * 256:(e + 1) * 256], T.book[:, 2048 + e * 512:2048 + e * 512 + 256], ["gap"], ["g2_%d" % e], 1 << 18)
+            mm(T.kb[:, 320:352], T.one[:], T.nm[:], True, True, ["one"] + ["nm_%d" % e for e in range(NCH)], "kb", 32)
+            op("v", lambda: v.tensor_reduce(T.mc[:, 0:1], T.kb[:, 320:352], AxisListType.X, ALU.add, negate=True), [], ["mc"], vc(32), ["kb"])
+            cp(T.mi[:, 0:1], T.mc[:, 0:1], ["mc"], ["mi0"], 1)
+            ts(T.mi[:, 1:2], T.mi[:, 0:1], 15, None, ALU.bitwise_and, None, ["mi0"], ["mi1"], 1)
+            ts(T.mc[:, 2:3], T.mi[:, 1:2], -2048.0, -1024.0, ALU.mult, ALU.add, ["mi1"], ["mb"], 1)
+    return ops
+
+
+def depend(ops):
+    lw, rds = {}, {}
+    for i, o in enumerate(ops):
+        d = set()
+        for x in o["rd"]:
+            if x in lw:
+                d.add(lw[x])
+        for x in o["bk"]:
+            if x in lw:
+                d.add(lw[x])
+            for j in rds.get(x, []):
+                if ops[j]["eng"] != o["eng"]:
+                    d.add(j)
+        for x in o["wr"]:
+            if x in lw:
+                d.add(lw[x])
+            d.update(rds.get(x, []))
+        d.discard(i)
+        o["dep"] = sorted(d)
+        for x in o["rd"] + o["bk"]:
+            rds.setdefault(x, []).append(i)
+        for x in o["wr"]:
+            lw[x] = i
+            rds[x] = []
+
+
+def gap_after(ops, j, i):
+    if ops[j]["eng"] == "p" and ops[i]["eng"] == "p":
+        return 0.0
+    return ops[j]["lat"] + HOP
+
+
+def place(ops, seq, before, tail, eng):
+    slots = {e: ([], []) for e in "vspgy"}
+    m = len(ops)
+    t0, t1, got = [0.0] * m, [0.0] * m, [None] * m
+    end = 0.0
+    for i in seq:
+        o = ops[i]
+        rdy = tail[0][i]
+        for j, lag in before[i]:
+            if t1[j] + lag > rdy:
+                rdy = t1[j] + lag
+        ways = [(o["eng"], o["cost"])]
+        if o["alt"] is not None:
+            if eng is None:
+                ways.append(("v", o["alt"][1]))
+            elif eng[i] == "v":
+                ways = [("v", o["alt"][1])]
+        best = None
+        for e, cost in ways:
+            st, en = slots[e]
+            x = int(np.searchsorted(en, rdy, side="right")) if en else 0
+            t = rdy
+            while x < len(st) and st[x] < t + cost - 1e-6:
+                t = max(t, en[x])
+                x += 1
+            fin = t + cost + (BIAS if e != o["eng"] else 0.0)
+            if best is None or fin < best[0]:
+                best = (fin, e, t, cost, x)
+        _, e, t, cost, x = best
+        slots[e][0].insert(x, t)
+        slots[e][1].insert(x, t + cost)
+        t0[i], t1[i], got[i] = t, t + cost, e
+        end = max(end, t + cost + tail[1][i])
+    return t0, t1, got, end
+
+
+def schedule(ops):
+    m = len(ops)
+    pre = [[(j, gap_after(ops, j, i)) for j in o["dep"]] + [(j, 0.0) for j in o["ord"]] for i, o in enumerate(ops)]
+    suc = [[] for _ in range(m)]
+    for i in range(m):
+        for j, lag in pre[i]:
+            suc[j].append((i, lag))
+    rank = [0.0] * m
+    for i in range(m - 1, -1, -1):
+        rank[i] = ops[i]["cost"] + max([lag + rank[x] for x, lag in suc[i]] + [ops[i]["lat"]])
+    key = [LAM * ops[i]["c"] - rank[i] for i in range(m)]
+    for i in range(m):
+        for j, lag in pre[i]:
+            key[i] = max(key[i], key[j] + 1e-3)
+    zero, lat = [0.0] * m, [o["lat"] for o in ops]
+    free = [i for i in range(m) if ops[i]["alt"] is not None]
+    rng = np.random.default_rng(SEED)
+    best, keep = None, None
+    eng = None
+    for x in range(ROUNDS):
+        t0, t1, eng, end = place(ops, sorted(range(m), key=lambda i: (key[i], i)), pre, (zero, lat), eng)
+        if best is None or end < best[1]:
+            best = ([(i, eng[i], t0[i]) for i in sorted(range(m), key=lambda i: (t0[i], i))], end)
+        if keep is None or end < keep[2] + SLACK * (1.0 - x / ROUNDS):
+            keep = (t1, eng, end)
+        t1, eng = keep[0], list(keep[1])
+        for i in rng.choice(free, int(rng.integers(0, 3))):
+            eng[int(i)] = "s" if eng[int(i)] == "v" else "v"
+        lo = float(rng.random()) * end
+        amp = float(rng.choice([0.0, 200.0, 600.0, 1500.0]))
+        back = [-t1[i] + (amp * float(u) if lo < t1[i] < lo + 15000.0 else 0.0) for i, u in enumerate(rng.random(m))]
+        for i in range(m - 1, -1, -1):
+            for j, lag in suc[i]:
+                back[i] = max(back[i], back[j] + 1e-3)
+        b0, b1, _, _ = place(ops, sorted(range(m), key=lambda i: (back[i], -i)), suc, (lat, zero), eng)
+        key = [-b1[i] for i in range(m)]
+    return best
+
+
+ORDER = {}
+
+
+def rank_program(g, core, T, topo):
+    if T.rank_of(core) is None:
+        return
+    ops = build(g, core, T, topo)
+    depend(ops)
+    if "o" not in ORDER:
+        ORDER["o"] = schedule(ops)[0]
+    order = [x[0] for x in ORDER["o"]]
+    for i, e, _ in ORDER["o"]:
+        if ops[i]["eng"] != e:
+            ops[i]["eng"], ops[i]["fn"] = e, ops[i]["alt"][0]
+    pos = {i: x for x, i in enumerate(order)}
+    queue = {"v": g.vector, "s": g.scalar, "p": g.tensor, "g": g, "y": g.sync}
+    seen = {}
+    for i in order:
+        o = ops[i]
+        need = {}
+        o["w"] = []
+        for j in o["dep"]:
+            d = ops[j]
+            if d["sem"] is not None:
+                if (o["eng"], d["sem"][0]) not in seen:
+                    seen[(o["eng"], d["sem"][0])] = 1
+                    o["w"].append(j)
+            elif not (d["eng"] == "p" and o["eng"] == "p"):
+                if d["eng"] not in need or pos[j] > pos[need[d["eng"]]]:
+                    need[d["eng"]] = j
+        for e, j in need.items():
+            if pos[j] > seen.get((o["eng"], e), -1):
+                seen[(o["eng"], e)] = pos[j]
+                ops[j]["inc"] = True
+                o["w"].append(j)
+    count = {e: 0 for e in "vspg"}
+    for i in order:
+        o = ops[i]
+        if o.get("inc"):
+            count[o["eng"]] += 1
+            o["n"] = count[o["eng"]]
+    sent = 0
+    for i in order:
+        o = ops[i]
+        qu = queue[o["eng"]]
+        for j in o["w"]:
+            d = ops[j]
+            if d["sem"] is not None:
+                qu.wait_ge(T.sem[d["sem"][0]], d["sem"][1])
+            else:
+                qu.wait_ge(T.sem["c" + d["eng"]], d["n"])
+        ins = o["fn"]()
+        if o["sem"] is not None:
+            if len(o["sem"]) == 3:
+                sent += o["sem"][2]
+            else:
+                ins.then_inc(T.sem[o["sem"][0]], 16)
+        elif o.get("inc"):
+            ins.then_inc(T.sem["c" + o["eng"]], 1)
+    g.wait_ge(T.sem["sent"], sent)
+    waited = set(x[1] for x in seen)
+    for o in ops:
+        if o["sem"] is not None and o["sem"][0] not in waited:
+            g.wait_ge(T.sem[o["sem"][0]], o["sem"][1])

@@ -14,10 +14,11 @@ MW = 128
 NE = 8
 GP = 64
 LAM = 5000.0
-ROUNDS = 220
+ROUNDS = 2600
 BIAS = 9.0e9
-SEED = 2
-SLACK = 1000.0
+PV = 0.2
+SEED = 7
+SLACK = 600.0
 YB = 4
 
 SCRATCH = {
@@ -37,7 +38,7 @@ SCRATCH = {
     "ki": ("sbuf", [128, 32], "int32"), "nm": ("sbuf", [128, 32], "bfloat16"),
     "s0": ("sbuf", [128, 32], "int32"), "s1": ("sbuf", [128, 32], "int32"), "t1": ("sbuf", [128, 32], "int32"),
     "zz": ("sbuf", [128, 32], "int32"), "i9": ("sbuf", [128, 32], "int32"), "wv": ("sbuf", [128, 32], "int32"),
-    "lst": ("sbuf", [128, 96], "int32"), "lu": ("sbuf", [128, 96], "uint16"),
+    "lst": ("sbuf", [128, 128], "int32"), "lu": ("sbuf", [128, 128], "uint16"),
     "gw0": ("sbuf", [128, 32], "int32"), "gw1": ("sbuf", [128, 32], "int32"), "gwu": ("sbuf", [128, 32], "uint16"),
     "cc": ("sbuf", [128, 32], "int32"), "cl": ("sbuf", [128, 16], "int32"), "c16": ("sbuf", [128, 32], "int32"),
     "mc": ("sbuf", [128, 8], "float32"), "mi": ("sbuf", [128, 8], "int32"),
@@ -48,6 +49,7 @@ SCRATCH = {
     "okn": ("sbuf", [128, 512], "int32"),
     "ih": ("sbuf", [128, 128], "float16"), "ib": ("sbuf", [128, 128], "bfloat16"), "ineg": ("sbuf", [128, 128], "bfloat16"),
     "ibig": ("sbuf", [128, 128], "bfloat16"), "wblk": ("sbuf", [128, 128], "bfloat16"), "wide": ("sbuf", [128, 144], "bfloat16"),
+    "wneg": ("sbuf", [128, 144], "bfloat16"), "c257": ("sbuf", [128, 16], "float16"),
     "hb": ("sbuf", [128, 256], "bfloat16"), "dmx": ("sbuf", [128, 16], "bfloat16"), "dab": ("sbuf", [128, 16], "bfloat16"),
     "dx": ("sbuf", [128, 16], "bfloat16"),
     "bs": ("sbuf", [128, 8], "float32"), "r0": ("sbuf", [128, 128], "float32"), "r1": ("sbuf", [128, 128], "float32"),
@@ -55,7 +57,7 @@ SCRATCH = {
     "cep": ("sbuf", [128, 512], "float16"), "ck": ("sbuf", [128, 256], "float16"),
     "o2k": ("sbuf", [128, 128], "float16"), "one": ("sbuf", [128, 128], "bfloat16"),
     "rst": ("sbuf", [128, 256], "float32"), "dm": ("sbuf", [128, 256], "float32"),
-    "ut": ("sbuf", [128, 1024], "bfloat16"), "nt": ("sbuf", [128, 1024], "bfloat16"),
+    "ut": ("sbuf", [128, 1024], "bfloat16"), "ch": ("sbuf", [128, 16], "int32"),
     "st0": ("sbuf", [128, 1024], "bfloat16"), "st1": ("sbuf", [128, 1024], "bfloat16"),
 }
 for _i in range(2):
@@ -65,7 +67,7 @@ for _i in range(STEPS):
     SCRATCH["a%d" % _i] = ("sbuf", [128, 512], "float16")
     SCRATCH["say%d" % _i] = ("sbuf", [128, 512], "bfloat16")
 for _i in range(STEPS + 1):
-    SCRATCH["h%d" % _i] = ("sbuf", [128, 512], "bfloat16")
+    SCRATCH["h%d" % _i] = ("sbuf", [128, NCH * (CW + 16)], "bfloat16")
 for _n in ("ha0", "ha1", "sb", "ep0", "ep1", "kb", "yb0", "yb1"):
     SCRATCH[_n] = ("psum", [128, 512], "float32")
 
@@ -76,7 +78,11 @@ SEMAPHORES = ["cv", "cs", "cp", "cg", "sent"] + ["d%d" % _i for _i in range(NDMA
 CY, PCY, GA, SC, HOP = 1.04, 0.52, 1.56, 3.8, 120.0
 
 
-def build(g, core, T, topo):
+OTHER = []
+
+
+def build(g, core, T, topo, par=(CY, PCY, GA, SC)):
+    CY, PCY, GA, SC = par[:4]
     ops = []
     cores = list(T.cores)
     n = len(cores)
@@ -138,14 +144,16 @@ def build(g, core, T, topo):
     def gat(k):
         return 60.0 + k * GA * CY
 
-    dma("y", T.h0[:], T.heard[:], [], ["h0_%d" % c for c in range(NCH)], 1 << 17)
+    dma("y", T.tab[:, 6144:8192], T.cues[:, 2048:4096], [], ["tab1"], 11 << 16)
+    dma("y", T.tab[:, 4096:6144], T.cues[:, 0:2048], [], ["tab0"], 19 << 16)
     dma("s", T.wi[:, 0:1], T.w[:], [], ["wi"], 1 << 12)
-    dma("s", T.ai[:], T.scroll[:], [], ["ai"], 3 << 17)
-    dma("y", T.tab[:, 6144:8192], T.cues[:, 2048:4096], [], ["tab1"], 7 << 17)
-    dma("y", T.tab[:, 4096:6144], T.cues[:, 0:2048], [], ["tab0"], 11 << 17)
-    dma("s", T.thi[:, 0:1], T.th[:], [], ["thi"], 1 << 12)
-    dma("y", T.spi[:], T.spare[:], ["tab0", "tab1"], ["spi"], 1 << 20)
-    for i, j in ((3, 0), (4, 3), (2, 1), (5, 2)):
+    dma("s", T.h0[:, 16:16 + CW], T.heard[:, 0:CW], [], ["h0_0"], 2 << 16)
+    dma("s", T.ai[:, 0:CW], T.scroll[:, 0:CW], [], ["ai_0"], 6 << 16)
+    dma("s", T.thi[:, 0:1], T.th[:], [], ["thi"], 6 << 16)
+    dma("y", T.h0[:, 32 + CW:32 + C], T.heard[:, CW:C], [], ["h0_%d" % c for c in range(1, NCH)], 20 << 16)
+    dma("y", T.ai[:, CW:C], T.scroll[:, CW:C], [], ["ai_%d" % c for c in range(1, NCH)], 22 << 16)
+    dma("y", T.spi[:], T.spare[:], [], ["spi"], 38 << 16)
+    for i, j in ((1, 0), (3, 2), (4, 3), (5, 4), (6, 1), (7, 6), (8, 7)):
         ops[i]["ord"].append(j)
 
     io(T.pi[:, 0:1], [[0, 1]], 0, 1, ["pi"], 1, False)
@@ -155,7 +163,6 @@ def build(g, core, T, topo):
     op("g", lambda: g.affine_select(T.jm[:], T.jh[:], [[0, 8], [-1, 16]], ALU.is_ge, -1.0, 15 - NA, 0), ["jh"], ["jm"], 170.0 + 256 * CY)
     io(T.bi[:], [[1, 16]], 0, 0, ["bi"], 16, False)
     io(T.c16[:], [[16, 32]], 512, 0, ["c16"], 32, False)
-    io(T.nt[:, 0:512], [[0, 256], [1, 2]], 0, 0, ["nt0"], 512, True)
     io(T.vv[:], [[0, 16], [1, 16], [0, 2]], 0, -1, ["vv"], 512, False)
     io(T.okn[:], [[1, 16], [0, 16], [64, 2]], 0, 0, ["okn"], 512, False)
     io(T.kk[:], [[0, 16], [1, 16], [64, 2]], 0, 0, ["kk"], 512, True)
@@ -171,7 +178,7 @@ def build(g, core, T, topo):
     ts(T.ib[:], T.jj[:, 0:128], col(PF), None, ALU.is_equal, None, ["jj", "col"], ["ib"], 128)
     ts(T.ineg[:], T.jj[:, 0:128], col(PF), -1.0, ALU.is_equal, ALU.mult, ["jj", "col"], ["ineg"], 128)
     for c in range(NCH):
-        cp(T.a0[:, c * CW:(c + 1) * CW], T.ai[:, c * CW:(c + 1) * CW], ["ai"], ["a0_%d" % c], CW)
+        cp(T.a0[:, c * CW:(c + 1) * CW], T.ai[:, c * CW:(c + 1) * CW], ["ai_%d" % c], ["a0_%d" % c], CW)
     ts(T.ibig[:], T.ib[:], float(1 << 24), None, ALU.mult, None, ["ib"], ["ibig"], 128, 0.5)
     ts(col(G15), col(GRP), 16.0, 15.0, ALU.mult, ALU.add, ["col"], ["g15"], 1)
     ts(T.wide[:], T.jj[:], col(G15), col(WF), ALU.is_equal, ALU.mult, ["jj", "g15", "wf"], ["wide"], 144)
@@ -202,15 +209,24 @@ def build(g, core, T, topo):
     cp(T.bl[:], T.bi[:], ["bi"], ["bl"], 16)
     ts(T.cc[:], T.c16[:], col(LANE), None, ALU.add, None, ["c16", "col"], ["cc"], 32)
     ts(T.cl[:], T.cc[:, 0:16], -512.0, 2.0, ALU.add, ALU.mult, ["cc"], ["cl"], 16)
-    ms(T.nt[:, 512:1024], 1.0, ["nt1"], 512, 0.5)
+    ts(T.ch[:, 0:NC], T.cc[:, 0:NC], -496.0, None, ALU.add, None, ["cc"], ["ch"], NC)
+    for t in range(STEPS):
+        for c in range(NCH):
+            ms(T["h%d" % t][:, c * (CW + 16):c * (CW + 16) + 16], 0.0, ["hzero%d_%d" % (t, c)], 16)
     ms(T.ut[:, 512:1024], 0.0, ["ut1"], 512, 0.5)
     ms(T.st0[:, 512:1024], 0.0, ["st0_%d" % c for c in range(NCH)], 512, 0.5)
     ts(T.vw[:], T.vv[:], 15, None, ALU.bitwise_and, None, ["vv"], ["vw"], 512)
     tt(T.ut[:, 0:512], T.vw[:], T.okn[:], ALU.is_le, ["vw", "okn"], ["ut0"], 512)
     ts(T.st0[:, 0:512], T.kk[:], col(LANE), None, ALU.is_lt, None, ["kk", "col"], ["stt0"], 512)
-    either(T.st1[:, 0:512], T.st0[:, 0:512], ["stt0"], ["stt1"], vc(512), vc(512, 0.5))
+
+    def pool_copy(out, in_, rd, wr, k):
+        op("g", lambda: g.affine_select(out, in_, [[0, k]], ALU.is_ge, 0.0, 0, 0), rd, wr, 170.0 + 2 * k * CY)
+
     for e in range(2):
-        either(T.tab[:, e:2048:2], T.tab[:, 4097 - e:6144:2], ["tab0"], ["sw%d" % e], vc(1024), vc(1024, 0.5))
+        pool_copy(T.tab[:, e:2048:2], T.tab[:, 4097 - e:6144:2], ["tab0"], ["sw%d" % e], 1024)
+    pool_copy(T.st1[:, 0:512], T.st0[:, 0:512], ["stt0"], ["stt1"], 512)
+    ts(T.wneg[:], T.jj[:], col(G15), -0.0625, ALU.is_equal, ALU.mult, ["jj", "g15"], ["wneg"], 144)
+    ms(T.c257[:], 257.0 / 128.0, ["c257"], 16)
     for e in range(2):
         either(T.tab[:, 2048 + e * 1024:3072 + e * 1024], T.tab[:, 6144 + e * 1024:7168 + e * 1024], ["tab1"], ["tab%d" % (2 + e)], vc(1024), vc(1024, 0.5))
     for e in range(4):
@@ -239,17 +255,20 @@ def build(g, core, T, topo):
             ha = "ha%d" % q
             HA, X, MX = T[ha], T["xg%d" % q], T["mx%d" % q]
             r = lambda name: "%s_%d" % (name, c)
-            mm(T.sb[:, 0:CW], T.wblk[:], H[:, cs], True, True, ["wblk", h], "sb", CW)
-            act(T.yr[:, cs], T.sb[:, 0:CW], ACT.Identity, [], [r("yr")], vc(CW), ["sb"], bias=524288.0)
-            mm(HA[:, 0:CW], T.wblk[:], H[:, cs], True, False, ["wblk", h], ha, CW)
-            mm(HA[:, 0:CW], T.ih[:], A[:, cs], False, False, ["ih", a], ha, CW)
+            h0 = c * (CW + 16) + 16
+            hs = slice(h0, h0 + CW)
+            mm(T.sb[:, 0:CW], T.wblk[:], H[:, hs], True, True, ["wblk", h], "sb", CW)
+            op("s", lambda o_=T.yr[:, cs]: s.activation(o_, T.sb[:, 0:CW], ACT.Identity, bias=524288.0), [], [r("yr")], vc(CW), ["sb"],
+               alt=(lambda o_=T.yr[:, cs]: v.tensor_scalar(o_, T.sb[:, 0:CW], 524288.0, None, ALU.add), vc(CW)))
+            if t == 0:
+                mm(HA[:, 0:CW], T.ih[:], A[:, cs], True, False, ["ih", a], ha, CW)
+            else:
+                mm(HA[:, 0:CW], T.ih[:], T["a%d" % (t - 1)][:, cs], True, False, ["ih", "a%d_%d" % (t - 1, c)], ha, CW)
+                mm(HA[:, 0:CW], T.ih[:], T.mm[:, cs], False, False, ["ih", r("mm")], ha, CW)
+            mm(HA[:, 0:CW], T.wblk[:], H[:, hs], False, False, ["wblk", h], ha, CW)
             mm(HA[:, 0:CW], T.ineg[:], T.yr[:, cs], False, True, ["ineg", r("yr")], ha, CW)
-            mm(HA[:, 256:256 + CW], T.ib[:], H[:, cs], True, True, ["ib", h], ha, CW)
+            mm(HA[:, 256:256 + CW], T.ib[:], H[:, hs], True, True, ["ib", h], ha, CW)
             ts(T.off[:, cs], HA[:, 0:CW], 526336.0, None, ALU.add, None, [], [r("off")], CW, 1.0, [ha])
-            for m in range(16):
-                mm(T.sb[:, 256:256 + NC], T.wide[:, 15 - m:143 - m], H[:, c0 + m:c0 + CW:16], m == 0, m == 15, ["wide", h], "sb", NC)
-            ts(T.s0[:, ws], T.sb[:, 256:256 + NC], 2048.0, None, ALU.add, None, [], [r("s0")], NC, 1.0, ["sb"])
-            ts(T.s1[:, ws], T.s0[:, ws], 4095, None, ALU.bitwise_and, None, [r("s0")], [r("s1")], NC)
             xs = [["x%d_%d" % (q, e) for e in range(b * 128 // GP, (b + 1) * 128 // GP)] for b in range(NS)]
             for e in range(CW // GP):
                 either(X[:, e * GP * 16:(e + 1) * GP * 16], T.tab[:, 2048:8192].indirect(T.off[:, c0 + e * GP:c0 + (e + 1) * GP]),
@@ -260,7 +279,7 @@ def build(g, core, T, topo):
                 EP = T[ep]
                 bs_ = slice(c0 + b * 128, c0 + (b + 1) * 128)
                 mm(EP[:, 0:256], T.o2k[:], T.cep[:, 0:256], True, False, ["o2k", "cep0", "cep1"], ep, 256)
-                mid(EP[:, 0:256], H[:, bs_], T.hb[:], [h, "hb0", "hb1"], ep, 256)
+                mid(EP[:, 0:256], H[:, h0 + b * 128:h0 + (b + 1) * 128], T.hb[:], [h, "hb0", "hb1"], ep, 256)
                 if t > 0:
                     mid(EP[:, 128:256], STo[:, 512 + c0 + b * 128:512 + c0 + (b + 1) * 128], T.rsp[:], [sto, "rsp"], ep, 128)
                 for i in range(16 - NA):
@@ -276,7 +295,7 @@ def build(g, core, T, topo):
                     js = list(range(j0, min(NA, j0 + YB)))
                     for j in js:
                         o_ = T[yb][:, (j - j0) * 128:(j - j0 + 1) * 128]
-                        mm(o_, T.ineg[:], H[:, c0 + b * 128:c0 + (b + 1) * 128], True, False, ["ineg", h], yb, 128)
+                        mm(o_, T.ineg[:], H[:, h0 + b * 128:h0 + (b + 1) * 128], True, False, ["ineg", h], yb, 128)
                         mm(o_, T.ib[:], X[:, b * 2048 + 16 - NA + j:(b + 1) * 2048:16], False, True, ["ib"] + xs[b], yb, 128)
                     m0 = (16 - NA) * CW + b * NA * 128
                     mxr = "ab%d_%d_%d" % (q, b, j0)
@@ -287,6 +306,12 @@ def build(g, core, T, topo):
                 act(T.gg[:, bs_], EP[:, 0:128], ACT.Sign, ["mb"], [r("gg%d" % b)], vc(128), [ep], bias=T.mc[:, 2:3])
                 op("v", lambda o_=T.scp[:, bs_], i_=EP[:, 128:256]: v.tensor_tensor_scan(o_, T.rst[:, 0:128], i_, 0.0, ALU.add, ALU.min),
                    ["rst"], [r("scp%d" % b)], vc(128), [ep])
+            sw_ = T.kb[:, 288:288 + NC]
+            mm(sw_, T.o2k[:], T.c257[:, 0:NC], True, False, ["o2k", "c257"], "kb", NC)
+            for m in range(16):
+                mm(sw_, T.wide[:, 15 - m:143 - m], H[:, h0 + m:h0 + CW:16], False, False, ["wide", h], "kb", NC)
+            for m in range(16):
+                mm(sw_, T.wneg[:, 15 - m:143 - m], T.yr[:, c0 + m:c0 + CW:16], False, m == 15, ["wneg", r("yr")], "kb", NC)
             mm(T.kb[:, 0:CW], T.o2k[:], T.ck[:, 0:CW], True, False, ["o2k"] + cks, "kb", CW)
             for b in range(NS):
                 if t > 0:
@@ -301,22 +326,24 @@ def build(g, core, T, topo):
             for b in range(NS):
                 mm(T.kb[:, 256 + b * 8:256 + (b + 1) * 8], T.ll[:, c0 + b * 128:c0 + (b + 1) * 128], T.bs[:], True, True, [r("ll"), "bs"], "kb", 8, 4.0)
             kw = T.kb[:, 256:256 + NC]
-            l0 = c * 3 * NC
+            l0 = c * 4 * NC
             cp(T.ki[:, ws], kw, [], [r("ki")], NC, 1.0, ["kb"])
             ts(T.nm[:, ws], kw, -240.0 * 65536.0, None, ALU.is_ge, None, [], [r("nm")], NC, 1.0, ["kb"])
             ts(T.lst[:, l0 + NC:l0 + 2 * NC], T.ki[:, ws], 4095, None, ALU.bitwise_and, None, [r("ki")], [r("bk")], NC)
             ts(T.i9[:, ws], T.ki[:, ws], 11, 511, ALU.arith_shift_right, ALU.bitwise_and, [r("ki")], [r("i9")], NC)
-            tt(T.t1[:, ws], T.nm[:, ws], T.s1[:, ws], ALU.mult, [r("nm"), r("s1")], [r("t1")], NC)
+            tt(T.t1[:, ws], T.nm[:, ws], sw_, ALU.mult, [r("nm")], [r("t1")], NC, 1.0, ["kb"])
             WV, wv = (T.cc, "cc") if t == 0 else (T.wv, r("wv"))
             tt(T.zz[:, ws], T.nm[:, ws], WV[:, ws], ALU.mult, [r("nm"), wv], [r("zz")], NC)
             tt(T.lst[:, l0:l0 + NC], T.t1[:, ws], T.lst[:, l0 + NC:l0 + 2 * NC], ALU.add, [r("t1"), r("bk")], [r("spx")], NC)
             tt(T.lst[:, l0 + 2 * NC:l0 + 3 * NC], T.i9[:, ws], T.zz[:, ws], ALU.max, [r("i9"), r("zz")], [r("iu")], NC)
             cp(T.lu[:, l0:l0 + 3 * NC], T.lst[:, l0:l0 + 3 * NC], [r("spx"), r("bk"), r("iu")], [r("lu")], 3 * NC)
+            tt(T.lst[:, l0 + 3 * NC:l0 + 4 * NC], T.nm[:, ws], T.ch[:, 0:NC], ALU.mult, [r("nm"), "ch"], [r("z0")], NC)
+            cp(T.lu[:, l0 + 3 * NC:l0 + 4 * NC], T.lst[:, l0 + 3 * NC:l0 + 4 * NC], [r("z0")], [r("lz")], NC)
             if not last:
                 tt(T.wv[:, ws], T.cc[:, ws], T.zz[:, ws], ALU.subtract, ["cc", r("zz")], [r("wv")], NC)
             lsp, lbk, liu = T.lu[:, l0:l0 + NC], T.lu[:, l0 + NC:l0 + 2 * NC], T.lu[:, l0 + 2 * NC:l0 + 3 * NC]
-            op("v", lambda o_=T.hz[:, cs], l_=liu, h_=H[:, cs]: v.tensor_tensor(o_, T.nt[:, 0:1024].indirect(l_), h_, ALU.mult),
-               ["nt0", "nt1", r("lu"), h], [r("hz")], gat(CW))
+            either(T.hz[:, cs], H[:, h0 - 16:h0 + CW].indirect(T.lu[:, l0 + 3 * NC:l0 + 4 * NC]),
+                   ["hzero%d_%d" % (t, c), r("lz"), h], [r("hz")], gat(CW), gat(CW))
             op("v", lambda o_=T.yy[:, cs], l_=lsp, h_=T.hz[:, cs]: v.tensor_tensor(o_, T.tab[:, 0:8192].indirect(l_), h_, ALU.subtract),
                tabs + ["sw0", "sw1", r("lu"), r("hz")], [r("yy")], gat(CW))
             say = "say%d_%d" % (t, c)
@@ -327,7 +354,7 @@ def build(g, core, T, topo):
                 msk |= 1 << e
             got = len(topo.engines(src, core)[:NE])
             arr = "arr%d_%d" % (t, c)
-            op("g", lambda o_=T["h%d" % (t + 1)][:, cs], i_=T["say%d" % t][:, cs], a_=arr, pid=pid, rid=rid, msk=msk:
+            op("g", lambda o_=T["h%d" % (t + 1)][:, hs], i_=T["say%d" % t][:, cs], a_=arr, pid=pid, rid=rid, msk=msk:
                g.remote_dma(o_, i_, T.sem[a_], T.sem["sent"], pid, rid, msk),
                [say], ["h%d_%d" % (t + 1, c)], 300.0, lat=2500.0, sem=(arr, got, len(topo.engines(core, dst)[:NE])))
             if t == 0:
@@ -341,11 +368,18 @@ def build(g, core, T, topo):
             op("v", lambda o_=T.mm[:, cs], l_=liu, t_=T.tt[:, cs]: v.tensor_tensor(o_, T.ut[:, 0:1024].indirect(l_), t_, ALU.mult),
                ["ut0", "ut1", r("lu"), r("tt")], [r("mm")], gat(CW))
             if last:
-                tt(T.af[:, cs], A[:, cs], T.mm[:, cs], ALU.add, [a, r("mm")], [r("af")], CW)
+                mm(HA[:, 0:CW], T.ih[:], A[:, cs], True, False, ["ih", a], ha, CW)
+                mm(HA[:, 0:CW], T.ih[:], T.mm[:, cs], False, True, ["ih", r("mm")], ha, CW)
+                act(T.af[:, cs], HA[:, 0:CW], ACT.Copy, [], [r("af")], vc(CW), [ha])
                 dma("y", T.ys[:, cs], T.af[:, cs], [r("af")], [r("ys")], CW * 512)
-                dma("y", T.yh[:, cs], T["h%d" % STEPS][:, cs], ["h%d_%d" % (STEPS, c)], [r("yh")], CW * 256)
+                dma("y", T.yh[:, cs], T["h%d" % STEPS][:, hs], ["h%d_%d" % (STEPS, c)], [r("yh")], CW * 256)
             else:
-                tt(T["a%d" % (t + 1)][:, cs], A[:, cs], T.mm[:, cs], ALU.add, [a, r("mm")], ["a%d_%d" % (t + 1, c)], CW)
+                an = "a%d_%d" % (t + 1, c)
+                dma("y", T["a%d" % (t + 1)][:, cs], A[:, cs], [a], [an], CW * 256)
+                sem = "d%d" % nd[0]
+                nd[0] += 1
+                op("g", lambda o_=T["a%d" % (t + 1)][:, cs], i_=T.mm[:, cs]: g.dma_start(o_, i_, accum_op=ALU.add),
+                   [an, r("mm")], [an], 800.0, lat=2500.0, sem=(sem, 16))
                 either(STn[:, 512 + c0:512 + c0 + CW], STo[:, 0:1024].indirect(liu),
                        ["stt%d" % (t % 2), r("lu")] + ["st%d_%d" % (t % 2, e) for e in range(NCH)], ["st%d_%d" % ((t + 1) % 2, c)], gat(CW), gat(CW))
             if last and (c + 1) * CW == 256:
@@ -431,7 +465,13 @@ def place(ops, seq, before, tail, eng):
         best = None
         for e, cost in ways:
             st, en = slots[e]
-            x = int(np.searchsorted(en, rdy, side="right")) if en else 0
+            x, hi = 0, len(en)
+            while x < hi:
+                md = (x + hi) >> 1
+                if en[md] <= rdy:
+                    x = md + 1
+                else:
+                    hi = md
             t = rdy
             while x < len(st) and st[x] < t + cost - 1e-6:
                 t = max(t, en[x])
@@ -447,7 +487,25 @@ def place(ops, seq, before, tail, eng):
     return t0, t1, got, end
 
 
-def schedule(ops):
+def rerun(ops, oth, seq, eng, pre, more):
+    fin = [0.0] * len(ops)
+    free = {e: 0.0 for e in "vspgy"}
+    end = 0.0
+    for i in seq:
+        e = eng[i]
+        t = free[e]
+        for j, lag in pre[i]:
+            u = fin[j] + (lag + more if lag > 0.0 else 0.0)
+            if u > t:
+                t = u
+        t += oth[i]["cost"] if e == ops[i]["eng"] else oth[i]["alt"][1]
+        fin[i] = free[e] = t
+        if t + ops[i]["lat"] > end:
+            end = t + ops[i]["lat"]
+    return end
+
+
+def schedule(ops, others):
     m = len(ops)
     pre = [[(j, gap_after(ops, j, i)) for j in o["dep"]] + [(j, 0.0) for j in o["ord"]] for i, o in enumerate(ops)]
     suc = [[] for _ in range(m)]
@@ -468,13 +526,17 @@ def schedule(ops):
     eng = None
     for x in range(ROUNDS):
         t0, t1, eng, end = place(ops, sorted(range(m), key=lambda i: (key[i], i)), pre, (zero, lat), eng)
+        seq = sorted(range(m), key=lambda i: (t0[i], i))
+        for oth, par in others:
+            end += par[5] * (rerun(ops, oth, seq, eng, pre, par[4] - HOP))
+        end /= 1 + len(others)
         if best is None or end < best[1]:
-            best = ([(i, eng[i], t0[i]) for i in sorted(range(m), key=lambda i: (t0[i], i))], end)
+            best = ([(i, eng[i], t0[i]) for i in seq], end)
         if keep is None or end < keep[2] + SLACK * (1.0 - x / ROUNDS):
             keep = (t1, eng, end)
         t1, eng = keep[0], list(keep[1])
         for i in rng.choice(free, int(rng.integers(0, 3))):
-            eng[int(i)] = "s" if eng[int(i)] == "v" else "v"
+            eng[int(i)] = "v" if rng.random() < PV else "s"
         lo = float(rng.random()) * end
         amp = float(rng.choice([0.0, 200.0, 600.0, 1500.0]))
         back = [-t1[i] + (amp * float(u) if lo < t1[i] < lo + 15000.0 else 0.0) for i, u in enumerate(rng.random(m))]
@@ -495,7 +557,7 @@ def rank_program(g, core, T, topo):
     ops = build(g, core, T, topo)
     depend(ops)
     if "o" not in ORDER:
-        ORDER["o"] = schedule(ops)[0]
+        ORDER["o"] = schedule(ops, [(build(g, core, T, topo, par), par) for par in OTHER])[0]
     order = [x[0] for x in ORDER["o"]]
     for i, e, _ in ORDER["o"]:
         if ops[i]["eng"] != e:

@@ -5,84 +5,93 @@ from concourse.mybir import dt, AluOpType, AxisListType, ActivationFunctionType
 ALU = AluOpType
 ACT = ActivationFunctionType
 C, V, VX, STEPS = 512, 2048, 4096, 4
-NCH = 2
-CW = C // NCH
-NS = CW // 128
-NC = CW // 16
-NA = 8
-MW = 128
+WIDTHS = (256, 256)
+NA = 6
+YB = 3
+NCUT = 2
+GPC = 1
+NH = 1
+PG = 4
 NE = 8
-GP = 64
-LAM = 5000.0
-ROUNDS = 2600
-BIAS = 9.0e9
-PV = 0.2
-SEED = 7
-SLACK = 600.0
-YB = 4
+LUT = 272
+LAM = 4000.0
+ROUNDS = 1500
+PV = 0.5
+FLIP = 2
+SEED = 5
+SLACK = 200.0
+MOVES = 40000
+HEAT = 80.0
 
-SCRATCH = {
-    "tab": ("sbuf", [128, 8192], "bfloat16"),
-    "book": ("sbuf", [128, 6144], "float32"),
-    "spi": ("sbuf", [128, 2048], "int32"),
-    "g2": ("sbuf", [128, 2048], "float32"),
-    "ai": ("sbuf", [128, 512], "int32"),
-    "thi": ("sbuf", [128, 8], "int32"), "wi": ("sbuf", [128, 8], "int32"),
-    "af": ("sbuf", [128, 512], "float32"),
-    "tt": ("sbuf", [128, 512], "float16"), "mm": ("sbuf", [128, 512], "float16"),
-    "yr": ("sbuf", [128, 512], "bfloat16"), "off": ("sbuf", [128, 512], "uint16"),
-    "hz": ("sbuf", [128, 512], "bfloat16"), "yy": ("sbuf", [128, 512], "bfloat16"),
-    "gg": ("sbuf", [128, 512], "bfloat16"),
-    "scp": ("sbuf", [128, 512], "float32"), "sck": ("sbuf", [128, 512], "float32"), "ll": ("sbuf", [128, 512], "float32"),
-    "km": ("sbuf", [128, 32], "float32"),
-    "ki": ("sbuf", [128, 32], "int32"), "nm": ("sbuf", [128, 32], "bfloat16"),
-    "s0": ("sbuf", [128, 32], "int32"), "s1": ("sbuf", [128, 32], "int32"), "t1": ("sbuf", [128, 32], "int32"),
-    "zz": ("sbuf", [128, 32], "int32"), "i9": ("sbuf", [128, 32], "int32"), "wv": ("sbuf", [128, 32], "int32"),
-    "lst": ("sbuf", [128, 128], "int32"), "lu": ("sbuf", [128, 128], "uint16"),
-    "gw0": ("sbuf", [128, 32], "int32"), "gw1": ("sbuf", [128, 32], "int32"), "gwu": ("sbuf", [128, 32], "uint16"),
-    "cc": ("sbuf", [128, 32], "int32"), "cl": ("sbuf", [128, 16], "int32"), "c16": ("sbuf", [128, 32], "int32"),
-    "mc": ("sbuf", [128, 8], "float32"), "mi": ("sbuf", [128, 8], "int32"),
-    "pi": ("sbuf", [128, 8], "int32"), "pj": ("sbuf", [128, 8], "int32"), "col": ("sbuf", [128, 16], "float32"),
-    "jj": ("sbuf", [128, 144], "float32"), "jl": ("sbuf", [128, 256], "float32"), "jh": ("sbuf", [128, 128], "float32"),
-    "jm": ("sbuf", [128, 128], "float32"), "bi": ("sbuf", [128, 16], "int32"), "bl": ("sbuf", [128, 16], "uint16"),
-    "kk": ("sbuf", [128, 512], "float32"), "vv": ("sbuf", [128, 512], "int32"), "vw": ("sbuf", [128, 512], "int32"),
-    "okn": ("sbuf", [128, 512], "int32"),
-    "ih": ("sbuf", [128, 128], "float16"), "ib": ("sbuf", [128, 128], "bfloat16"), "ineg": ("sbuf", [128, 128], "bfloat16"),
-    "ibig": ("sbuf", [128, 128], "bfloat16"), "wblk": ("sbuf", [128, 128], "bfloat16"), "wide": ("sbuf", [128, 144], "bfloat16"),
-    "wneg": ("sbuf", [128, 144], "bfloat16"), "c257": ("sbuf", [128, 16], "float16"),
-    "hb": ("sbuf", [128, 256], "bfloat16"), "dmx": ("sbuf", [128, 16], "bfloat16"), "dab": ("sbuf", [128, 16], "bfloat16"),
-    "dx": ("sbuf", [128, 16], "bfloat16"),
-    "bs": ("sbuf", [128, 8], "float32"), "r0": ("sbuf", [128, 128], "float32"), "r1": ("sbuf", [128, 128], "float32"),
-    "rsp": ("sbuf", [128, 128], "bfloat16"), "rsk": ("sbuf", [128, 128], "bfloat16"),
-    "cep": ("sbuf", [128, 512], "float16"), "ck": ("sbuf", [128, 256], "float16"),
-    "o2k": ("sbuf", [128, 128], "float16"), "one": ("sbuf", [128, 128], "bfloat16"),
-    "rst": ("sbuf", [128, 256], "float32"), "dm": ("sbuf", [128, 256], "float32"),
-    "ut": ("sbuf", [128, 1024], "bfloat16"), "ch": ("sbuf", [128, 16], "int32"),
-    "st0": ("sbuf", [128, 1024], "bfloat16"), "st1": ("sbuf", [128, 1024], "bfloat16"),
-}
-for _i in range(2):
-    SCRATCH["xg%d" % _i] = ("sbuf", [128, 16 * CW], "bfloat16")
-    SCRATCH["mx%d" % _i] = ("sbuf", [128, 16 * CW], "bfloat16")
-for _i in range(STEPS):
-    SCRATCH["a%d" % _i] = ("sbuf", [128, 512], "float16")
-    SCRATCH["say%d" % _i] = ("sbuf", [128, 512], "bfloat16")
-for _i in range(STEPS + 1):
-    SCRATCH["h%d" % _i] = ("sbuf", [128, NCH * (CW + 16)], "bfloat16")
-for _n in ("ha0", "ha1", "sb", "ep0", "ep1", "kb", "yb0", "yb1"):
-    SCRATCH[_n] = ("psum", [128, 512], "float32")
 
-NDMA = 40
+def buffers():
+    nch = len(WIDTHS)
+    b = {
+        "tab": ("sbuf", [128, 8192], "bfloat16"),
+        "book": ("sbuf", [128, 6144], "int32"),
+        "ai": ("sbuf", [128, 512], "int32"),
+        "thi": ("sbuf", [128, 8], "int32"), "wi": ("sbuf", [128, 8], "int32"),
+        "af": ("sbuf", [128, 512], "float32"),
+        "tt": ("sbuf", [128, 512], "float16"), "mm": ("sbuf", [128, 512], "float16"),
+        "yr": ("sbuf", [128, 512], "bfloat16"), "off": ("sbuf", [128, 512], "uint16"),
+        "yw": ("sbuf", [128, 16 * nch], "bfloat16"), "sm": ("sbuf", [128, 16 * nch], "float32"),
+        "hz": ("sbuf", [128, 512], "bfloat16"), "yy": ("sbuf", [128, 512], "bfloat16"),
+        "gg": ("sbuf", [128, 256 * nch], "bfloat16"), "hr": ("sbuf", [128, 768], "bfloat16"),
+        "scp": ("sbuf", [128, 256 * nch], "float32"), "sck": ("sbuf", [128, 256 * nch], "float32"), "ll": ("sbuf", [128, 128 * nch], "float32"),
+        "km": ("sbuf", [128, 16 * nch], "float32"), "nm": ("sbuf", [128, 48 * nch], "float16"),
+        "qq": ("sbuf", [128, 112 * nch], "int32"), "pr": ("sbuf", [128, 64 * nch], "float32"), "lu": ("sbuf", [128, 96 * nch], "uint16"),
+        "mc": ("sbuf", [128, 8], "float32"), "mj": ("sbuf", [128, 16], "float32"),
+        "pi": ("sbuf", [128, 8], "int32"), "pj": ("sbuf", [128, 8], "int32"), "col": ("sbuf", [128, 16], "float32"),
+        "jj": ("sbuf", [128, 144], "bfloat16"), "jl": ("sbuf", [128, 256], "bfloat16"), "jh": ("sbuf", [128, 128], "bfloat16"),
+        "jm": ("sbuf", [128, 128], "bfloat16"), "jd": ("sbuf", [128, 128], "bfloat16"), "tk": ("sbuf", [128, 256], "bfloat16"),
+        "loc": ("sbuf", [128, 32 * nch], "float32"), "l2": ("sbuf", [128, 32 * nch], "float16"), "bl": ("sbuf", [128, 16], "uint16"),
+        "ih": ("sbuf", [128, 128], "float16"), "ib": ("sbuf", [128, 128], "bfloat16"), "ineg": ("sbuf", [128, 128], "bfloat16"),
+        "inf": ("sbuf", [128, 128], "float32"), "i16": ("sbuf", [128, 128], "bfloat16"),
+        "ibig": ("sbuf", [128, 128], "bfloat16"), "wblk": ("sbuf", [128, 128], "bfloat16"), "wide": ("sbuf", [128, 144], "bfloat16"),
+        "cz": ("sbuf", [128, 160], "float16"), "cap": ("sbuf", [128, 32], "float32"),
+        "hb": ("sbuf", [128, 256], "bfloat16"), "dmx": ("sbuf", [128, 16], "bfloat16"), "dx": ("sbuf", [128, 16], "bfloat16"),
+        "bs": ("sbuf", [128, 64], "float32"), "r0": ("sbuf", [128, 128], "bfloat16"),
+        "rsp": ("sbuf", [128, 128], "bfloat16"), "rsk": ("sbuf", [128, 128], "bfloat16"),
+        "cep": ("sbuf", [128, 256], "float16"), "ck": ("sbuf", [128, 256], "float16"),
+        "o2k": ("sbuf", [128, 128], "float16"),
+        "rst": ("sbuf", [128, 256], "bfloat16"), "dm": ("sbuf", [128, 128], "bfloat16"),
+        "ut": ("sbuf", [128, LUT + 512], "bfloat16"),
+        "st0": ("sbuf", [128, LUT + 512], "bfloat16"), "st1": ("sbuf", [128, LUT + 512], "bfloat16"),
+    }
+    for i, w in enumerate(WIDTHS):
+        b["xg%d" % i] = ("sbuf", [128, 24 * w + 32], "bfloat16")
+        b["mx%d" % i] = ("sbuf", [128, 24 * w], "bfloat16")
+        b["g2%d" % i] = ("sbuf", [128, 4112], "float32")
+    for i in range(STEPS):
+        b["a%d" % i] = ("sbuf", [128, 512], "float16")
+        b["say%d" % i] = ("sbuf", [128, 512], "bfloat16")
+    for i in range(STEPS + 1):
+        b["h%d" % i] = ("sbuf", [128, 16 + C], "bfloat16")
+    for x in ("of0", "of1", "ep0", "ep1", "kb0", "kb1", "yb", "xb"):
+        b[x] = ("psum", [128, 512], "float32")
+    return b
+
+
+SCRATCH = buffers()
+NDMA = 11 + 16 * len(WIDTHS)
 SEMAPHORES = ["cv", "cs", "cp", "cg", "sent"] + ["d%d" % _i for _i in range(NDMA)] + \
-             ["arr%d_%d" % (_t, _c) for _t in range(STEPS) for _c in range(NCH)]
+             ["arr%d_%d_%d" % (_t, _c, _f) for _t in range(STEPS) for _c in range(len(WIDTHS)) for _f in range(NH)]
 
-CY, PCY, GA, SC, HOP = 1.04, 0.52, 1.56, 3.8, 120.0
-
-
+PAR = (0.83, 0.43, 1.56, 3.8, (190.0, 200.0), 5.0, 1600.0, 350.0, 700.0, 300.0, (10.0, 0.0), 1400.0)
+FIRST = 2000.0
+ONV = {"yr": 1, "gg": 1, "hz": 1, "yw": 1, "hr": 1, "af": 0, "st": 0, "k": 0}
+VG = {None: (), (0, 0): (1, 3)}
 OTHER = []
 
 
-def build(g, core, T, topo, par=(CY, PCY, GA, SC)):
-    CY, PCY, GA, SC = par[:4]
+def cuts(lo, hi, n):
+    return [lo + 2 * ((hi - lo) // 2 * i // n) for i in range(n + 1)]
+
+
+def build(g, core, T, topo, par=None):
+    CY, PCY, GA, SC, HOP, FIX, DL, RATE, RL, GI, SFIX, RB = par or PAR
+    NCH = len(WIDTHS)
+    C0 = [sum(WIDTHS[:c]) for c in range(NCH + 1)]
     ops = []
     cores = list(T.cores)
     n = len(cores)
@@ -91,11 +100,12 @@ def build(g, core, T, topo, par=(CY, PCY, GA, SC)):
 
     now = [0]
 
-    def op(eng, fn, rd, wr, cost, banks=(), lat=0.0, sem=None, alt=None):
-        ops.append({"ord": [], "alt": alt, "c": now[0], "eng": eng, "fn": fn, "rd": list(rd), "wr": list(wr), "bk": list(banks), "cost": cost, "lat": lat, "sem": sem})
+    def op(eng, fn, rd, wr, cost, banks=(), lat=0.0, sem=None, alt=None, onv=0):
+        ops.append({"onv": onv, "ord": [], "alt": alt, "c": now[0], "eng": eng, "fn": fn, "rd": list(rd), "wr": list(wr), "bk": list(banks),
+                    "cost": cost * (1.25 if eng == "g" and sem is None else 1.0) + (SFIX[0] + SFIX[1] * cost if eng == "s" and sem is None else 0.0), "lat": lat, "sem": sem, "hop": HOP})
 
     def vc(k, f=1.0):
-        return max(64.0, k * f) * CY + 30.0
+        return max(64.0, k * f) * CY + FIX
 
     def ts(out, in0, s1, s2, o0, o1, rd, wr, k, f=1.0, banks=()):
         if o1 is None:
@@ -112,14 +122,18 @@ def build(g, core, T, topo, par=(CY, PCY, GA, SC)):
     def ms(ap, val, wr, k, f=1.0):
         op("v", lambda: v.memset(ap, val), [], wr, vc(k, f))
 
-    def act(out, in_, fn, rd, wr, cost, banks=(), bias=None):
-        if bias is None:
-            op("s", lambda: s.activation(out, in_, fn), rd, wr, cost, banks)
-        else:
-            op("s", lambda: s.activation(out, in_, fn, bias=bias), rd, wr, cost, banks)
+    def scan(out, d0, d1, o0, o1, rd, wr, k, f=1.0, banks=()):
+        op("v", lambda: v.tensor_tensor_scan(out, d0, d1, 0.0, o0, o1), rd, wr, vc(k, f), banks)
 
-    def either(out, in_, rd, wr, cost_s, cost_v):
-        op("s", lambda: s.activation(out, in_, ACT.Copy), rd, wr, cost_s, alt=(lambda: v.tensor_copy(out, in_), cost_v))
+    def act(out, in_, fn, rd, wr, cost, banks=()):
+        op("s", lambda: s.activation(out, in_, fn), rd, wr, cost, banks)
+
+    def either(onv, out, in_, rd, wr, cost_s, cost_v, add=None, banks=()):
+        if add is None:
+            op("s", lambda: s.activation(out, in_, ACT.Copy), rd, wr, cost_s, banks, alt=(lambda: v.tensor_copy(out, in_), cost_v), onv=onv)
+        else:
+            op("s", lambda: s.activation(out, in_, ACT.Identity, bias=add), rd, wr, cost_s, banks,
+               alt=(lambda: v.tensor_scalar(out, in_, add, None, ALU.add), cost_v), onv=onv)
 
     def mm(out, lhs, rhs, st, sp, rd, bank, k, f=1.0):
         op("p", lambda: p.matmul(out, lhs, rhs, st, sp), rd, [bank], max(64.0, k) * f * PCY)
@@ -127,116 +141,138 @@ def build(g, core, T, topo, par=(CY, PCY, GA, SC)):
     def mid(out, lhs, rhs, rd, bank, k):
         op("p", lambda: p.matmul(out, lhs, rhs, False, False), rd, [], max(64.0, k) * PCY, [bank])
 
-    def io(out, pat, base, cm, wr, k, flt):
+    def mms(calls, rd, wr, banks, k):
+        op("p", lambda: [p.matmul(*x) for x in calls][-1], rd, wr, len(calls) * max(64.0, k) * PCY, banks)
+
+    def io(out, pat, base, cm, wr, k, flt=True):
         if flt:
             op("g", lambda: g.iota(out, pat, base, cm, allow_small_or_imprecise_dtypes=True), [], wr, 130.0 + 2 * k * CY)
         else:
             op("g", lambda: g.iota(out, pat, base, cm), [], wr, 130.0 + 2 * k * CY)
 
+    def pool_copy(out, in_, rd, wr, k):
+        op("g", lambda: g.affine_select(out, in_, [[0, k]], ALU.is_ge, 0.0, 0, 0), rd, wr, 170.0 + 2 * k * CY)
+
     nd = [0]
 
-    def dma(q, out, in_, rd, wr, nbytes):
+    def flight(q, fn, rd, wr, cost, lat, busy, sem, gate=()):
+        op(q, fn, rd, wr, cost, lat=lat, sem=sem)
+        ops[-1]["gate"] = list(gate)
+        op("d", None, rd, wr, busy, sem=sem)
+
+    def dma(q, out, in_, rd, wr, nbytes, gate=()):
         sem = "d%d" % nd[0]
         nd[0] += 1
         e = y if q == "y" else s
-        op(q, lambda: e.dma_start(out, in_), rd, wr, 60.0, lat=1800.0 + nbytes / 150.0, sem=(sem, 16))
+        flight(q, lambda: e.dma_start(out, in_), rd, wr, 60.0, DL, 240.0 + nbytes / RATE, (sem, 16), gate)
 
     def gat(k):
         return 60.0 + k * GA * CY
 
-    dma("y", T.tab[:, 6144:8192], T.cues[:, 2048:4096], [], ["tab1"], 11 << 16)
-    dma("y", T.tab[:, 4096:6144], T.cues[:, 0:2048], [], ["tab0"], 19 << 16)
-    dma("s", T.wi[:, 0:1], T.w[:], [], ["wi"], 1 << 12)
-    dma("s", T.h0[:, 16:16 + CW], T.heard[:, 0:CW], [], ["h0_0"], 2 << 16)
-    dma("s", T.ai[:, 0:CW], T.scroll[:, 0:CW], [], ["ai_0"], 6 << 16)
-    dma("s", T.thi[:, 0:1], T.th[:], [], ["thi"], 6 << 16)
-    dma("y", T.h0[:, 32 + CW:32 + C], T.heard[:, CW:C], [], ["h0_%d" % c for c in range(1, NCH)], 20 << 16)
-    dma("y", T.ai[:, CW:C], T.scroll[:, CW:C], [], ["ai_%d" % c for c in range(1, NCH)], 22 << 16)
-    dma("y", T.spi[:], T.spare[:], [], ["spi"], 38 << 16)
-    for i, j in ((1, 0), (3, 2), (4, 3), (5, 4), (6, 1), (7, 6), (8, 7)):
-        ops[i]["ord"].append(j)
+    W0 = WIDTHS[0]
+    dma("s", T.wi[:, 0:1], T.w[:], [], ["wi"], 512)
+    dma("y", T.h0[:, 16:16 + W0], T.heard[:, 0:W0], [], ["h0_0_%d" % f for f in range(NH)], 256 * W0)
+    dma("s", T.ai[:, 0:W0], T.scroll[:, 0:W0], [], ["ai_0"], 512 * W0)
+    dma("y", T.tab[:, 2048:4096], T.cues[:, 2048:4096], [], ["tab1"], 1 << 19)
+    dma("y", T.tab[:, 4096:6160], T.cues[:, 0:2064], [], ["tab0"], 1 << 19)
+    dma("y", T.h0[:, 16 + W0:16 + C], T.heard[:, W0:C], [], ["h0_%d_%d" % (c, f) for c in range(1, NCH) for f in range(NH)], 256 * (C - W0))
+    dma("y", T.ai[:, W0:C], T.scroll[:, W0:C], [], ["ai_%d" % c for c in range(1, NCH)], 512 * (C - W0))
+    dma("y", T.thi[:, 0:1], T.th[:], [], ["thi"], 512)
+    dma("y", T.tab[:, 6160:8192], T.cues[:, 2064:4096], [], ["tab2"], 1 << 19)
+    dma("y", T.book[:, 0:2048], T.spare[:], [], ["spare"], 1 << 20)
+    dma("y", T.book[:, 2048:4096], T.spare[:], [], ["gap"], 1 << 20)
+    for i, j in ((2, 0), (3, 1), (4, 3), (5, 4), (6, 5), (7, 6), (8, 7), (9, 8), (10, 9)):
+        ops[2 * i]["ord"].append(2 * j)
+    for i in range(1, 11):
+        ops[2 * i + 1]["ord"].append(2 * i - 1)
 
     io(T.pi[:, 0:1], [[0, 1]], 0, 1, ["pi"], 1, False)
-    io(T.jj[:], [[1, 144]], 0, 0, ["jj"], 144, True)
-    io(T.jh[:], [[1, 8], [0, 16]], 0, 0, ["jh"], 128, True)
-    io(T.jl[:], [[0, 16], [1, 16]], 0, 0, ["jl"], 256, True)
-    op("g", lambda: g.affine_select(T.jm[:], T.jh[:], [[0, 8], [-1, 16]], ALU.is_ge, -1.0, 15 - NA, 0), ["jh"], ["jm"], 170.0 + 256 * CY)
-    io(T.bi[:], [[1, 16]], 0, 0, ["bi"], 16, False)
-    io(T.c16[:], [[16, 32]], 512, 0, ["c16"], 32, False)
-    io(T.vv[:], [[0, 16], [1, 16], [0, 2]], 0, -1, ["vv"], 512, False)
-    io(T.okn[:], [[1, 16], [0, 16], [64, 2]], 0, 0, ["okn"], 512, False)
-    io(T.kk[:], [[0, 16], [1, 16], [64, 2]], 0, 0, ["kk"], 512, True)
-    col = lambda j: T.col[:, j:j + 1]
-    PF, LANE, GRP, WF, THN, L2, L34, G15 = 0, 1, 2, 3, 4, 5, 6, 7
-    cp(T.pj[:, 0:1], T.pi[:, 0:1], ["pi"], ["pj0"], 1)
-    ts(T.pj[:, 1:2], T.pi[:, 0:1], 15, None, ALU.bitwise_and, None, ["pi"], ["pj1"], 1)
-    ts(T.pj[:, 2:3], T.pi[:, 0:1], 4, None, ALU.arith_shift_right, None, ["pi"], ["pj2"], 1)
-    cp(T.col[:, 0:3], T.pj[:, 0:3], ["pj0", "pj1", "pj2"], ["col"], 3)
-    cp(col(WF), T.wi[:, 0:1], ["wi"], ["wf"], 1)
-    ts(T.wblk[:], T.jh[:], col(GRP), col(WF), ALU.is_equal, ALU.mult, ["jh", "col", "wf"], ["wblk"], 128)
-    ts(T.ih[:], T.jj[:, 0:128], col(PF), None, ALU.is_equal, None, ["jj", "col"], ["ih"], 128)
-    ts(T.ib[:], T.jj[:, 0:128], col(PF), None, ALU.is_equal, None, ["jj", "col"], ["ib"], 128)
-    ts(T.ineg[:], T.jj[:, 0:128], col(PF), -1.0, ALU.is_equal, ALU.mult, ["jj", "col"], ["ineg"], 128)
+    io(T.jh[:], [[1, 8], [0, 16]], 0, 0, ["jh"], 128)
+    io(T.jj[:], [[1, 144]], 0, 0, ["jj"], 144)
+    io(T.jl[:], [[0, 16], [1, 16]], 0, 0, ["jl"], 256)
     for c in range(NCH):
-        cp(T.a0[:, c * CW:(c + 1) * CW], T.ai[:, c * CW:(c + 1) * CW], ["ai_%d" % c], ["a0_%d" % c], CW)
-    ts(T.ibig[:], T.ib[:], float(1 << 24), None, ALU.mult, None, ["ib"], ["ibig"], 128, 0.5)
+        io(T.loc[:, 32 * c:32 * c + 32], [[0, 2], [16, 16]], 16 + C0[c], 1, ["loc%d" % c], 32)
+    io(T.jd[:], [[0, 8], [1, 8], [0, 2]], 0, 0, ["jd"], 128)
+    io(T.tk[:], [[1, 16], [-1, 16]], 0, 0, ["tk"], 256)
+    if NA:
+        op("g", lambda: g.affine_select(T.jm[:], T.jh[:], [[0, 8], [-1, 16]], ALU.is_ge, -1.0, 15 - NA, 0), ["jh"], ["jm"], 170.0 + 256 * CY)
+    JM, jm = (T.jm, "jm") if NA else (T.jh, "jh")
+    col = lambda j: T.col[:, j:j + 1]
+    PF, LANE, GRP, P7, P8, P1, WF, THN, L2, L34, G15, G16, PAR8 = range(13)
+    cp(col(PF), T.pi[:, 0:1], ["pi"], ["pf"], 1)
+    for j, (o, k) in enumerate(((ALU.bitwise_and, 15), (ALU.arith_shift_right, 4), (ALU.bitwise_and, 7), (ALU.arith_shift_right, 3), (ALU.bitwise_and, 1))):
+        ts(T.pj[:, j:j + 1], T.pi[:, 0:1], k, None, o, None, ["pi"], ["pj%d" % j], 1)
+    cp(T.col[:, 1:3], T.pj[:, 0:2], ["pj0", "pj1"], ["col"], 2)
+    cp(T.col[:, 3:6], T.pj[:, 2:5], ["pj2", "pj3", "pj4"], ["col2"], 3)
+    cp(col(WF), T.wi[:, 0:1], ["wi"], ["wf"], 1)
+    ts(T.wblk[:], T.jh[:], col(GRP), col(WF), ALU.is_equal, ALU.mult, ["jh", "col", "wf"], ["wblk"], 128, 0.5)
+    ts(T.ih[:], T.jj[:, 0:128], col(PF), None, ALU.is_equal, None, ["jj", "pf"], ["ih"], 128, 0.5)
+    ts(T.ineg[:], T.jj[:, 0:128], col(PF), -1.0, ALU.is_equal, ALU.mult, ["jj", "pf"], ["ineg"], 128, 0.5)
+    ts(T.ib[:], T.jj[:, 0:128], col(PF), None, ALU.is_equal, None, ["jj", "pf"], ["ib"], 128, 0.5)
+    ts(T.inf[:], T.jj[:, 0:128], col(PF), -1.0, ALU.is_equal, ALU.mult, ["jj", "pf"], ["inf"], 128)
+    ts(T.ibig[:], T.jj[:, 0:128], col(PF), float(1 << 15), ALU.is_equal, ALU.mult, ["jj", "pf"], ["ibig"], 128, 0.5)
+    ts(T.i16[:], T.jj[:, 0:128], col(PF), -16.0, ALU.is_equal, ALU.mult, ["jj", "pf"], ["i16"], 128, 0.5)
+    for c in range(NCH):
+        cp(T.a0[:, C0[c]:C0[c + 1]], T.ai[:, C0[c]:C0[c + 1]], ["ai_%d" % c], ["a0_%d" % c], WIDTHS[c])
     ts(col(G15), col(GRP), 16.0, 15.0, ALU.mult, ALU.add, ["col"], ["g15"], 1)
-    ts(T.wide[:], T.jj[:], col(G15), col(WF), ALU.is_equal, ALU.mult, ["jj", "g15", "wf"], ["wide"], 144)
-    ts(T.hb[:, 0:128], T.jm[:], col(GRP), -2048.0, ALU.is_equal, ALU.mult, ["jm", "col"], ["hb0"], 128)
-    ts(T.hb[:, 128:256], T.jm[:], col(GRP), -65536.0, ALU.is_equal, ALU.mult, ["jm", "col"], ["hb1"], 128)
+    ts(col(G16), col(GRP), -16.0, None, ALU.mult, None, ["col"], ["g16"], 1)
+    ts(T.wide[:], T.jj[:], col(G15), col(WF), ALU.is_equal, ALU.mult, ["jj", "g15", "wf"], ["wide"], 144, 0.5)
+    ts(T.hb[:, 0:128], JM[:], col(GRP), 2048.0, ALU.is_equal, ALU.mult, [jm, "col"], ["hb0"], 128, 0.5)
+    ts(T.hb[:, 128:256], JM[:], col(GRP), 65536.0, ALU.is_equal, ALU.mult, [jm, "col"], ["hb1"], 128, 0.5)
     cp(T.dx[:], T.hb[:, 0::16], ["hb0", "hb1"], ["dx"], 16)
     ts(T.dmx[:], T.hb[:, 0::16], -2.0, None, ALU.mult, None, ["hb0", "hb1"], ["dmx"], 16)
-    ts(T.dab[:], T.hb[:, 0::16], -1.0, None, ALU.mult, None, ["hb0", "hb1"], ["dab"], 16)
-    ts(T.bs[:], T.jj[:, 0:8], col(GRP), None, ALU.is_equal, None, ["jj", "col"], ["bs"], 8)
-    ts(col(THN), T.thi[:, 0:1], -1.0, None, ALU.mult, None, ["thi"], ["thn"], 1)
-    ts(col(L2), col(LANE), 2.0, 1.0, ALU.mult, ALU.add, ["col"], ["l2"], 1)
+    ts(T.bs[:, 0:16], T.jl[:, 0:16], col(P8), 1.0 / 4096.0, ALU.is_equal, ALU.mult, ["jl", "col2"], ["bs0"], 16)
+    ts(T.bs[:, 16:64], T.jl[:, 0:48], col(P8), None, ALU.is_equal, None, ["jl", "col2"], ["bs1"], 48)
+    ts(col(THN), T.thi[:, 0:1], -1.0, -8.0, ALU.mult, ALU.add, ["thi"], ["thn"], 1)
+    ts(col(L2), col(LANE), 2.0, 1.0, ALU.mult, ALU.add, ["col"], ["l2c"], 1)
     ts(col(L34), col(LANE), 34.0, None, ALU.mult, None, ["col"], ["l34"], 1)
+    ts(col(PAR8), col(P1), 8.0, None, ALU.mult, None, ["col2"], ["par8"], 1)
     ts(T.cep[:, 0:128], T.ih[:], col(THN), None, ALU.mult, None, ["ih", "thn"], ["cep0"], 128, 0.5)
-    ts(T.cep[:, 128:256], T.ih[:], col(L2), -60.25, ALU.mult, ALU.add, ["ih", "l2"], ["cep1"], 128, 0.5)
-    for b in range(NS):
-        ts(T.ck[:, b * 128:(b + 1) * 128], T.ih[:], col(L34), None, ALU.mult, None, ["ih", "l34"], ["ck%d" % b], 128, 0.5)
-    cks = ["ck%d" % j for j in range(NS)]
+    ts(T.cep[:, 128:256], T.ih[:], col(L2), -60.25, ALU.mult, ALU.add, ["ih", "l2c"], ["cep1"], 128, 0.5)
+    for b in range(2):
+        ts(T.ck[:, b * 128:(b + 1) * 128], T.ih[:], col(L34), -64.0, ALU.mult, ALU.add, ["ih", "l34"], ["ck%d" % b], 128, 0.5)
     ms(T.o2k[:], 2048.0, ["o2k"], 128, 0.5)
-    ms(T.one[:], 1.0, ["one"], 128, 0.5)
-    ms(T.mc[:, 2:3], -1024.0, ["mb"], 1)
-    ts(T.r0[:], T.jh[:], col(GRP), None, ALU.is_equal, None, ["jh", "col"], ["r0"], 128)
-    ts(T.r1[:], T.ib[:], -16.0, None, ALU.mult, None, ["ib"], ["r1"], 128)
-    tt(T.r0[:], T.r0[:], T.r1[:], ALU.add, ["r0", "r1"], ["r0"], 128)
-    ts(T.rsp[:], T.r0[:], 4096.0, None, ALU.mult, None, ["r0"], ["rsp"], 128)
-    ts(T.rsk[:], T.r0[:], 65536.0, None, ALU.mult, None, ["r0"], ["rsk"], 128)
-    ts(T.rst[:, 0:CW], T.jl[:, 0:CW], 0.0, 1.0e9, ALU.is_equal, ALU.mult, ["jl"], ["rst"], CW)
-    ts(T.dm[:, 0:CW], T.jl[:, 0:CW], col(LANE), None, ALU.is_equal, None, ["jl", "col"], ["dm"], CW)
-    cp(T.bl[:], T.bi[:], ["bi"], ["bl"], 16)
-    ts(T.cc[:], T.c16[:], col(LANE), None, ALU.add, None, ["c16", "col"], ["cc"], 32)
-    ts(T.cl[:], T.cc[:, 0:16], -512.0, 2.0, ALU.add, ALU.mult, ["cc"], ["cl"], 16)
-    ts(T.ch[:, 0:NC], T.cc[:, 0:NC], -496.0, None, ALU.add, None, ["cc"], ["ch"], NC)
-    for t in range(STEPS):
-        for c in range(NCH):
-            ms(T["h%d" % t][:, c * (CW + 16):c * (CW + 16) + 16], 0.0, ["hzero%d_%d" % (t, c)], 16)
-    ms(T.ut[:, 512:1024], 0.0, ["ut1"], 512, 0.5)
-    ms(T.st0[:, 512:1024], 0.0, ["st0_%d" % c for c in range(NCH)], 512, 0.5)
-    ts(T.vw[:], T.vv[:], 15, None, ALU.bitwise_and, None, ["vv"], ["vw"], 512)
-    tt(T.ut[:, 0:512], T.vw[:], T.okn[:], ALU.is_le, ["vw", "okn"], ["ut0"], 512)
-    ts(T.st0[:, 0:512], T.kk[:], col(LANE), None, ALU.is_lt, None, ["kk", "col"], ["stt0"], 512)
-
-    def pool_copy(out, in_, rd, wr, k):
-        op("g", lambda: g.affine_select(out, in_, [[0, k]], ALU.is_ge, 0.0, 0, 0), rd, wr, 170.0 + 2 * k * CY)
-
+    ms(T.mc[:, 2:3], 15360.0, ["mb"], 1)
+    ts(T.r0[:], T.jh[:], col(GRP), 4096.0, ALU.is_equal, ALU.mult, ["jh", "col"], ["r0"], 128, 0.5)
+    op("g", lambda: g.affine_select(T.rsp[:], T.r0[:], [[-1, 128]], ALU.not_equal, 4096.0 - 65536.0, 0, 1), ["r0"], ["rsp"], 170.0 + 256 * CY)
+    ts(T.rsk[:], T.rsp[:], 16.0, None, ALU.mult, None, ["rsp"], ["rsk"], 128, 0.5)
+    ts(T.rst[:], T.jl[:], 0.0, 1.0e9, ALU.is_equal, ALU.mult, ["jl"], ["rst"], 256, 0.5)
+    ts(T.dm[:], T.jd[:], col(P7), None, ALU.is_equal, None, ["jd", "col2"], ["dm"], 128, 0.5)
+    ts(T.bl[:, 0:8], T.jj[:, 0:8], col(PAR8), None, ALU.add, None, ["jj", "par8"], ["bl"], 8)
+    ts(T.l2[:], T.loc[:], col(G16), None, ALU.add, None, ["loc%d" % c for c in range(NCH)] + ["g16"], ["l2"], 32 * NCH)
+    for c in range(NCH):
+        either(ONV["k"], T.pr[:, 64 * c:64 * c + 16], T.loc[:, 32 * c:32 * c + 16], ["loc%d" % c, "g16"], ["cc_%d" % c], vc(16), vc(16), col(G16))
+    ms(T.cz[:], 0.0, ["cz"], 160, 0.5)
+    ms(T.cz[:, 0:16], 1.0 / 64.0, ["cz"], 16)
+    ms(T.cz[:, 64:80], 258.0 / 128.0, ["cz"], 16)
+    ms(T.cz[:, 112:128], 257.0 / 128.0, ["cz"], 16)
+    ms(T.cap[:, 0:16], 256.0, ["cap0"], 16)
+    ms(T.cap[:, 16:32], float(1 << 24), ["cap1"], 16)
+    if min(WIDTHS) < 256:
+        ms(T.km[:], 0.0, ["km_%d" % c for c in range(NCH)], 16 * NCH)
+    ms(T.hr[:], 0.0, ["hr%d_%d" % (c, b) for c in range(NCH) for b in range(2)], 768, 0.5)
+    ms(T.h0[:, 0:16], 0.0, ["hzero0"], 16)
+    for t in range(1, STEPS):
+        either(ONV["k"], T["h%d" % t][:, 0:16], T.h0[:, 0:16], ["hzero0"], ["hzero%d" % t], vc(16), vc(16))
+    ms(T.xg0[:, 32::3], 0.0, ["xr0"], 8 * W0, 0.5)
+    for c in range(1, NCH):
+        io(T["xg%d" % c][:, 32::3], [[0, 8 * WIDTHS[c]]], 0, 0, ["xr%d" % c], 8 * WIDTHS[c])
+    ms(T.ut[:, 256:LUT], 1.0, ["ut1"], 16)
+    ms(T.ut[:, LUT:LUT + 512], 0.0, ["ut2"], 512, 0.5)
+    ms(T.st0[:, 256:LUT + 512], 0.0, ["stz0"] + ["st0_%d" % c for c in range(NCH)], 528, 0.5)
+    ms(T.st1[:, 256:LUT], 0.0, ["stz1"], 16)
+    for e in range(2):
+        ts(T["st%d" % e][:, 0:256], T.jl[:], col(LANE), None, ALU.is_lt, None, ["jl", "col"], ["stt%d" % e], 256, 0.5)
+    mm(T.xb[:, 0:256], T.ib[:], T.tk[:], True, False, ["ib", "tk"], "xb", 256)
+    mm(T.xb[:, 0:256], T.i16[:], T.st0[:, 0:256], False, True, ["i16", "stt0"], "xb", 256)
+    ts(T.ut[:, 0:256], T.xb[:, 0:256], col(LANE), 0.0, ALU.add, ALU.is_ge, ["col"], ["ut0"], 256, 1.0, ["xb"])
     for e in range(2):
         pool_copy(T.tab[:, e:2048:2], T.tab[:, 4097 - e:6144:2], ["tab0"], ["sw%d" % e], 1024)
-    pool_copy(T.st1[:, 0:512], T.st0[:, 0:512], ["stt0"], ["stt1"], 512)
-    ts(T.wneg[:], T.jj[:], col(G15), -0.0625, ALU.is_equal, ALU.mult, ["jj", "g15"], ["wneg"], 144)
-    ms(T.c257[:], 257.0 / 128.0, ["c257"], 16)
-    for e in range(2):
-        either(T.tab[:, 2048 + e * 1024:3072 + e * 1024], T.tab[:, 6144 + e * 1024:7168 + e * 1024], ["tab1"], ["tab%d" % (2 + e)], vc(1024), vc(1024, 0.5))
-    for e in range(4):
-        cp(T.book[:, e * 512:(e + 1) * 512], T.spi[:, e * 512:(e + 1) * 512], ["spi"], ["sp%d" % e], 512)
-    sps = ["sp%d" % e for e in range(4)]
-    dma("y", T.book[:, 2048:4096], T.book[:, 0:2048], sps, ["gap"], 1 << 20)
+        ops[-1]["ord"] += [i for i, o in enumerate(ops[:-1]) if o["eng"] == "g"]
+    gap = ["gap"]
 
-    tabs = ["tab0", "tab1", "tab2", "tab3"]
-    k = 0
-    ny = [0]
+    ny = [1]
+    notes = []
     for t in range(STEPS):
         last = t == STEPS - 1
         H, A = T["h%d" % t], T["a%d" % t]
@@ -244,179 +280,205 @@ def build(g, core, T, topo, par=(CY, PCY, GA, SC)):
         dst = cores[(rank + 1 + t % (n - 1)) % n]
         src = cores[(rank - 1 - t % (n - 1)) % n]
         for c in range(NCH):
-            q = k % 2
             now[0] = c
-            k += 1
-            c0 = c * CW
+            c0, CW = C0[c], WIDTHS[c]
+            M, NC, PW = CW // 2, CW // 16, CW // NH
             cs = slice(c0, c0 + CW)
-            ws = slice(c * NC, (c + 1) * NC)
-            h, a = "h%d_%d" % (t, c), "a%d_%d" % (t, c)
-            sto = "st%d_%d" % (t % 2, c)
-            ha = "ha%d" % q
-            HA, X, MX = T[ha], T["xg%d" % q], T["mx%d" % q]
-            r = lambda name: "%s_%d" % (name, c)
-            h0 = c * (CW + 16) + 16
+            h0 = 16 + c0
             hs = slice(h0, h0 + CW)
-            mm(T.sb[:, 0:CW], T.wblk[:], H[:, hs], True, True, ["wblk", h], "sb", CW)
-            op("s", lambda o_=T.yr[:, cs]: s.activation(o_, T.sb[:, 0:CW], ACT.Identity, bias=524288.0), [], [r("yr")], vc(CW), ["sb"],
-               alt=(lambda o_=T.yr[:, cs]: v.tensor_scalar(o_, T.sb[:, 0:CW], 524288.0, None, ALU.add), vc(CW)))
-            if t == 0:
-                mm(HA[:, 0:CW], T.ih[:], A[:, cs], True, False, ["ih", a], ha, CW)
-            else:
-                mm(HA[:, 0:CW], T.ih[:], T["a%d" % (t - 1)][:, cs], True, False, ["ih", "a%d_%d" % (t - 1, c)], ha, CW)
-                mm(HA[:, 0:CW], T.ih[:], T.mm[:, cs], False, False, ["ih", r("mm")], ha, CW)
-            mm(HA[:, 0:CW], T.wblk[:], H[:, hs], False, False, ["wblk", h], ha, CW)
-            mm(HA[:, 0:CW], T.ineg[:], T.yr[:, cs], False, True, ["ineg", r("yr")], ha, CW)
-            mm(HA[:, 256:256 + CW], T.ib[:], H[:, hs], True, True, ["ib", h], ha, CW)
-            ts(T.off[:, cs], HA[:, 0:CW], 526336.0, None, ALU.add, None, [], [r("off")], CW, 1.0, [ha])
-            xs = [["x%d_%d" % (q, e) for e in range(b * 128 // GP, (b + 1) * 128 // GP)] for b in range(NS)]
-            for e in range(CW // GP):
-                either(X[:, e * GP * 16:(e + 1) * GP * 16], T.tab[:, 2048:8192].indirect(T.off[:, c0 + e * GP:c0 + (e + 1) * GP]),
-                       tabs + [r("off")], ["x%d_%d" % (q, e)], gat(GP * 16), gat(GP * 16))
-            eps = ["ep%d" % ((k * NS + b) % 2) for b in range(NS)]
-            for b in range(NS):
-                ep = eps[b]
-                EP = T[ep]
-                bs_ = slice(c0 + b * 128, c0 + (b + 1) * 128)
-                mm(EP[:, 0:256], T.o2k[:], T.cep[:, 0:256], True, False, ["o2k", "cep0", "cep1"], ep, 256)
-                mid(EP[:, 0:256], H[:, h0 + b * 128:h0 + (b + 1) * 128], T.hb[:], [h, "hb0", "hb1"], ep, 256)
-                if t > 0:
-                    mid(EP[:, 128:256], STo[:, 512 + c0 + b * 128:512 + c0 + (b + 1) * 128], T.rsp[:], [sto, "rsp"], ep, 128)
+            hh, a = ["h%d_%d_%d" % (t, c, f) for f in range(NH)], "a%d_%d" % (t, c)
+            sto = "st%d_%d" % (t % 2, c)
+            of, kb = "of%d" % ((t * NCH + c) % 2), "kb%d" % ((t * NCH + c) % 2)
+            OF, KB, X, MX = T[of], T[kb], T["xg%d" % c], T["mx%d" % c]
+            r = lambda name: "%s_%d" % (name, c)
+            par2 = lambda buf, at, b: buf[:, at + b:at + CW:2]
+            r0 = 3 * c0 // 2
+            HR = lambda b: T.hr[:, r0 + b:r0 + 3 * M:3]
+            hr = ["hr%d_%d" % (c, b) for b in range(2)]
+            for f in range(NH):
+                f0, f1 = f * PW, (f + 1) * PW
+                fs = slice(c0 + f0, c0 + f1)
+                for B, bank in ((KB, kb), (OF, of)):
+                    if t == 0:
+                        mm(B[:, f0:f1], T.ih[:], A[:, fs], True, False, ["ih", a], bank, PW)
+                    else:
+                        mm(B[:, f0:f1], T.ih[:], T["a%d" % (t - 1)][:, fs], True, False, ["ih", "a%d_%d" % (t - 1, c)], bank, PW)
+                        mm(B[:, f0:f1], T.ih[:], T.mm[:, fs], False, False, ["ih", r("mm")], bank, PW)
+                    mm(B[:, f0:f1], T.wblk[:], H[:, h0 + f0:h0 + f1], False, bank == kb, ["wblk", hh[f]], bank, PW)
+                either(ONV["yr"], T.yr[:, fs], KB[:, f0:f1], [], [r("yr%d" % f)], vc(PW), vc(PW), 524288.0, [kb])
+                mm(OF[:, f0:f1], T.ineg[:], T.yr[:, fs], False, True, ["ineg", r("yr%d" % f)], of, PW)
+                for b in range(2):
+                    ts(T.off[:, c0 + M * b + f0 // 2:c0 + M * b + f1 // 2], OF[:, f0 + b:f1:2], 526336.0, None, ALU.add, None, [], [r("off%d_%d" % (b, f))], PW // 2, 1.0, [of])
+            for b in range(2):
+                either(ONV["hr"], HR(b), par2(H, h0, b), hh, [hr[b]], vc(M), vc(M, 0.5), 32.0 if b else None)
+            SW, YW = OF[:, 256:256 + NC], T.yw[:, 16 * c:16 * c + NC]
+            z = 64 if t == 0 else 112
+            mm(OF[:, 256:304], T.o2k[:], T.cz[:, z:z + 48], True, False, ["o2k", "cz"], of, 48)
+            mm(OF[:, 272:304], T.ih[:], T.l2[:, 32 * c:32 * c + 32], False, False, ["ih", "l2"], of, 32)
+            if t > 0:
+                mm(OF[:, 272:288], T.inf[:], T.pr[:, 64 * c + 32:64 * c + 48], False, False, ["inf", r("pr")], of, 16, 4.0)
+            for m0 in range(0, 16, PG):
+                mms([(KB[:, 320:320 + NC], T.wide[:, 15 - m:143 - m], H[:, h0 + m:h0 + CW:16], m == 0, m == 15) for m in range(m0, m0 + PG)], ["wide"] + hh, [kb], [], NC)
+            either(ONV["yw"], YW, KB[:, 320:320 + NC], [], [r("yw")], vc(16), vc(16), 524288.0, [kb])
+            SM = T.sm[:, 16 * c:16 * c + NC]
+            tt(SM, YW, KB[:, 320:320 + NC], ALU.subtract, [r("yw")], [r("sm")], 16, 1.0, [kb])
+            mm(SW, T.inf[:], SM, False, True, ["inf", r("sm")], of, 16, 4.0)
+            xs = [[], []]
+            mxs = [[] for i in range(16)]
+            marks = cuts(0, M, NCUT)
+            for e in range(NCUT):
+                u0, u1 = marks[e], marks[e + 1]
+                cut = []
+                calls = cuts(u0, u1, GPC)
+                for w0, w1 in zip(calls, calls[1:]):
+                    for b in range(2):
+                        x = "x%d_%d_%d" % (c, b, w0)
+                        onv = len(xs[0]) + len(xs[1]) in VG.get((t, c), VG[None])
+                        xs[b].append(x)
+                        cut.append(x)
+                        k = (w1 - w0) * 16
+                        either(onv, X[:, 16 * b + 48 * w0:16 * b + 48 * w1:3], T.tab[:, 2048:6160].indirect(T.off[:, c0 + M * b + w0:c0 + M * b + w1]),
+                               ["tab0", "tab1"] + [r("off%d_%d" % (b, f)) for f in range(2 * w0 // PW, (2 * w1 - 1) // PW + 1)], [x], gat(k), gat(k), 32.0 if b else None)
                 for i in range(16 - NA):
-                    mid(EP[:, i:256:16], X[:, b * 2048 + i:(b + 1) * 2048:16], T.dx[:], xs[b] + ["dx"], ep, 16)
-                for i in range(16 - NA):
-                    mxr = "mx%d_%d_%d" % (q, i, b)
-                    o_ = MX[:, i * CW + b * 128:i * CW + (b + 1) * 128]
-                    tt(o_, X[:, b * 2048 + i:(b + 1) * 2048:16], HA[:, 256 + b * 128:256 + (b + 1) * 128], ALU.max, xs[b], [mxr], 128, 1.0, [ha])
-                    mid(EP[:, i:256:16], o_, T.dmx[:], [mxr, "dmx"], ep, 16)
-                for j0 in range(0, NA, YB):
-                    yb = "yb%d" % (ny[0] % 2)
+                    mxs[i].append("mx%d_%d_%d" % (c, i, e))
+                    k = 3 * (u1 - u0)
+                    scan(MX[:, 3 * M * i + 3 * u0:3 * M * i + 3 * u1], X[:, 3 * i + 48 * u0:3 * i + 48 * u0 + 16 * k - 15:16], T.hr[:, r0 + 3 * u0:r0 + 3 * u1],
+                         ALU.max, ALU.min, cut + ["xr%d" % c] + hr, [mxs[i][e]], k, 0.5)
+                for j0 in range(16 - NA, 16, YB):
+                    nj = min(16, j0 + YB) - j0
+                    yb = ("yb", "xb")[ny[0] % 2]
                     ny[0] += 1
-                    js = list(range(j0, min(NA, j0 + YB)))
-                    for j in js:
-                        o_ = T[yb][:, (j - j0) * 128:(j - j0 + 1) * 128]
-                        mm(o_, T.ineg[:], H[:, h0 + b * 128:h0 + (b + 1) * 128], True, False, ["ineg", h], yb, 128)
-                        mm(o_, T.ib[:], X[:, b * 2048 + 16 - NA + j:(b + 1) * 2048:16], False, True, ["ib"] + xs[b], yb, 128)
-                    m0 = (16 - NA) * CW + b * NA * 128
-                    mxr = "ab%d_%d_%d" % (q, b, j0)
-                    act(MX[:, m0 + j0 * 128:m0 + (j0 + len(js)) * 128], T[yb][:, 0:len(js) * 128], ACT.Abs, [], [mxr], vc(len(js) * 128), [yb])
-                    for j in js:
-                        mid(EP[:, 16 - NA + j:256:16], MX[:, m0 + j * 128:m0 + (j + 1) * 128], T.dab[:], [mxr, "dab"], ep, 16)
-                mm(EP[:, 128:256], A[:, bs_], T.ih[:], False, True, [a, "ih"], ep, 128)
-                act(T.gg[:, bs_], EP[:, 0:128], ACT.Sign, ["mb"], [r("gg%d" % b)], vc(128), [ep], bias=T.mc[:, 2:3])
-                op("v", lambda o_=T.scp[:, bs_], i_=EP[:, 128:256]: v.tensor_tensor_scan(o_, T.rst[:, 0:128], i_, 0.0, ALU.add, ALU.min),
-                   ["rst"], [r("scp%d" % b)], vc(128), [ep])
-            sw_ = T.kb[:, 288:288 + NC]
-            mm(sw_, T.o2k[:], T.c257[:, 0:NC], True, False, ["o2k", "c257"], "kb", NC)
-            for m in range(16):
-                mm(sw_, T.wide[:, 15 - m:143 - m], H[:, h0 + m:h0 + CW:16], False, False, ["wide", h], "kb", NC)
-            for m in range(16):
-                mm(sw_, T.wneg[:, 15 - m:143 - m], T.yr[:, c0 + m:c0 + CW:16], False, m == 15, ["wneg", r("yr")], "kb", NC)
-            mm(T.kb[:, 0:CW], T.o2k[:], T.ck[:, 0:CW], True, False, ["o2k"] + cks, "kb", CW)
-            for b in range(NS):
+                    k = (u1 - u0) * 2 * nj
+                    for b in range(2):
+                        calls = []
+                        for j in range(nj):
+                            o_ = T[yb][:, b * nj + j:k:2 * nj]
+                            x0 = 16 * b + 3 * (j0 + j)
+                            calls.append((o_, T.ineg[:], T.hr[:, r0 + b + 3 * u0:r0 + 3 * u1:3], True, False))
+                            calls.append((o_, T.ib[:], X[:, x0 + 48 * u0:x0 + 48 * u1 - 47:48], False, True))
+                        mms(calls, ["ineg", "ib", hr[b]] + [x for x in cut if x in xs[b]], [yb], [], u1 - u0)
+                    m0 = 3 * M * j0 + 2 * nj * u0
+                    mxr = "ab%d_%d_%d" % (c, j0, e)
+                    act(MX[:, m0:m0 + k], T[yb][:, 0:k], ACT.Abs, [], [mxr], vc(k), [yb])
+                    for j in range(nj):
+                        mxs[j0 + j].append(mxr)
+            k0 = 256 * c
+            for b in range(2):
+                ep = "ep%d" % b
+                EP = T[ep]
+                bs_ = slice(k0 + b * 128, k0 + (b + 1) * 128)
+                XP = lambda i: X[:, 16 * b + 3 * i:16 * b + 3 * i + 48 * M - 47:48]
+                mm(EP[0:M, 0:256], T.o2k[:, 0:M], T.cep[:, 0:256], True, False, ["o2k", "cep0", "cep1"], ep, 256)
+                mid(EP[0:M, 0:256], HR(b), T.hb[:], [hr[b], "hb0", "hb1"], ep, 256)
                 if t > 0:
-                    mm(T.kb[:, b * 128:(b + 1) * 128], STo[:, 512 + c0 + b * 128:512 + c0 + (b + 1) * 128], T.rsk[:], False, False, [sto, "rsk"], "kb", 128)
-                mm(T.kb[:, b * 128:(b + 1) * 128], A[:, c0 + b * 128:c0 + (b + 1) * 128], T.ih[:], False, False, [a, "ih"], "kb", 128)
-            mm(T.kb[:, 0:CW], T.ibig[:], T.gg[:, cs], False, True, ["ibig"] + [r("gg%d" % b) for b in range(NS)], "kb", CW)
-            op("v", lambda o_=T.sck[:, cs]: v.tensor_tensor_scan(o_, T.rst[:, 0:CW], T.kb[:, 0:CW], 0.0, ALU.add, ALU.min),
-               ["rst"], [r("sck")], vc(CW), ["kb"])
-            tt(T.km[:, ws], T.scp[:, c0 + 15:c0 + CW:16], T.sck[:, c0 + 15:c0 + CW:16], ALU.min, [r("sck")] + [r("scp%d" % b) for b in range(NS)], [r("km")], NC)
-            op("v", lambda o_=T.ll[:, cs], w_=T.km[:, ws]: v.tensor_tensor(o_, w_.indirect(T.bl[:, 0:NC]), T.dm[:, 0:CW], ALU.mult),
-               [r("km"), "bl", "dm"], [r("ll")], gat(CW))
-            for b in range(NS):
-                mm(T.kb[:, 256 + b * 8:256 + (b + 1) * 8], T.ll[:, c0 + b * 128:c0 + (b + 1) * 128], T.bs[:], True, True, [r("ll"), "bs"], "kb", 8, 4.0)
-            kw = T.kb[:, 256:256 + NC]
-            l0 = c * 4 * NC
-            cp(T.ki[:, ws], kw, [], [r("ki")], NC, 1.0, ["kb"])
-            ts(T.nm[:, ws], kw, -240.0 * 65536.0, None, ALU.is_ge, None, [], [r("nm")], NC, 1.0, ["kb"])
-            ts(T.lst[:, l0 + NC:l0 + 2 * NC], T.ki[:, ws], 4095, None, ALU.bitwise_and, None, [r("ki")], [r("bk")], NC)
-            ts(T.i9[:, ws], T.ki[:, ws], 11, 511, ALU.arith_shift_right, ALU.bitwise_and, [r("ki")], [r("i9")], NC)
-            tt(T.t1[:, ws], T.nm[:, ws], sw_, ALU.mult, [r("nm")], [r("t1")], NC, 1.0, ["kb"])
-            WV, wv = (T.cc, "cc") if t == 0 else (T.wv, r("wv"))
-            tt(T.zz[:, ws], T.nm[:, ws], WV[:, ws], ALU.mult, [r("nm"), wv], [r("zz")], NC)
-            tt(T.lst[:, l0:l0 + NC], T.t1[:, ws], T.lst[:, l0 + NC:l0 + 2 * NC], ALU.add, [r("t1"), r("bk")], [r("spx")], NC)
-            tt(T.lst[:, l0 + 2 * NC:l0 + 3 * NC], T.i9[:, ws], T.zz[:, ws], ALU.max, [r("i9"), r("zz")], [r("iu")], NC)
-            cp(T.lu[:, l0:l0 + 3 * NC], T.lst[:, l0:l0 + 3 * NC], [r("spx"), r("bk"), r("iu")], [r("lu")], 3 * NC)
-            tt(T.lst[:, l0 + 3 * NC:l0 + 4 * NC], T.nm[:, ws], T.ch[:, 0:NC], ALU.mult, [r("nm"), "ch"], [r("z0")], NC)
-            cp(T.lu[:, l0 + 3 * NC:l0 + 4 * NC], T.lst[:, l0 + 3 * NC:l0 + 4 * NC], [r("z0")], [r("lz")], NC)
-            if not last:
-                tt(T.wv[:, ws], T.cc[:, ws], T.zz[:, ws], ALU.subtract, ["cc", r("zz")], [r("wv")], NC)
-            lsp, lbk, liu = T.lu[:, l0:l0 + NC], T.lu[:, l0 + NC:l0 + 2 * NC], T.lu[:, l0 + 2 * NC:l0 + 3 * NC]
-            either(T.hz[:, cs], H[:, h0 - 16:h0 + CW].indirect(T.lu[:, l0 + 3 * NC:l0 + 4 * NC]),
-                   ["hzero%d_%d" % (t, c), r("lz"), h], [r("hz")], gat(CW), gat(CW))
-            op("v", lambda o_=T.yy[:, cs], l_=lsp, h_=T.hz[:, cs]: v.tensor_tensor(o_, T.tab[:, 0:8192].indirect(l_), h_, ALU.subtract),
-               tabs + ["sw0", "sw1", r("lu"), r("hz")], [r("yy")], gat(CW))
-            say = "say%d_%d" % (t, c)
-            act(T["say%d" % t][:, cs], T.yy[:, cs], ACT.Abs, [r("yy")], [say], vc(CW))
+                    mid(EP[0:M, 128:256], par2(STo, LUT + c0, b), T.rsp[:], [sto, "rsp"], ep, 128)
+                for i0 in range(0, 16 - NA, PG):
+                    mms([(EP[0:M, i:256:16], XP(i), T.dx[:], False, False) for i in range(i0, min(16 - NA, i0 + PG))], xs[b] + ["dx"], [], [ep], 16)
+                for i in range(16 - NA):
+                    mid(EP[0:M, i:256:16], MX[:, 3 * M * i + b:3 * M * (i + 1):3], T.dmx[:], mxs[i] + ["dmx"], ep, 16)
+                for j0 in range(16 - NA, 16, YB):
+                    nj = min(16, j0 + YB) - j0
+                    mms([(EP[0:M, j0 + j:256:16], MX[:, 3 * M * j0 + b * nj + j:3 * M * j0 + CW * nj:2 * nj], T.dx[:], False, False) for j in range(nj)],
+                        mxs[j0] + ["dx"], [], [ep], 16)
+                mm(EP[0:M, 128:256], par2(A, c0, b), T.ih[:], False, True, [a, "ih"], ep, 128)
+                op("s", lambda o_=T.gg[0:M, bs_], i_=EP[0:M, 0:128], b_=T.mc[0:M, 2:3]: s.activation(o_, i_, ACT.Relu, bias=b_), ["mb"], [r("gg%d" % b)], vc(128), [ep],
+                   alt=(lambda o_=T.gg[0:M, bs_], i_=EP[0:M, 0:128], b_=T.mc[0:M, 2:3]: v.tensor_scalar(o_, i_, b_, 0.0, ALU.add, ALU.max), vc(128)), onv=ONV["gg"])
+                scan(T.scp[0:M, bs_], T.rst[0:M, 0:128], EP[0:M, 128:256], ALU.add, ALU.min, ["rst"], [r("scp%d" % b)], 128, 1.0, [ep])
+            mm(KB[0:M, 0:256], T.o2k[:, 0:M], T.ck[:], True, False, ["o2k", "ck0", "ck1"], kb, 256)
+            for b in range(2):
+                if t > 0:
+                    mm(KB[0:M, b * 128:(b + 1) * 128], par2(STo, LUT + c0, b), T.rsk[:], False, False, [sto, "rsk"], kb, 128)
+                mm(KB[0:M, b * 128:(b + 1) * 128], par2(A, c0, b), T.ih[:], False, False, [a, "ih"], kb, 128)
+            mm(KB[0:M, 0:256], T.ibig[0:M, 0:M], T.gg[0:M, k0:k0 + 256], False, True, ["ibig", r("gg0"), r("gg1")], kb, 256)
+            scan(T.sck[0:M, k0:k0 + 256], T.rst[0:M, :], KB[0:M, 0:256], ALU.add, ALU.min, ["rst"], [r("sck")], 256, 1.0, [kb])
+            if last and notes:
+                ops[-1]["ord"].append(notes[-1])
+            KM, LL = T.km[:, 16 * c:16 * c + 16], T.ll[:, 128 * c:128 * c + 128]
+            tt(T.km[0:M, 16 * c:16 * c + 16], T.scp[0:M, k0 + 15:k0 + 256:16], T.sck[0:M, k0 + 15:k0 + 256:16], ALU.min, [r("sck"), r("scp0"), r("scp1")], [r("km")], 16)
+            mm(KB[:, 256:320], T.o2k[:], T.cz[:, 0:64], True, False, ["o2k", "cz"], kb, 64)
+            op("v", lambda o_=LL, w_=KM: v.tensor_tensor(o_, w_.indirect(T.bl[:, 0:8]), T.dm[:], ALU.mult), [r("km"), "bl", "dm"], [r("ll")], gat(128))
+            mm(KB[:, 256:320], LL, T.bs[:], False, True, [r("ll"), "bs0", "bs1"], kb, 64, 4.0)
+            Q = lambda i, j: T.qq[:, 112 * c + 16 * i:112 * c + 16 * j]
+            PR = lambda i, j: T.pr[:, 64 * c + 16 * i:64 * c + 16 * j]
+            LU = lambda i, j: T.lu[:, 96 * c + 16 * i:96 * c + 16 * j]
+            NM = T.nm[:, 48 * c:48 * c + 48]
+            ts(NM, KB[:, 272:320], -240.0 * 65536.0, None, ALU.is_ge, None, [], [r("nm")], 48, 1.0, [kb])
+            tt(Q(5, 7), KB[:, 256:288], T.cap[:], ALU.min, ["cap0", "cap1"], [r("ki")], 32, 1.0, [kb])
+            tt(PR(1, 4), NM, OF[:, 256:304], ALU.mult, [r("nm")], [r("pr")], 48, 1.0, [of])
+            cp(LU(5, 6), PR(3, 4), [r("pr")], [r("lz")], 16)
+            ts(Q(4, 5), Q(6, 7), 2047 if t == 0 else 4095, None, ALU.bitwise_and, None, [r("ki")], [r("bk")], 16)
+            ts(Q(3, 4), Q(6, 7), 3584, None, ALU.bitwise_and, None, [r("ki")], [r("gw0")], 16)
+            tt(Q(0, 3), PR(0, 3), Q(3, 6), ALU.add, [r("cc"), r("pr"), r("ki"), r("bk"), r("gw0")], [r("q3")], 48)
+            cp(LU(0, 5), Q(0, 5), [r("q3"), r("bk"), r("gw0")], [r("lu")], 80)
+            lst = lambda i: T.lu[:, 96 * c + 16 * i:96 * c + 16 * i + NC]
+            lgw, liu, lbk = lst(0), lst(2), lst(4)
             rid, pid, _ = topo.addr(dst)
             msk = 0
             for e in topo.engines(core, dst)[:NE]:
                 msk |= 1 << e
             got = len(topo.engines(src, core)[:NE])
-            arr = "arr%d_%d" % (t, c)
-            op("g", lambda o_=T["h%d" % (t + 1)][:, hs], i_=T["say%d" % t][:, cs], a_=arr, pid=pid, rid=rid, msk=msk:
-               g.remote_dma(o_, i_, T.sem[a_], T.sem["sent"], pid, rid, msk),
-               [say], ["h%d_%d" % (t + 1, c)], 300.0, lat=2500.0, sem=(arr, got, len(topo.engines(core, dst)[:NE])))
-            if t == 0:
-                ts(T.gw0[:, ws], T.ki[:, ws], 2047, None, ALU.bitwise_and, None, [r("ki")], [r("n0")], NC)
-                cp(T.gwu[:, ws], T.gw0[:, ws], [r("n0")], [r("n1")], NC)
-                op("v", lambda o_=T.tt[:, cs], l_=T.gwu[:, ws], a_=A[:, cs]: v.tensor_tensor(o_, T.spi[:, 0:2048].indirect(l_), a_, ALU.subtract),
-                   ["spi", r("n1"), a], [r("tt")], gat(CW))
-            else:
-                op("v", lambda o_=T.tt[:, cs], l_=lbk, a_=A[:, cs]: v.tensor_tensor(o_, T.book[:, 0:4096].indirect(l_), a_, ALU.subtract),
-                   sps + ["gap", r("lu"), a], [r("tt")], gat(CW))
-            op("v", lambda o_=T.mm[:, cs], l_=liu, t_=T.tt[:, cs]: v.tensor_tensor(o_, T.ut[:, 0:1024].indirect(l_), t_, ALU.mult),
-               ["ut0", "ut1", r("lu"), r("tt")], [r("mm")], gat(CW))
+            for f in range(NH):
+                fs = slice(c0 + f * PW, c0 + (f + 1) * PW)
+                part = lambda i: T.lu[:, 96 * c + 16 * i + f * PW // 16:96 * c + 16 * i + (f + 1) * PW // 16]
+                either(ONV["hz"], T.hz[:, fs], H[:, 0:h0 + CW].indirect(part(5)), ["hzero%d" % t, r("lz")] + ["h%d_%d_%d" % (t, e, x) for e in range(c + 1) for x in range(NH)],
+                       [r("hz%d" % f)], gat(PW), gat(PW))
+                op("v", lambda o_=T.yy[:, fs], l_=part(1), h_=T.hz[:, fs]: v.tensor_tensor(o_, T.tab[:, 0:8192].indirect(l_), h_, ALU.subtract),
+                   ["tab0", "tab1", "tab2", "sw0", "sw1", r("lu"), r("hz%d" % f)], [r("yy%d" % f)], gat(PW))
+                say = "say%d_%d_%d" % (t, c, f)
+                act(T["say%d" % t][:, fs], T.yy[:, fs], ACT.Abs, [r("yy%d" % f)], [say], vc(PW))
+                arr = "arr%d_%d_%d" % (t, c, f)
+                flight("g", lambda o_=T["h%d" % (t + 1)][:, h0 + f * PW:h0 + (f + 1) * PW], i_=T["say%d" % t][:, fs], a_=arr, pid=pid, rid=rid, msk=msk:
+                       g.remote_dma(o_, i_, T.sem[a_], T.sem["sent"], pid, rid, msk),
+                       [say], ["h%d_%d_%d" % (t + 1, c, f)], GI, RL + (FIRST if t + c + f == 0 else 0.0), RB, (arr, got, len(topo.engines(core, dst)[:NE])))
+            op("v", lambda o_=T.tt[:, cs], l_=lbk, a_=A[:, cs], w_=T.book[:, 0:2048 if t == 0 else 4096]: v.tensor_tensor(o_, w_.indirect(l_), a_, ALU.subtract),
+               [r("lu"), a, "spare"] + ([] if t == 0 else gap), [r("tt")], gat(CW))
+            op("v", lambda o_=T.mm[:, cs], l_=liu, t_=T.tt[:, cs]: v.tensor_tensor(o_, T.ut[:].indirect(l_), t_, ALU.mult),
+               ["ut0", "ut1", "ut2", r("lu"), r("tt")], [r("mm")], gat(CW))
             if last:
-                mm(HA[:, 0:CW], T.ih[:], A[:, cs], True, False, ["ih", a], ha, CW)
-                mm(HA[:, 0:CW], T.ih[:], T.mm[:, cs], False, True, ["ih", r("mm")], ha, CW)
-                act(T.af[:, cs], HA[:, 0:CW], ACT.Copy, [], [r("af")], vc(CW), [ha])
+                mm(OF[:, 0:CW], T.ih[:], A[:, cs], True, False, ["ih", a], of, CW)
+                mm(OF[:, 0:CW], T.ih[:], T.mm[:, cs], False, True, ["ih", r("mm")], of, CW)
+                either(ONV["af"], T.af[:, cs], OF[:, 0:CW], [], [r("af")], vc(CW), vc(CW), None, [of])
                 dma("y", T.ys[:, cs], T.af[:, cs], [r("af")], [r("ys")], CW * 512)
-                dma("y", T.yh[:, cs], T["h%d" % STEPS][:, hs], ["h%d_%d" % (STEPS, c)], [r("yh")], CW * 256)
+                dma("y", T.yh[:, cs], T["h%d" % STEPS][:, hs], ["h%d_%d_%d" % (STEPS, c, f) for f in range(NH)], [r("yh")], CW * 256)
+                G2 = T["g2%d" % c]
+                g2 = ["g2%d_%d" % (c, e) for e in range(4)]
+                op("v", lambda w_=G2[:], l_=lgw, a_=A[:, cs]: v.tensor_copy(w_.indirect(l_), a_), [r("lu"), a], g2, 60.0 + CW * SC * CY)
+                notes.append(len(ops) - 1)
+                for e in range(4):
+                    dma("y" if e % 2 == 0 or c < NCH - 1 else "s", T.yg[:, e * 512 + c0:e * 512 + c0 + CW], G2[:, 16 + e * 512 + c0:16 + e * 512 + c0 + CW],
+                        [g2[e]], ["yg%d_%d" % (c, e)], CW * 512)
             else:
                 an = "a%d_%d" % (t + 1, c)
                 dma("y", T["a%d" % (t + 1)][:, cs], A[:, cs], [a], [an], CW * 256)
                 sem = "d%d" % nd[0]
                 nd[0] += 1
-                op("g", lambda o_=T["a%d" % (t + 1)][:, cs], i_=T.mm[:, cs]: g.dma_start(o_, i_, accum_op=ALU.add),
-                   [an, r("mm")], [an], 800.0, lat=2500.0, sem=(sem, 16))
-                either(STn[:, 512 + c0:512 + c0 + CW], STo[:, 0:1024].indirect(liu),
-                       ["stt%d" % (t % 2), r("lu")] + ["st%d_%d" % (t % 2, e) for e in range(NCH)], ["st%d_%d" % ((t + 1) % 2, c)], gat(CW), gat(CW))
-            if last and (c + 1) * CW == 256:
-                kis = ["ki_%d" % e for e in range(c + 1)]
-                ts(T.gw0[:, 0:16], T.ki[:, 0:16], 3584, None, ALU.bitwise_and, None, kis, ["gw0a"], 16)
-                tt(T.gw1[:, 0:16], T.gw0[:, 0:16], T.cl[:], ALU.add, ["gw0a", "cl"], ["gw1a"], 16)
-                ts(T.gwu[:, 0:16], T.gw1[:, 0:16], 0.5, None, ALU.mult, None, ["gw1a"], ["gwua"], 16)
-                op("v", lambda a_=A[:, 0:256]: v.tensor_copy(T.g2[:, 0:2048].indirect(T.gwu[:, 0:16]), a_),
-                   ["gwua"] + ["a%d_%d" % (t, e) for e in range(c + 1)], ["g2_%d" % e for e in range(4)], 60.0 + 256 * SC * CY)
-                for e in range(4):
-                    dma("y", T.yg[:, e * 512:e * 512 + 256], T.g2[:, e * 256:(e + 1) * 256], ["g2_%d" % e], ["yga%d" % e], 1 << 17)
-        w0 = 16 if last else 0
-        kis = ["ki_%d" % e for e in range(NCH)]
-        ts(T.gw0[:, w0:32], T.ki[:, w0:32], 3584, None, ALU.bitwise_and, None, kis, ["gw0"] + ([] if last else ["gw0a"]) + ["n0_%d" % e for e in range(NCH)], 32)
-        tt(T.gw1[:, w0:32], T.gw0[:, w0:32], T.cc[:, w0:32], ALU.add, ["gw0", "cc"], ["gw1"] + ([] if last else ["gw1a"]), 32)
-        cp(T.gwu[:, w0:32], T.gw1[:, w0:32], ["gw1"], ["gwu"] + ([] if last else ["gwua"]) + ["n1_%d" % e for e in range(NCH)], 32)
-        op("v", lambda a_=A[:, 16 * w0:512], w0=w0: v.tensor_copy(T.book[:, 1536:6144].indirect(T.gwu[:, w0:32]), a_),
-           ["gwu"] + ([] if last else ["gwua"]) + ["a%d_%d" % (t, e) for e in range(NCH)], ["gap", "sp3"], 60.0 + (512 - 16 * w0) * SC * CY)
-        if last:
-            for e in range(4):
-                dma("y" if e % 2 == 0 else "s", T.yg[:, e * 512 + 256:(e + 1) * 512], T.book[:, 2048 + e * 512 + 256:2048 + (e + 1) * 512], ["gap"], ["ygb%d" % e], 1 << 18)
-        else:
+                flight("g", lambda o_=T["a%d" % (t + 1)][:, cs], i_=T.mm[:, cs]: g.dma_start(o_, i_, accum_op=ALU.add),
+                       [an, r("mm")], [an], 1300.0 + (1500.0 if t + c == 0 else 0.0), 2200.0, 240.0 + CW * 512 / RATE, (sem, 16))
+                either(ONV["st"], STn[:, LUT + c0:LUT + c0 + CW], STo[:].indirect(liu),
+                       ["stt%d" % (t % 2), "stz%d" % (t % 2), r("lu")] + ["st%d_%d" % (t % 2, e) for e in range(NCH)], ["st%d_%d" % ((t + 1) % 2, c)], gat(CW), gat(CW))
+        if not last:
+            for c in range(NCH):
+                op("v", lambda l_=T.lu[:, 96 * c:96 * c + WIDTHS[c] // 16], a_=A[:, C0[c]:C0[c + 1]]: v.tensor_copy(T.book[:, 2032:6144].indirect(l_), a_),
+                   ["lu_%d" % c, "a%d_%d" % (t, c)], gap + ["spare"], 60.0 + WIDTHS[c] * SC * CY)
+                notes.append(len(ops) - 1)
             if t == STEPS - 2:
-                for e in range(4):
-                    dma("y", T.g2[:, e * 256:(e + 1) * 256], T.book[:, 2048 + e * 512:2048 + e * 512 + 256], ["gap"], ["g2_%d" % e], 1 << 18)
-            mm(T.kb[:, 320:352], T.one[:], T.nm[:], True, True, ["one"] + ["nm_%d" % e for e in range(NCH)], "kb", 32)
-            op("v", lambda: v.tensor_reduce(T.mc[:, 0:1], T.kb[:, 320:352], AxisListType.X, ALU.add, negate=True), [], ["mc"], vc(32), ["kb"])
-            cp(T.mi[:, 0:1], T.mc[:, 0:1], ["mc"], ["mi0"], 1)
-            ts(T.mi[:, 1:2], T.mi[:, 0:1], 15, None, ALU.bitwise_and, None, ["mi0"], ["mi1"], 1)
-            ts(T.mc[:, 2:3], T.mi[:, 1:2], -2048.0, -1024.0, ALU.mult, ALU.add, ["mi1"], ["mb"], 1)
+                for c in range(NCH):
+                    for e in range(4):
+                        at = e * 512 + C0[c]
+                        pool_copy(T["g2%d" % c][:, 16 + at:16 + at + WIDTHS[c]], T.book[:, 2048 + at:2048 + at + WIDTHS[c]], gap, ["g2%d_%d" % (c, e)], WIDTHS[c])
+            for c in range(NCH):
+                mm(KB[:, 336:352], T.o2k[:], T.nm[:, 48 * c:48 * c + 16], c == 0, c == NCH - 1, ["o2k", "nm_%d" % c], kb, 16)
+            op("s", lambda i_=KB[:, 336:352]: s.activation(T.mj[:], i_, ACT.Identity, bias=-0.46875, scale=-1.0 / 2048.0, accum_out=T.mc[:, 0:1]),
+               [], ["mc"], vc(16) + 20.0, [kb])
+            ts(T.mc[:, 1:2], T.mc[:, 0:1], 201326592.0, -201326592.0, ALU.add, ALU.add, ["mc"], ["mr"], 1)
+            ts(T.mc[:, 2:3], T.mc[:, 0:1], T.mc[:, 1:2], -2048.0, ALU.subtract, ALU.mult, ["mc", "mr"], ["mb"], 1)
     return ops
 
 
 def depend(ops):
     lw, rds = {}, {}
     for i, o in enumerate(ops):
-        d = set()
+        d = set(lw[x] for x in o.get("gate", []))
         for x in o["rd"]:
             if x in lw:
                 d.add(lw[x])
@@ -424,7 +486,7 @@ def depend(ops):
             if x in lw:
                 d.add(lw[x])
             for j in rds.get(x, []):
-                if ops[j]["eng"] != o["eng"]:
+                if ops[j]["eng"] != o["eng"] or o["alt"] is not None or ops[j]["alt"] is not None:
                     d.add(j)
         for x in o["wr"]:
             if x in lw:
@@ -439,113 +501,260 @@ def depend(ops):
             rds[x] = []
 
 
-def gap_after(ops, j, i):
-    if ops[j]["eng"] == "p" and ops[i]["eng"] == "p":
-        return 0.0
-    return ops[j]["lat"] + HOP
-
-
 def place(ops, seq, before, tail, eng):
-    slots = {e: ([], []) for e in "vspgy"}
+    slots = {e: ([], []) for e in "vspgyd"}
     m = len(ops)
-    t0, t1, got = [0.0] * m, [0.0] * m, [None] * m
+    t0, t1 = [0.0] * m, [0.0] * m
     end = 0.0
+    near, far = ops[0]["hop"]
     for i in seq:
         o = ops[i]
         rdy = tail[0][i]
-        for j, lag in before[i]:
-            if t1[j] + lag > rdy:
-                rdy = t1[j] + lag
-        ways = [(o["eng"], o["cost"])]
-        if o["alt"] is not None:
-            if eng is None:
-                ways.append(("v", o["alt"][1]))
-            elif eng[i] == "v":
-                ways = [("v", o["alt"][1])]
-        best = None
-        for e, cost in ways:
-            st, en = slots[e]
-            x, hi = 0, len(en)
-            while x < hi:
-                md = (x + hi) >> 1
-                if en[md] <= rdy:
-                    x = md + 1
-                else:
-                    hi = md
-            t = rdy
-            while x < len(st) and st[x] < t + cost - 1e-6:
-                t = max(t, en[x])
-                x += 1
-            fin = t + cost + (BIAS if e != o["eng"] else 0.0)
-            if best is None or fin < best[0]:
-                best = (fin, e, t, cost, x)
-        _, e, t, cost, x = best
-        slots[e][0].insert(x, t)
-        slots[e][1].insert(x, t + cost)
-        t0[i], t1[i], got[i] = t, t + cost, e
+        e = eng[i]
+        for j, lag, wait in before[i]:
+            u = t1[j] + lag
+            if wait:
+                u += near if eng[j] == e else far
+            if u > rdy:
+                rdy = u
+        cost = o["cost"] if e == o["eng"] else o["alt"][1]
+        st, en = slots[e]
+        x, hi = 0, len(en)
+        while x < hi:
+            md = (x + hi) >> 1
+            if en[md] <= rdy:
+                x = md + 1
+            else:
+                hi = md
+        t = rdy
+        while x < len(st) and st[x] < t + cost - 1e-6:
+            t = max(t, en[x])
+            x += 1
+        st.insert(x, t)
+        en.insert(x, t + cost)
+        t0[i], t1[i] = t, t + cost
         end = max(end, t + cost + tail[1][i])
-    return t0, t1, got, end
+    return t0, t1, end
 
 
-def rerun(ops, oth, seq, eng, pre, more):
-    fin = [0.0] * len(ops)
-    free = {e: 0.0 for e in "vspgy"}
+def links(ops):
+    return [[(j, ops[j]["lat"], o["eng"] != "d" and not ops[j]["eng"] == o["eng"] == "p") for j in o["dep"]] + [(j, 0.0, False) for j in o["ord"]] for o in ops]
+
+
+def rerun(oth, pre, seq, eng):
+    fin = [0.0] * len(oth)
+    free = {e: 0.0 for e in "vspgyd"}
     end = 0.0
+    near, far = oth[0]["hop"]
     for i in seq:
         e = eng[i]
         t = free[e]
-        for j, lag in pre[i]:
-            u = fin[j] + (lag + more if lag > 0.0 else 0.0)
+        for j, lag, wait in pre[i]:
+            u = fin[j] + lag
+            if wait:
+                u += near if eng[j] == e else far
             if u > t:
                 t = u
-        t += oth[i]["cost"] if e == ops[i]["eng"] else oth[i]["alt"][1]
+        o = oth[i]
+        t += o["cost"] if e == o["eng"] else o["alt"][1]
         fin[i] = free[e] = t
-        if t + ops[i]["lat"] > end:
-            end = t + ops[i]["lat"]
+        if t + o["lat"] > end:
+            end = t + o["lat"]
     return end
 
 
 def schedule(ops, others):
     m = len(ops)
-    pre = [[(j, gap_after(ops, j, i)) for j in o["dep"]] + [(j, 0.0) for j in o["ord"]] for i, o in enumerate(ops)]
+    pre = links(ops)
     suc = [[] for _ in range(m)]
     for i in range(m):
-        for j, lag in pre[i]:
-            suc[j].append((i, lag))
+        for j, lag, wait in pre[i]:
+            suc[j].append((i, lag, wait))
     rank = [0.0] * m
     for i in range(m - 1, -1, -1):
-        rank[i] = ops[i]["cost"] + max([lag + rank[x] for x, lag in suc[i]] + [ops[i]["lat"]])
+        rank[i] = ops[i]["cost"] + max([lag + 120.0 * wait + rank[x] for x, lag, wait in suc[i]] + [ops[i]["lat"]])
     key = [LAM * ops[i]["c"] - rank[i] for i in range(m)]
     for i in range(m):
-        for j, lag in pre[i]:
+        for j, lag, wait in pre[i]:
             key[i] = max(key[i], key[j] + 1e-3)
     zero, lat = [0.0] * m, [o["lat"] for o in ops]
     free = [i for i in range(m) if ops[i]["alt"] is not None]
     rng = np.random.default_rng(SEED)
     best, keep = None, None
-    eng = None
+    eng = ["v" if o["onv"] else o["eng"] for o in ops]
     for x in range(ROUNDS):
-        t0, t1, eng, end = place(ops, sorted(range(m), key=lambda i: (key[i], i)), pre, (zero, lat), eng)
+        t0, t1, end = place(ops, sorted(range(m), key=lambda i: (key[i], i)), pre, (zero, lat), eng)
         seq = sorted(range(m), key=lambda i: (t0[i], i))
-        for oth, par in others:
-            end += par[5] * (rerun(ops, oth, seq, eng, pre, par[4] - HOP))
-        end /= 1 + len(others)
+        weight = 1.0
+        for oth, opre, wt in others:
+            end += wt * rerun(oth, opre, seq, eng)
+            weight += wt
+        end /= weight
         if best is None or end < best[1]:
             best = ([(i, eng[i], t0[i]) for i in seq], end)
         if keep is None or end < keep[2] + SLACK * (1.0 - x / ROUNDS):
             keep = (t1, eng, end)
         t1, eng = keep[0], list(keep[1])
-        for i in rng.choice(free, int(rng.integers(0, 3))):
-            eng[int(i)] = "v" if rng.random() < PV else "s"
-        lo = float(rng.random()) * end
+        for i in rng.choice(free, int(rng.integers(0, FLIP + 1))):
+            eng[int(i)] = "v" if (rng.random() < PV) != bool(ops[int(i)]["onv"]) else "s"
+        lo = float(rng.random()) * t1[seq[-1]]
         amp = float(rng.choice([0.0, 200.0, 600.0, 1500.0]))
-        back = [-t1[i] + (amp * float(u) if lo < t1[i] < lo + 15000.0 else 0.0) for i, u in enumerate(rng.random(m))]
+        back = [-t1[i] + (amp * float(u) if lo < t1[i] < lo + 12000.0 else 0.0) for i, u in enumerate(rng.random(m))]
         for i in range(m - 1, -1, -1):
-            for j, lag in suc[i]:
+            for j, lag, wait in suc[i]:
                 back[i] = max(back[i], back[j] + 1e-3)
-        b0, b1, _, _ = place(ops, sorted(range(m), key=lambda i: (back[i], -i)), suc, (lat, zero), eng)
+        b0, b1, _ = place(ops, sorted(range(m), key=lambda i: (back[i], -i)), suc, (lat, zero), eng)
         key = [-b1[i] for i in range(m)]
     return best
+
+
+def times(ops, pre, seq, eng, fin, why, start):
+    near, far = ops[0]["hop"]
+    prev = {e: -1 for e in "vspgy"}
+    left = 5
+    for x in range(start - 1, -1, -1):
+        e = eng[seq[x]]
+        if e != "d" and prev[e] < 0:
+            prev[e] = seq[x]
+            left -= 1
+            if left == 0:
+                break
+    busy = sorted((fin[i] - ops[i]["cost"], fin[i], i) for i in seq[:start] if eng[i] == "d")
+    for x in range(start, len(seq)):
+        i = seq[x]
+        e = eng[i]
+        if e == "d":
+            t, w = max((fin[j] + lag, j) for j, lag, wait in pre[i])
+            cost = ops[i]["cost"]
+            k = 0
+            while k < len(busy) and busy[k][0] < t + cost:
+                if busy[k][1] > t:
+                    t, w = busy[k][1], busy[k][2]
+                k += 1
+            busy.insert(k, (t, t + cost, i))
+            fin[i], why[i] = t + cost, w
+            continue
+        w = prev[e]
+        t = fin[w] if w >= 0 else 0.0
+        w = -2 - w
+        for j, lag, wait in pre[i]:
+            u = fin[j] + lag
+            if wait:
+                u += near if eng[j] == e else far
+            if u > t:
+                t, w = u, j
+        o = ops[i]
+        fin[i] = t + (o["cost"] if e == o["eng"] else o["alt"][1])
+        why[i] = w
+        prev[e] = i
+
+
+def polish(worlds, seq, eng):
+    ops, pre = worlds[0][0], worlds[0][1]
+    m = len(ops)
+    up = [set(j for j, _, _ in pre[i]) for i in range(m)]
+    ends = [i for i in range(m) if ops[i]["eng"] == "d"]
+    rng = np.random.default_rng(SEED)
+    draw = rng.random((MOVES, 5))
+    total = sum(w[2] for w in worlds)
+
+    def value(fins):
+        return sum(w[2] * max(f[i] + w[0][i]["lat"] for i in ends) for w, f in zip(worlds, fins)) / total
+
+    fins, whys = [[0.0] * m for w in worlds], [[-1] * m for w in worlds]
+    for w, f, y in zip(worlds, fins, whys):
+        times(w[0], w[1], seq, eng, f, y, 0)
+    now = value(fins)
+    best = (now, list(seq), list(eng))
+    held = None
+    for x in range(MOVES):
+        d = draw[x]
+        if held is None:
+            pos = {i: k for k, i in enumerate(seq)}
+            held = []
+            for w, f, y in zip(worlds, fins, whys):
+                i = max(ends, key=lambda i: f[i] + w[0][i]["lat"])
+                while i >= 0:
+                    j = y[i]
+                    if j <= -2:
+                        j = -2 - j
+                        held.append((j, i))
+                    i = j
+        j, i = held[int(d[0] * len(held))]
+        new, neng = seq, eng
+        if d[1] < 0.25:
+            k = i if d[2] < 0.5 else j
+            if ops[k]["alt"] is None:
+                continue
+            neng = list(eng)
+            neng[k] = "v" if eng[k] == "s" else "s"
+            lo = pos[k]
+        else:
+            lo, hi = pos[j], pos[i]
+            if d[1] < 0.65:
+                more = int(d[2] * d[2] * 6)
+                k = lo - 1
+                while more > 0 and k >= 0:
+                    if eng[seq[k]] == eng[i]:
+                        lo, more = k, more - 1
+                    k -= 1
+                need, go, stay = set(up[i]), [i], []
+                for k in range(hi - 1, lo - 1, -1):
+                    if seq[k] in need:
+                        need |= up[seq[k]]
+                        go.append(seq[k])
+                    else:
+                        stay.append(seq[k])
+                new = seq[:lo] + go[::-1] + stay[::-1] + seq[hi + 1:]
+            else:
+                more = int(d[2] * d[2] * 6)
+                k = hi + 1
+                while more > 0 and k < m:
+                    if eng[seq[k]] == eng[i]:
+                        hi, more = k, more - 1
+                    k += 1
+                late, go, stay = {j}, [j], []
+                for k in range(lo + 1, hi + 1):
+                    if up[seq[k]] & late:
+                        late.add(seq[k])
+                        go.append(seq[k])
+                    else:
+                        stay.append(seq[k])
+                new = seq[:lo] + stay + go + seq[hi + 1:]
+            if new == seq:
+                continue
+        room = -HEAT * (1.0 - x / MOVES) * np.log(d[3] + 1e-9) * total
+        nf, ny, more = [], [], 0.0
+        for w, f, y in zip(worlds, fins, whys):
+            nf.append(list(f))
+            ny.append(list(y))
+            times(w[0], w[1], new, neng, nf[-1], ny[-1], lo)
+            more += w[2] * (max(nf[-1][i] for i in ends) - max(f[i] for i in ends))
+            if more > room + 400.0:
+                break
+        if more <= room:
+            val = value(nf)
+            seq, eng, fins, whys, now, held = new, neng, nf, ny, val, None
+            if now < best[0]:
+                best = (now, list(seq), list(eng))
+    now, seq, eng = best
+    times(ops, pre, seq, eng, fins[0], whys[0], 0)
+    return [(i, eng[i], fins[0][i] - (ops[i]["cost"] if eng[i] == ops[i]["eng"] else ops[i]["alt"][1])) for i in seq], now
+
+
+def plan(g, core, T, topo):
+    ops = build(g, core, T, topo)
+    depend(ops)
+    others = []
+    for par, wt in OTHER:
+        oth = build(g, core, T, topo, par)
+        depend(oth)
+        others.append((oth, links(oth), wt))
+    first = schedule(ops, others)[0]
+    eng = [None] * len(ops)
+    for i, e, _ in first:
+        eng[i] = e
+    return polish([(ops, links(ops), 1.0)] + others, [x[0] for x in first], eng)
 
 
 ORDER = {}
@@ -554,11 +763,11 @@ ORDER = {}
 def rank_program(g, core, T, topo):
     if T.rank_of(core) is None:
         return
+    if "o" not in ORDER:
+        ORDER["o"] = plan(g, core, T, topo)[0]
     ops = build(g, core, T, topo)
     depend(ops)
-    if "o" not in ORDER:
-        ORDER["o"] = schedule(ops, [(build(g, core, T, topo, par), par) for par in OTHER])[0]
-    order = [x[0] for x in ORDER["o"]]
+    order = [x[0] for x in ORDER["o"] if x[1] != "d"]
     for i, e, _ in ORDER["o"]:
         if ops[i]["eng"] != e:
             ops[i]["eng"], ops[i]["fn"] = e, ops[i]["alt"][0]

@@ -1,3 +1,4 @@
+import math
 import numpy as np
 import comms_topo
 from concourse.mybir import dt, AluOpType, AxisListType, ActivationFunctionType
@@ -6,82 +7,86 @@ ALU = AluOpType
 ACT = ActivationFunctionType
 C, V, VX, STEPS = 512, 2048, 4096, 4
 WIDTHS = (256, 256)
-NA = 6
-YB = 3
-NCUT = 2
-GPC = 1
-NH = 1
+MARKS = (0.0, 0.5, 1.0)
+NA = 4
+YB = 4
+YPE = False
+GPC = 2
 PG = 4
 NE = 8
-LUT = 272
-LAM = 4000.0
-ROUNDS = 1500
-PV = 0.5
+KW = 8 * 17
+LUT = 296
+LAM = 1000.0
+ROUNDS = 3600
+PV = 0.7
 FLIP = 2
 SEED = 5
-SLACK = 200.0
-MOVES = 40000
-HEAT = 80.0
+SLACK = 120.0
+MOVES = 12000
+HEAT = 30.0
+TRIES = 0
+PLAN = {"off0": 500, "off1": 850, "hr0": 200, "hr1": 330, "x0": 810, "x1": 1200, "x2": 1540, "x3": 2270, "x4": 3200, "x5": 3000, "x6": 3950, "x7": 4700,
+        "mx0": 3930, "mx1": 5620, "ybp0": 3200, "ybp1": 3400, "xbp0": 5600, "xbp1": 5800, "ab0": 5420, "ab1": 6050, "rst0": 7000,
+        "epp0": 1000, "epp1": 5500, "epp2": 5700, "epp3": 6000, "epp4": 6600, "epp5": 1200, "epp6": 5550, "epp7": 5750, "epp8": 6050, "epp9": 6700,
+        "so0": 7300, "so1": 7650, "km0": 7600, "km1": 7900, "la0": 8100, "lt0": 8400, "lu0": 9430, "hz0": 9700, "yy0": 10300, "say0": 11200,
+        "h0": 11500, "hd0": 12500, "tt0": 12450, "mk0": 14000, "sg0": 14400, "a0": 14700, "mj0": 8200, "cep0": 9600, "gap0": 14150, "gap1": 21650, "g0": 23000}
+FAST = True
+TURN = False
+AMPS = (100.0, 400.0, 1000.0, 2500.0)
+WIDE = 6000.0
+FIXED = ()
+WARM = 60.0
+STEP = (300.0, 1500.0)
+CLASS = ("ab", "cc", "cc", "cd")
+PERIOD = 15000.0
+LATE = {"tt": 2000.0, "mk": 2000.0, "a": 2000.0, "sg": 2000.0, "gap": 6000.0}
+REACH = 150
+RESORT = 8
+SPAN = 40
 
 
 def buffers():
-    nch = len(WIDTHS)
-    b = {
-        "tab": ("sbuf", [128, 8192], "bfloat16"),
-        "book": ("sbuf", [128, 6144], "int32"),
-        "ai": ("sbuf", [128, 512], "int32"),
-        "thi": ("sbuf", [128, 8], "int32"), "wi": ("sbuf", [128, 8], "int32"),
-        "af": ("sbuf", [128, 512], "float32"),
-        "tt": ("sbuf", [128, 512], "float16"), "mm": ("sbuf", [128, 512], "float16"),
-        "yr": ("sbuf", [128, 512], "bfloat16"), "off": ("sbuf", [128, 512], "uint16"),
-        "yw": ("sbuf", [128, 16 * nch], "bfloat16"), "sm": ("sbuf", [128, 16 * nch], "float32"),
-        "hz": ("sbuf", [128, 512], "bfloat16"), "yy": ("sbuf", [128, 512], "bfloat16"),
-        "gg": ("sbuf", [128, 256 * nch], "bfloat16"), "hr": ("sbuf", [128, 768], "bfloat16"),
-        "scp": ("sbuf", [128, 256 * nch], "float32"), "sck": ("sbuf", [128, 256 * nch], "float32"), "ll": ("sbuf", [128, 128 * nch], "float32"),
-        "km": ("sbuf", [128, 16 * nch], "float32"), "nm": ("sbuf", [128, 48 * nch], "float16"),
-        "qq": ("sbuf", [128, 112 * nch], "int32"), "pr": ("sbuf", [128, 64 * nch], "float32"), "lu": ("sbuf", [128, 96 * nch], "uint16"),
-        "mc": ("sbuf", [128, 8], "float32"), "mj": ("sbuf", [128, 16], "float32"),
-        "pi": ("sbuf", [128, 8], "int32"), "pj": ("sbuf", [128, 8], "int32"), "col": ("sbuf", [128, 16], "float32"),
-        "jj": ("sbuf", [128, 144], "bfloat16"), "jl": ("sbuf", [128, 256], "bfloat16"), "jh": ("sbuf", [128, 128], "bfloat16"),
-        "jm": ("sbuf", [128, 128], "bfloat16"), "jd": ("sbuf", [128, 128], "bfloat16"), "tk": ("sbuf", [128, 256], "bfloat16"),
-        "loc": ("sbuf", [128, 32 * nch], "float32"), "l2": ("sbuf", [128, 32 * nch], "float16"), "bl": ("sbuf", [128, 16], "uint16"),
-        "ih": ("sbuf", [128, 128], "float16"), "ib": ("sbuf", [128, 128], "bfloat16"), "ineg": ("sbuf", [128, 128], "bfloat16"),
-        "inf": ("sbuf", [128, 128], "float32"), "i16": ("sbuf", [128, 128], "bfloat16"),
-        "ibig": ("sbuf", [128, 128], "bfloat16"), "wblk": ("sbuf", [128, 128], "bfloat16"), "wide": ("sbuf", [128, 144], "bfloat16"),
-        "cz": ("sbuf", [128, 160], "float16"), "cap": ("sbuf", [128, 32], "float32"),
-        "hb": ("sbuf", [128, 256], "bfloat16"), "dmx": ("sbuf", [128, 16], "bfloat16"), "dx": ("sbuf", [128, 16], "bfloat16"),
-        "bs": ("sbuf", [128, 64], "float32"), "r0": ("sbuf", [128, 128], "bfloat16"),
-        "rsp": ("sbuf", [128, 128], "bfloat16"), "rsk": ("sbuf", [128, 128], "bfloat16"),
-        "cep": ("sbuf", [128, 256], "float16"), "ck": ("sbuf", [128, 256], "float16"),
-        "o2k": ("sbuf", [128, 128], "float16"),
-        "rst": ("sbuf", [128, 256], "bfloat16"), "dm": ("sbuf", [128, 128], "bfloat16"),
-        "ut": ("sbuf", [128, LUT + 512], "bfloat16"),
-        "st0": ("sbuf", [128, LUT + 512], "bfloat16"), "st1": ("sbuf", [128, LUT + 512], "bfloat16"),
-    }
+    bf, hf, fl = "bfloat16", "float16", "float32"
+    NCH = len(WIDTHS)
+    b = {"book": ("sbuf", [128, 6144], "int32"), "ai": ("sbuf", [128, 512], "int32"),
+         "thi": ("sbuf", [128, 8], "int32"), "wi": ("sbuf", [128, 8], "int32"),
+         "pi": ("sbuf", [128, 8], "int32"), "pj": ("sbuf", [128, 8], "int32"),
+         "off": ("sbuf", [128, 512], "uint16"), "lu": ("sbuf", [128, 96 * NCH], "uint16"), "bl": ("sbuf", [128, 16], "uint16")}
+    for dtype, sizes in (
+            (bf, {"tab": 8208, "hz": 512, "yy": 512, "hr": 768, "sg": 512, "jj": 128, "jl": 256, "jh": 128, "jd": 128, "tk": 256,
+                  "jb": 16, "ib": 128, "i16": 128, "ibig": 128, "ibn": 128, "wblk": 128, "wneg": 128, "wc": 32, "bigc": 128,
+                  "czb": 256, "eq": KW, "hb": 2 * KW, "rs": 2 * KW, "dx": 32, "bn": KW, "dm": 128,
+                  "mk": 2 * C, "lt": 256, "ut": LUT, "st": LUT, "jm": KW, "jg": KW, "jx": KW, "ineg": 128}),
+            (hf, {"ih": 128, "ihn": 128, "o15": 128, "iha": KW, "ck": 2 * KW, "cep": KW, "czh": 208,
+                  "czc": 80 * NCH, "thn": 8}),
+            (fl, {"km": 16 * NCH, "af": 512, "ll": 256 * NCH, "bs": 240, "col": 16, "loc": 32, "mj": 16, "cnt": 8, "onp": 128, "onn": 128})):
+        for name, k in sizes.items():
+            b[name] = ("sbuf", [128, k], dtype)
     for i, w in enumerate(WIDTHS):
-        b["xg%d" % i] = ("sbuf", [128, 24 * w + 32], "bfloat16")
-        b["mx%d" % i] = ("sbuf", [128, 24 * w], "bfloat16")
-        b["g2%d" % i] = ("sbuf", [128, 4112], "float32")
+        b["xg%d" % i] = ("sbuf", [128, 24 * w + 32], bf)
+        b["mx%d" % i] = ("sbuf", [128, 24 * w], bf)
+        b["g2%d" % i] = ("sbuf", [128, 4112], fl)
+        b["so%d" % i] = ("sbuf", [128, 4 * KW], fl)
+        b["rst%d" % i] = ("sbuf", [128, 4 * KW], fl)
     for i in range(STEPS):
-        b["a%d" % i] = ("sbuf", [128, 512], "float16")
-        b["say%d" % i] = ("sbuf", [128, 512], "bfloat16")
+        b["say%d" % i] = ("sbuf", [128, 512], bf)
     for i in range(STEPS + 1):
-        b["h%d" % i] = ("sbuf", [128, 16 + C], "bfloat16")
-    for x in ("of0", "of1", "ep0", "ep1", "kb0", "kb1", "yb", "xb"):
-        b[x] = ("psum", [128, 512], "float32")
+        b["a%d" % i] = ("sbuf", [128, 2 * C], hf)
+        b["h%d" % i] = ("sbuf", [128, 16 + C], bf)
+    for x in ("of0", "of1", "ep0", "ep1", "yb", "xb", "kb", "ub"):
+        b[x] = ("psum", [128, 512], fl)
     return b
 
 
 SCRATCH = buffers()
-NDMA = 11 + 16 * len(WIDTHS)
-SEMAPHORES = ["cv", "cs", "cp", "cg", "sent"] + ["d%d" % _i for _i in range(NDMA)] + \
-             ["arr%d_%d_%d" % (_t, _c, _f) for _t in range(STEPS) for _c in range(len(WIDTHS)) for _f in range(NH)]
+NDMA = 12 + 16 * len(WIDTHS)
+SEMAPHORES = ["cv", "cs", "cp", "cg", "sent"] + ["d%d" % _i for _i in range(NDMA)] + ["arr%d_%d" % (_t, _c) for _t in range(STEPS) for _c in range(len(WIDTHS))]
 
 PAR = (0.83, 0.43, 1.56, 3.8, (190.0, 200.0), 5.0, 1600.0, 350.0, 700.0, 300.0, (10.0, 0.0), 1400.0)
 FIRST = 2000.0
-ONV = {"yr": 1, "gg": 1, "hz": 1, "yw": 1, "hr": 1, "af": 0, "st": 0, "k": 0}
+ONV = {"hz": 1, "hr": 0, "af": 0, "st": 0, "k": 0, "cap": 0, "mk": 0}
 VG = {None: (), (0, 0): (1, 3)}
-OTHER = []
+OTHER = [((0.83 * 1.45, 0.43 * 1.45, 1.9, 5.0, (240.0, 250.0), 5.0, 1600.0, 350.0, 1200.0, 300.0, (10.0, 0.0), 2000.0), 0.7)]
 
 
 def cuts(lo, hi, n):
@@ -90,7 +95,7 @@ def cuts(lo, hi, n):
 
 def build(g, core, T, topo, par=None):
     CY, PCY, GA, SC, HOP, FIX, DL, RATE, RL, GI, SFIX, RB = par or PAR
-    NCH = len(WIDTHS)
+    NCH, W0 = len(WIDTHS), WIDTHS[0]
     C0 = [sum(WIDTHS[:c]) for c in range(NCH + 1)]
     ops = []
     cores = list(T.cores)
@@ -98,10 +103,20 @@ def build(g, core, T, topo, par=None):
     rank = T.rank_of(core)
     v, s, p, y = g.vector, g.scalar, g.tensor, g.sync
 
-    now = [0]
+    now, step, seen = [0], [None], {}
+    GROUP = {"vmx": 16 - NA, "pof": 4, "pep": 4, "gg": 8}
 
     def op(eng, fn, rd, wr, cost, banks=(), lat=0.0, sem=None, alt=None, onv=0):
-        ops.append({"onv": onv, "ord": [], "alt": alt, "c": now[0], "eng": eng, "fn": fn, "rd": list(rd), "wr": list(wr), "bk": list(banks),
+        kind = None
+        if step[0] is not None:
+            name = eng + "".join(x for x in (list(wr) + list(banks))[0] if not x.isdigit() and x != "_")
+            seen[name, step[0], now[0]] = k = seen.get((name, step[0], now[0]), -1) + 1
+            kind = name[1:] + ("" if eng != "d" else "d") + ("" if eng != "p" else "p") + str(k // GROUP.get(name, 1))
+        if kind and alt and kind.rstrip("0123456789") in FIXED:
+            if onv:
+                eng, fn, cost = "v", alt[0], alt[1]
+            alt, onv = None, 0
+        ops.append({"kind": kind, "at": (step[0], now[0]), "onv": onv, "ord": [], "alt": alt, "c": now[0], "eng": eng, "fn": fn, "rd": list(rd), "wr": list(wr), "bk": list(banks),
                     "cost": cost * (1.25 if eng == "g" and sem is None else 1.0) + (SFIX[0] + SFIX[1] * cost if eng == "s" and sem is None else 0.0), "lat": lat, "sem": sem, "hop": HOP})
 
     def vc(k, f=1.0):
@@ -128,8 +143,11 @@ def build(g, core, T, topo, par=None):
     def act(out, in_, fn, rd, wr, cost, banks=()):
         op("s", lambda: s.activation(out, in_, fn), rd, wr, cost, banks)
 
-    def either(onv, out, in_, rd, wr, cost_s, cost_v, add=None, banks=()):
-        if add is None:
+    def either(onv, out, in_, rd, wr, cost_s, cost_v, add=None, banks=(), mul=None):
+        if mul is not None:
+            op("s", lambda: s.activation(out, in_, ACT.Identity, scale=mul), rd, wr, cost_s, banks,
+               alt=(lambda: v.tensor_scalar(out, in_, mul, None, ALU.mult), cost_v), onv=onv)
+        elif add is None:
             op("s", lambda: s.activation(out, in_, ACT.Copy), rd, wr, cost_s, banks, alt=(lambda: v.tensor_copy(out, in_), cost_v), onv=onv)
         else:
             op("s", lambda: s.activation(out, in_, ACT.Identity, bias=add), rd, wr, cost_s, banks,
@@ -150,35 +168,36 @@ def build(g, core, T, topo, par=None):
         else:
             op("g", lambda: g.iota(out, pat, base, cm), [], wr, 130.0 + 2 * k * CY)
 
+    def sel(out, in_, pat, o, fill, base, cm, rd, wr, k):
+        op("g", lambda: g.affine_select(out, in_, pat, o, fill, base, cm), rd, wr, 170.0 + 2 * k * CY)
+
     def pool_copy(out, in_, rd, wr, k):
-        op("g", lambda: g.affine_select(out, in_, [[0, k]], ALU.is_ge, 0.0, 0, 0), rd, wr, 170.0 + 2 * k * CY)
+        sel(out, in_, [[0, k]], ALU.is_ge, 0.0, 0, 0, rd, wr, k)
 
     nd = [0]
 
-    def flight(q, fn, rd, wr, cost, lat, busy, sem, gate=()):
+    def flight(q, fn, rd, wr, cost, lat, busy, sem):
         op(q, fn, rd, wr, cost, lat=lat, sem=sem)
-        ops[-1]["gate"] = list(gate)
         op("d", None, rd, wr, busy, sem=sem)
 
-    def dma(q, out, in_, rd, wr, nbytes, gate=()):
+    def dma(q, out, in_, rd, wr, nbytes):
         sem = "d%d" % nd[0]
         nd[0] += 1
         e = y if q == "y" else s
-        flight(q, lambda: e.dma_start(out, in_), rd, wr, 60.0, DL, 240.0 + nbytes / RATE, (sem, 16), gate)
+        flight(q, lambda: e.dma_start(out, in_), rd, wr, 60.0, DL, 240.0 + nbytes / RATE, (sem, 16))
 
     def gat(k):
         return 60.0 + k * GA * CY
 
-    W0 = WIDTHS[0]
     dma("s", T.wi[:, 0:1], T.w[:], [], ["wi"], 512)
-    dma("y", T.h0[:, 16:16 + W0], T.heard[:, 0:W0], [], ["h0_0_%d" % f for f in range(NH)], 256 * W0)
+    dma("y", T.h0[:, 16:16 + W0], T.heard[:, 0:W0], [], ["h0_0"], 256 * W0)
     dma("s", T.ai[:, 0:W0], T.scroll[:, 0:W0], [], ["ai_0"], 512 * W0)
-    dma("y", T.tab[:, 2048:4096], T.cues[:, 2048:4096], [], ["tab1"], 1 << 19)
-    dma("y", T.tab[:, 4096:6160], T.cues[:, 0:2064], [], ["tab0"], 1 << 19)
-    dma("y", T.h0[:, 16 + W0:16 + C], T.heard[:, W0:C], [], ["h0_%d_%d" % (c, f) for c in range(1, NCH) for f in range(NH)], 256 * (C - W0))
+    dma("y", T.tab[:, 2048:4104], T.cues[:, 2040:4096], [], ["tab1"], 1 << 19)
+    dma("y", T.tab[:, 4104:6160], T.cues[:, 0:2056], [], ["tab0"], 1 << 19)
+    dma("y", T.h0[:, 16 + W0:16 + C], T.heard[:, W0:C], [], ["h0_%d" % c for c in range(1, NCH)], 256 * (C - W0))
     dma("y", T.ai[:, W0:C], T.scroll[:, W0:C], [], ["ai_%d" % c for c in range(1, NCH)], 512 * (C - W0))
     dma("y", T.thi[:, 0:1], T.th[:], [], ["thi"], 512)
-    dma("y", T.tab[:, 6160:8192], T.cues[:, 2064:4096], [], ["tab2"], 1 << 19)
+    dma("y", T.tab[:, 6160:8200], T.cues[:, 2056:4096], [], ["tab2"], 1 << 19)
     dma("y", T.book[:, 0:2048], T.spare[:], [], ["spare"], 1 << 20)
     dma("y", T.book[:, 2048:4096], T.spare[:], [], ["gap"], 1 << 20)
     for i, j in ((2, 0), (3, 1), (4, 3), (5, 4), (6, 5), (7, 6), (8, 7), (9, 8), (10, 9)):
@@ -188,17 +207,17 @@ def build(g, core, T, topo, par=None):
 
     io(T.pi[:, 0:1], [[0, 1]], 0, 1, ["pi"], 1, False)
     io(T.jh[:], [[1, 8], [0, 16]], 0, 0, ["jh"], 128)
-    io(T.jj[:], [[1, 144]], 0, 0, ["jj"], 144)
+    io(T.jj[:], [[1, 128]], 0, 0, ["jj"], 128)
     io(T.jl[:], [[0, 16], [1, 16]], 0, 0, ["jl"], 256)
-    for c in range(NCH):
-        io(T.loc[:, 32 * c:32 * c + 32], [[0, 2], [16, 16]], 16 + C0[c], 1, ["loc%d" % c], 32)
     io(T.jd[:], [[0, 8], [1, 8], [0, 2]], 0, 0, ["jd"], 128)
+    io(T.jb[:, 0:8], [[17, 8]], 15, 0, ["jb"], 8)
     io(T.tk[:], [[1, 16], [-1, 16]], 0, 0, ["tk"], 256)
-    if NA:
-        op("g", lambda: g.affine_select(T.jm[:], T.jh[:], [[0, 8], [-1, 16]], ALU.is_ge, -1.0, 15 - NA, 0), ["jh"], ["jm"], 170.0 + 256 * CY)
-    JM, jm = (T.jm, "jm") if NA else (T.jh, "jh")
+    io(T.loc[:, 0:32], [[1024, 2], [16, 16]], 16 - 1024, 1, ["loc"], 32)
+    io(T.jg[:], [[1, 8], [0, 17]], 0, 0, ["jg"], KW)
+    io(T.jx[:], [[16, 8], [1, 17]], 0, 0, ["jx"], KW)
+    sel(T.jm[:], T.jg[:], [[0, 8], [-1, 17]], ALU.is_ge, -1.0, 15 - NA, 0, ["jg"], ["jm"], KW)
     col = lambda j: T.col[:, j:j + 1]
-    PF, LANE, GRP, P7, P8, P1, WF, THN, L2, L34, G15, G16, PAR8 = range(13)
+    PF, LANE, GRP, P7, P8, P1, WF, L15, G16, PAR8, _, L17 = range(12)
     cp(col(PF), T.pi[:, 0:1], ["pi"], ["pf"], 1)
     for j, (o, k) in enumerate(((ALU.bitwise_and, 15), (ALU.arith_shift_right, 4), (ALU.bitwise_and, 7), (ALU.arith_shift_right, 3), (ALU.bitwise_and, 1))):
         ts(T.pj[:, j:j + 1], T.pi[:, 0:1], k, None, o, None, ["pi"], ["pj%d" % j], 1)
@@ -206,128 +225,142 @@ def build(g, core, T, topo, par=None):
     cp(T.col[:, 3:6], T.pj[:, 2:5], ["pj2", "pj3", "pj4"], ["col2"], 3)
     cp(col(WF), T.wi[:, 0:1], ["wi"], ["wf"], 1)
     ts(T.wblk[:], T.jh[:], col(GRP), col(WF), ALU.is_equal, ALU.mult, ["jh", "col", "wf"], ["wblk"], 128, 0.5)
-    ts(T.ih[:], T.jj[:, 0:128], col(PF), None, ALU.is_equal, None, ["jj", "pf"], ["ih"], 128, 0.5)
-    ts(T.ineg[:], T.jj[:, 0:128], col(PF), -1.0, ALU.is_equal, ALU.mult, ["jj", "pf"], ["ineg"], 128, 0.5)
-    ts(T.ib[:], T.jj[:, 0:128], col(PF), None, ALU.is_equal, None, ["jj", "pf"], ["ib"], 128, 0.5)
-    ts(T.inf[:], T.jj[:, 0:128], col(PF), -1.0, ALU.is_equal, ALU.mult, ["jj", "pf"], ["inf"], 128)
-    ts(T.ibig[:], T.jj[:, 0:128], col(PF), float(1 << 15), ALU.is_equal, ALU.mult, ["jj", "pf"], ["ibig"], 128, 0.5)
-    ts(T.i16[:], T.jj[:, 0:128], col(PF), -16.0, ALU.is_equal, ALU.mult, ["jj", "pf"], ["i16"], 128, 0.5)
+    either(1, T.wneg[:], T.wblk[:], ["wblk"], ["wneg"], vc(128), vc(64), mul=-1.0)
+    ts(T.ih[:], T.jj[:], col(PF), None, ALU.is_equal, None, ["jj", "pf"], ["ih"], 128, 0.5)
+    for name, k in (("ihn", -1.0), ("ib", 1.0), ("i16", -16.0), ("ibig", 2.0 ** 15), ("ibn", -2.0 ** 15)):
+        ts(T[name][:], T.jj[:], col(PF), k, ALU.is_equal, ALU.mult, ["jj", "pf"], [name], 128, 0.5)
+    ms(T.bigc[:], 1.5 * 2.0 ** 20, ["bigc"], 128, 0.5)
     for c in range(NCH):
-        cp(T.a0[:, C0[c]:C0[c + 1]], T.ai[:, C0[c]:C0[c + 1]], ["ai_%d" % c], ["a0_%d" % c], WIDTHS[c])
-    ts(col(G15), col(GRP), 16.0, 15.0, ALU.mult, ALU.add, ["col"], ["g15"], 1)
+        cp(T.a0[:, 2 * C0[c] + 1:2 * C0[c + 1]:2], T.ai[:, C0[c]:C0[c + 1]], ["ai_%d" % c], ["a0_%d" % c], WIDTHS[c])
+    io(T.mk[:, 0::2], [[0, C]], 0, 0, ["mkz"], C)
+    either(ONV["k"], T.wc[:, 0:8], T.wblk[:, 0::16], ["wblk"], ["wc0"], vc(8), vc(8), mul=-65536.0)
+    either(ONV["k"], T.wc[:, 8:16], T.wblk[:, 0::16], ["wblk"], ["wc1"], vc(8), vc(8), mul=65536.0)
+    ts(T.wc[:, 16:24], T.jj[:, 0:8], col(GRP), 128.0, ALU.is_equal, ALU.mult, ["jj", "col"], ["wc2"], 8)
+    ts(col(L15), col(LANE), -15.0, 1.0 / 16.0, ALU.add, ALU.mult, ["col"], ["l15"], 1)
     ts(col(G16), col(GRP), -16.0, None, ALU.mult, None, ["col"], ["g16"], 1)
-    ts(T.wide[:], T.jj[:], col(G15), col(WF), ALU.is_equal, ALU.mult, ["jj", "g15", "wf"], ["wide"], 144, 0.5)
-    ts(T.hb[:, 0:128], JM[:], col(GRP), 2048.0, ALU.is_equal, ALU.mult, [jm, "col"], ["hb0"], 128, 0.5)
-    ts(T.hb[:, 128:256], JM[:], col(GRP), 65536.0, ALU.is_equal, ALU.mult, [jm, "col"], ["hb1"], 128, 0.5)
-    cp(T.dx[:], T.hb[:, 0::16], ["hb0", "hb1"], ["dx"], 16)
-    ts(T.dmx[:], T.hb[:, 0::16], -2.0, None, ALU.mult, None, ["hb0", "hb1"], ["dmx"], 16)
-    ts(T.bs[:, 0:16], T.jl[:, 0:16], col(P8), 1.0 / 4096.0, ALU.is_equal, ALU.mult, ["jl", "col2"], ["bs0"], 16)
-    ts(T.bs[:, 16:64], T.jl[:, 0:48], col(P8), None, ALU.is_equal, None, ["jl", "col2"], ["bs1"], 48)
-    ts(col(THN), T.thi[:, 0:1], -1.0, -8.0, ALU.mult, ALU.add, ["thi"], ["thn"], 1)
-    ts(col(L2), col(LANE), 2.0, 1.0, ALU.mult, ALU.add, ["col"], ["l2c"], 1)
-    ts(col(L34), col(LANE), 34.0, None, ALU.mult, None, ["col"], ["l34"], 1)
     ts(col(PAR8), col(P1), 8.0, None, ALU.mult, None, ["col2"], ["par8"], 1)
-    ts(T.cep[:, 0:128], T.ih[:], col(THN), None, ALU.mult, None, ["ih", "thn"], ["cep0"], 128, 0.5)
-    ts(T.cep[:, 128:256], T.ih[:], col(L2), -60.25, ALU.mult, ALU.add, ["ih", "l2c"], ["cep1"], 128, 0.5)
-    for b in range(2):
-        ts(T.ck[:, b * 128:(b + 1) * 128], T.ih[:], col(L34), -64.0, ALU.mult, ALU.add, ["ih", "l34"], ["ck%d" % b], 128, 0.5)
-    ms(T.o2k[:], 2048.0, ["o2k"], 128, 0.5)
-    ms(T.mc[:, 2:3], 15360.0, ["mb"], 1)
-    ts(T.r0[:], T.jh[:], col(GRP), 4096.0, ALU.is_equal, ALU.mult, ["jh", "col"], ["r0"], 128, 0.5)
-    op("g", lambda: g.affine_select(T.rsp[:], T.r0[:], [[-1, 128]], ALU.not_equal, 4096.0 - 65536.0, 0, 1), ["r0"], ["rsp"], 170.0 + 256 * CY)
-    ts(T.rsk[:], T.rsp[:], 16.0, None, ALU.mult, None, ["rsp"], ["rsk"], 128, 0.5)
-    ts(T.rst[:], T.jl[:], 0.0, 1.0e9, ALU.is_equal, ALU.mult, ["jl"], ["rst"], 256, 0.5)
+    ts(col(12), col(P1), 2.0 * KW, None, ALU.mult, None, ["col2"], ["parw"], 1)
+    ts(T.thn[:, 0:1], T.thi[:, 0:1], -2.0, 1023.0, ALU.mult, ALU.add, ["thi"], ["thn"], 1)
+    cp(T.col[:, 10:11], T.thn[:, 0:1], ["thn"], ["thf"], 1)
+    DX = ["dx0", "dx1"]
+    for f, k in enumerate((2.0 ** 20, 2.0 ** 11)):
+        ts(T.hb[:, KW * f:KW * f + KW], T.jm[:], col(GRP), k, ALU.is_equal, ALU.mult, ["jm", "col"], ["hb%d" % f], KW, 0.5)
+        ts(T.dx[:, 8 * f:8 * f + 8], T.jj[:, 0:8], col(GRP), k, ALU.is_equal, ALU.mult, ["jj", "col"], ["dx%d" % f], 8)
+    either(ONV["k"], T.dx[:, 16:32], T.dx[:, 0:16], DX, ["dmx"], vc(16), vc(16), mul=-2.0)
+    ts(T.ineg[:], T.jj[:], col(PF), -1.0, ALU.is_equal, ALU.mult, ["jj", "pf"], ["ineg"], 128, 0.5)
+    ts(T.eq[:], T.jg[:], col(GRP), -128.0, ALU.is_equal, ALU.mult, ["jg", "col"], ["eq"], KW, 0.5)
+    sel(T.rs[:, KW:2 * KW], T.eq[:], [[16, 8], [1, 17]], ALU.not_equal, 15.0 * 128.0, 0, -1, ["eq"], ["rs1"], KW)
+    either(ONV["k"], T.rs[:, 0:KW], T.rs[:, KW:2 * KW], ["rs1"], ["rs0"], vc(KW), vc(KW, 0.5), mul=16.0)
+    ts(T.iha[:], T.jx[:], col(PF), 0.0625, ALU.is_equal, ALU.mult, ["jx", "pf"], ["iha"], KW, 0.5)
+    ts(col(L17), col(L15), 17.0, None, ALU.mult, None, ["l15"], ["l17"], 1)
+    for f, (j, x) in enumerate(((L17, "l17"), (L15, "l15"))):
+        ts(T.ck[:, KW * f:KW * f + KW], T.iha[:], col(j), -30.0 / 256.0, ALU.mult, ALU.add, ["iha", x], ["ck%d" % f], KW, 0.5)
+    ms(T.bn[:], 1.5 * 2.0 ** 38, ["bn"], KW, 0.5)
+    ts(T.cep[:], T.iha[:], T.col[:, 10:11], 256.0, ALU.mult, ALU.mult, ["iha", "thf"], ["cep"], KW, 0.5)
+    ms(T.o15[:], 2.0 ** 15, ["o15"], 128, 0.5)
+    io(T.onp[:], [[0, 128]], 1, 0, ["onp"], 128)
+    io(T.onn[:], [[0, 128]], -1, 0, ["onn"], 128)
+    ms(T.rst0[:], -1.0e9, ["rst_0"], 4 * KW)
+    for c in range(1, NCH):
+        either(ONV["k"], T["rst%d" % c][:], T.rst0[:], ["rst_0"], ["rst_%d" % c], vc(4 * KW), vc(4 * KW))
     ts(T.dm[:], T.jd[:], col(P7), None, ALU.is_equal, None, ["jd", "col2"], ["dm"], 128, 0.5)
-    ts(T.bl[:, 0:8], T.jj[:, 0:8], col(PAR8), None, ALU.add, None, ["jj", "par8"], ["bl"], 8)
-    ts(T.l2[:], T.loc[:], col(G16), None, ALU.add, None, ["loc%d" % c for c in range(NCH)] + ["g16"], ["l2"], 32 * NCH)
+    ts(T.bl[:, 0:8], T.jb[:, 0:8], col(12), None, ALU.add, None, ["jb", "parw"], ["bl0"], 8)
+    ts(T.bl[:, 8:16], T.jj[:, 0:8], col(PAR8), None, ALU.add, None, ["jj", "par8"], ["bl8"], 8)
+    ts(T.bs[:, 0:64], T.jl[:, 0:64], col(P8), -16.0, ALU.is_equal, ALU.mult, ["jl", "col2"], ["bs0"], 64)
+    ms(T.bs[:, 32:48], 0.0, ["bs0"], 16)
+    either(ONV["k"], T.bs[:, 64:128], T.bs[:, 0:64], ["bs0"], ["bs1"], vc(64), vc(64), mul=-1.0)
+    for at, k, x in ((128, 32, -2.0 ** -21), (160, 16, -2.0 ** -22), (176, 16, 0.0), (192, 16, 2.0 ** -11), (208, 16, -2.0 ** -20), (224, 16, -2.0 ** -11)):
+        either(ONV["k"], T.bs[:, at:at + k], T.bs[:, 0:k], ["bs0"], ["bs%d" % at], vc(k), vc(k), mul=x)
+    for at, k, e, name in ((0, 144, 19, "czb0"), (32, 16, 18, "czb0"), (64, 16, 17, "czb0"), (144, 16, 17, "czb144"), (160, 48, 8, "czb144"),
+                           (208, 32, 36, "czb208"), (240, 16, 13, "czb224")):
+        ms(T.czb[:, at:at + k], 1.5 * 2.0 ** e, [name] + (["czb80"] if at == 0 else []), k, 0.5)
+    ms(T.czb[:, 112:128], 0.0, ["czb80"], 16)
+    for at, k, x, name in ((0, 64, 0.0, "czh0"), (64, 16, 128.0, "czh0"), (80, 64, 1023.5, "czh80"), (112, 16, 0.0, "czh80"), (144, 16, 32.0, "czh80"),
+                           (160, 32, 32768.0, "czh160"), (192, 16, -15.0, "czh176")):
+        ms(T.czh[:, at:at + k], x, [name], k, 0.5)
     for c in range(NCH):
-        either(ONV["k"], T.pr[:, 64 * c:64 * c + 16], T.loc[:, 32 * c:32 * c + 16], ["loc%d" % c, "g16"], ["cc_%d" % c], vc(16), vc(16), col(G16))
-    ms(T.cz[:], 0.0, ["cz"], 160, 0.5)
-    ms(T.cz[:, 0:16], 1.0 / 64.0, ["cz"], 16)
-    ms(T.cz[:, 64:80], 258.0 / 128.0, ["cz"], 16)
-    ms(T.cz[:, 112:128], 257.0 / 128.0, ["cz"], 16)
-    ms(T.cap[:, 0:16], 256.0, ["cap0"], 16)
-    ms(T.cap[:, 16:32], float(1 << 24), ["cap1"], 16)
-    if min(WIDTHS) < 256:
-        ms(T.km[:], 0.0, ["km_%d" % c for c in range(NCH)], 16 * NCH)
+        z = 80 * c
+        for at, x in ((0, -255.5), (32, 7.75), (48, -2047.0 / 4096.0)):
+            ms(T.czc[:, z + at:z + at + 16], x, ["czc%d" % (z + at)], 16)
+        for j in range(2):
+            at = z + 16 + 48 * j
+            ts(T.czc[:, at:at + 16], T.loc[:, 16 * j:16 * j + 16], col(G16), float(C0[c]), ALU.add, ALU.add, ["loc", "g16"], ["czc%d" % at], 16)
     ms(T.hr[:], 0.0, ["hr%d_%d" % (c, b) for c in range(NCH) for b in range(2)], 768, 0.5)
     ms(T.h0[:, 0:16], 0.0, ["hzero0"], 16)
     for t in range(1, STEPS):
-        either(ONV["k"], T["h%d" % t][:, 0:16], T.h0[:, 0:16], ["hzero0"], ["hzero%d" % t], vc(16), vc(16))
+        io(T["h%d" % t][:, 0:16], [[0, 16]], 0, 0, ["hzero%d" % t], 16)
     ms(T.xg0[:, 32::3], 0.0, ["xr0"], 8 * W0, 0.5)
     for c in range(1, NCH):
-        io(T["xg%d" % c][:, 32::3], [[0, 8 * WIDTHS[c]]], 0, 0, ["xr%d" % c], 8 * WIDTHS[c])
-    ms(T.ut[:, 256:LUT], 1.0, ["ut1"], 16)
-    ms(T.ut[:, LUT:LUT + 512], 0.0, ["ut2"], 512, 0.5)
-    ms(T.st0[:, 256:LUT + 512], 0.0, ["stz0"] + ["st0_%d" % c for c in range(NCH)], 528, 0.5)
-    ms(T.st1[:, 256:LUT], 0.0, ["stz1"], 16)
+        k = 8 * WIDTHS[c]
+        either(0, T["xg%d" % c][:, 32::3], T.xg0[:, 32:32 + 3 * k:3], ["xr0"], ["xr%d" % c], vc(k), vc(k, 0.5))
+    ms(T.ut[:, 0:16], 0.0, ["ut1"], 16)
+    ms(T.ut[:, 16:40], 1.0, ["ut2"], 24)
+    ts(T.lt[:], T.jl[:], col(LANE), None, ALU.is_lt, None, ["jl", "col"], ["lt"], 256, 0.5)
+    mm(T.kb[:, 0:256], T.ib[:], T.tk[:], True, False, ["ib", "tk"], "kb", 256)
+    mm(T.kb[:, 0:256], T.i16[:], T.lt[:], False, True, ["i16", "lt"], "kb", 256)
+    ts(T.ut[:, 33:289], T.kb[:, 0:256], col(LANE), 0.0, ALU.add, ALU.is_ge, ["col", "ut2"], ["ut0"], 256, 1.0, ["kb"])
+    ts(T.st[:, 0:16], T.jl[:, 0:16], col(LANE), 1.0, ALU.is_gt, ALU.add, ["jl", "col"], ["st1"], 16)
+    ms(T.st[:, 16:40], 0.0, ["st2"], 24)
+    ts(T.st[:, 33:289], T.jl[:], col(LANE), None, ALU.is_ge, None, ["jl", "col", "st2"], ["st0"], 256, 0.5)
+    ms(T.st[:, 48:289:16], 0.0, ["st0"], 16)
     for e in range(2):
-        ts(T["st%d" % e][:, 0:256], T.jl[:], col(LANE), None, ALU.is_lt, None, ["jl", "col"], ["stt%d" % e], 256, 0.5)
-    mm(T.xb[:, 0:256], T.ib[:], T.tk[:], True, False, ["ib", "tk"], "xb", 256)
-    mm(T.xb[:, 0:256], T.i16[:], T.st0[:, 0:256], False, True, ["i16", "stt0"], "xb", 256)
-    ts(T.ut[:, 0:256], T.xb[:, 0:256], col(LANE), 0.0, ALU.add, ALU.is_ge, ["col"], ["ut0"], 256, 1.0, ["xb"])
-    for e in range(2):
-        pool_copy(T.tab[:, e:2048:2], T.tab[:, 4097 - e:6144:2], ["tab0"], ["sw%d" % e], 1024)
-        ops[-1]["ord"] += [i for i, o in enumerate(ops[:-1]) if o["eng"] == "g"]
+        pool_copy(T.tab[:, e:2048:2], T.tab[:, 4105 - e:6152:2], ["tab0"], ["sw%d" % e], 1024)
     gap = ["gap"]
 
-    ny = [1]
-    notes = []
+    notes, ny = [], [0]
+    KB, UB = T.kb, T.ub
     for t in range(STEPS):
         last = t == STEPS - 1
         H, A = T["h%d" % t], T["a%d" % t]
-        STo, STn = T["st%d" % (t % 2)], T["st%d" % ((t + 1) % 2)]
         dst = cores[(rank + 1 + t % (n - 1)) % n]
         src = cores[(rank - 1 - t % (n - 1)) % n]
         for c in range(NCH):
-            now[0] = c
+            now[0], step[0] = c, t
             c0, CW = C0[c], WIDTHS[c]
-            M, NC, PW = CW // 2, CW // 16, CW // NH
+            M, NC = CW // 2, CW // 16
             cs = slice(c0, c0 + CW)
             h0 = 16 + c0
             hs = slice(h0, h0 + CW)
-            hh, a = ["h%d_%d_%d" % (t, c, f) for f in range(NH)], "a%d_%d" % (t, c)
-            sto = "st%d_%d" % (t % 2, c)
-            of, kb = "of%d" % ((t * NCH + c) % 2), "kb%d" % ((t * NCH + c) % 2)
-            OF, KB, X, MX = T[of], T[kb], T["xg%d" % c], T["mx%d" % c]
+            hh, a = "h%d_%d" % (t, c), "a%d_%d" % (t, c)
+            X, MX, SO, RST = T["xg%d" % c], T["mx%d" % c], T["so%d" % c], T["rst%d" % c]
+            KM = T.km[:, 16 * c:16 * c + 16]
             r = lambda name: "%s_%d" % (name, c)
             par2 = lambda buf, at, b: buf[:, at + b:at + CW:2]
+            odd = slice(2 * c0 + 1, 2 * c0 + 2 * CW, 2)
+            AB = lambda b: A[:, 2 * c0 + 1 + 2 * b:2 * c0 + 2 * CW:4]
             r0 = 3 * c0 // 2
             HR = lambda b: T.hr[:, r0 + b:r0 + 3 * M:3]
             hr = ["hr%d_%d" % (c, b) for b in range(2)]
-            for f in range(NH):
-                f0, f1 = f * PW, (f + 1) * PW
-                fs = slice(c0 + f0, c0 + f1)
-                for B, bank in ((KB, kb), (OF, of)):
-                    if t == 0:
-                        mm(B[:, f0:f1], T.ih[:], A[:, fs], True, False, ["ih", a], bank, PW)
-                    else:
-                        mm(B[:, f0:f1], T.ih[:], T["a%d" % (t - 1)][:, fs], True, False, ["ih", "a%d_%d" % (t - 1, c)], bank, PW)
-                        mm(B[:, f0:f1], T.ih[:], T.mm[:, fs], False, False, ["ih", r("mm")], bank, PW)
-                    mm(B[:, f0:f1], T.wblk[:], H[:, h0 + f0:h0 + f1], False, bank == kb, ["wblk", hh[f]], bank, PW)
-                either(ONV["yr"], T.yr[:, fs], KB[:, f0:f1], [], [r("yr%d" % f)], vc(PW), vc(PW), 524288.0, [kb])
-                mm(OF[:, f0:f1], T.ineg[:], T.yr[:, fs], False, True, ["ineg", r("yr%d" % f)], of, PW)
-                for b in range(2):
-                    ts(T.off[:, c0 + M * b + f0 // 2:c0 + M * b + f1 // 2], OF[:, f0 + b:f1:2], 526336.0, None, ALU.add, None, [], [r("off%d_%d" % (b, f))], PW // 2, 1.0, [of])
             for b in range(2):
-                either(ONV["hr"], HR(b), par2(H, h0, b), hh, [hr[b]], vc(M), vc(M, 0.5), 32.0 if b else None)
-            SW, YW = OF[:, 256:256 + NC], T.yw[:, 16 * c:16 * c + NC]
-            z = 64 if t == 0 else 112
-            mm(OF[:, 256:304], T.o2k[:], T.cz[:, z:z + 48], True, False, ["o2k", "cz"], of, 48)
-            mm(OF[:, 272:304], T.ih[:], T.l2[:, 32 * c:32 * c + 32], False, False, ["ih", "l2"], of, 32)
+                of = "of%d" % b
+                O = T[of][:, 0:M]
+                if t == 0:
+                    mm(O, T.ihn[:], AB(b), True, False, ["ihn", a], of, M)
+                    mm(O, T.wneg[:], par2(H, h0, b), False, False, ["wneg", hh], of, M)
+                    mm(O, T.ibig[:], T.bigc[:, 0:M], False, False, ["ibig", "bigc"], of, M)
+                else:
+                    mm(O, T.ibig[:], T.bigc[:, 0:M], True, False, ["ibig", "bigc"], of, M)
+                    mm(O, T.wneg[:], par2(H, h0, b), False, False, ["wneg", hh], of, M)
+                mm(O, T.ibn[:], T.bigc[:, 0:M], False, False, ["ibn", "bigc"], of, M)
+                mm(O, T.wblk[:], par2(H, h0, b), False, False, ["wblk", hh], of, M)
+                mm(O, T.ih[:], AB(b), False, True, ["ih", a], of, M)
+                ts(T.off[:, c0 + M * b:c0 + M * b + M], O, 2056.0, None, ALU.add, None, [], [r("off%d" % b)], M, 1.0, [of])
+            for b in range(2):
+                either(ONV["hr"], HR(b), par2(H, h0, b), [hh], [hr[b]], vc(M), vc(M, 0.5), 32.0 if b else None)
+            CP = T.of1[0:M, 128:160]
+            half = lambda b: T.of1[0:M, 128 + 16 * b:136 + 16 * b]
+            calls = [(CP, T.ih[:, 0:M], T.czh[:, 160:192], True, False)] + [(half(b), par2(H, h0, b), T.wc[:, 0:8], False, False) for b in range(2)]
+            calls += [(CP, T.ibig[:, 0:M], T.czb[:, 208:240], False, False), (CP, T.ibn[:, 0:M], T.czb[:, 208:240], False, False)]
+            calls += [(half(b), par2(H, h0, b), T.wc[:, 8:16], False, b == 1 and t == 0) for b in range(2)]
             if t > 0:
-                mm(OF[:, 272:288], T.inf[:], T.pr[:, 64 * c + 32:64 * c + 48], False, False, ["inf", r("pr")], of, 16, 4.0)
-            for m0 in range(0, 16, PG):
-                mms([(KB[:, 320:320 + NC], T.wide[:, 15 - m:143 - m], H[:, h0 + m:h0 + CW:16], m == 0, m == 15) for m in range(m0, m0 + PG)], ["wide"] + hh, [kb], [], NC)
-            either(ONV["yw"], YW, KB[:, 320:320 + NC], [], [r("yw")], vc(16), vc(16), 524288.0, [kb])
-            SM = T.sm[:, 16 * c:16 * c + NC]
-            tt(SM, YW, KB[:, 320:320 + NC], ALU.subtract, [r("yw")], [r("sm")], 16, 1.0, [kb])
-            mm(SW, T.inf[:], SM, False, True, ["inf", r("sm")], of, 16, 4.0)
+                calls += [(half(b), par2(T.sg, c0, b), T.wc[:, 16:24], False, b == 1) for b in range(2)]
+            mms(calls, ["ih", "czh160", hh, "wc0", "wc1", "wc2", "ibig", "ibn", "czb208"] + ([r("sg")] if t else []), ["of1"], [], 16)
+            either(ONV["cap"], RST[0:M, 0::17], CP, [], [r("rst")], vc(16), vc(16), 2.0 ** 28 - 4032.0, ["of1"])
             xs = [[], []]
             mxs = [[] for i in range(16)]
-            marks = cuts(0, M, NCUT)
-            for e in range(NCUT):
-                u0, u1 = marks[e], marks[e + 1]
+            wide = 4112 if t == 0 else 6152
+            for e in range(len(MARKS) - 1):
+                u0, u1 = 2 * round(MARKS[e] * M / 2), 2 * round(MARKS[e + 1] * M / 2)
                 cut = []
                 calls = cuts(u0, u1, GPC)
                 for w0, w1 in zip(calls, calls[1:]):
@@ -337,8 +370,8 @@ def build(g, core, T, topo, par=None):
                         xs[b].append(x)
                         cut.append(x)
                         k = (w1 - w0) * 16
-                        either(onv, X[:, 16 * b + 48 * w0:16 * b + 48 * w1:3], T.tab[:, 2048:6160].indirect(T.off[:, c0 + M * b + w0:c0 + M * b + w1]),
-                               ["tab0", "tab1"] + [r("off%d_%d" % (b, f)) for f in range(2 * w0 // PW, (2 * w1 - 1) // PW + 1)], [x], gat(k), gat(k), 32.0 if b else None)
+                        either(onv, X[:, 16 * b + 48 * w0:16 * b + 48 * w1:3], T.tab[:, 2048:2048 + wide].indirect(T.off[:, c0 + M * b + w0:c0 + M * b + w1]),
+                               ["tab0", "tab1", r("off%d" % b)] + (["tab2"] if t else []), [x], gat(k), gat(k), 32.0 if b else None)
                 for i in range(16 - NA):
                     mxs[i].append("mx%d_%d_%d" % (c, i, e))
                     k = 3 * (u1 - u0)
@@ -362,123 +395,124 @@ def build(g, core, T, topo, par=None):
                     act(MX[:, m0:m0 + k], T[yb][:, 0:k], ACT.Abs, [], [mxr], vc(k), [yb])
                     for j in range(nj):
                         mxs[j0 + j].append(mxr)
-            k0 = 256 * c
             for b in range(2):
                 ep = "ep%d" % b
                 EP = T[ep]
-                bs_ = slice(k0 + b * 128, k0 + (b + 1) * 128)
+                E, EN, EF = EP[0:M, 0:2 * KW], EP[0:M, 0:KW], EP[0:M, KW:2 * KW]
+                EI = lambda i: EP[0:M, i:2 * KW:17]
                 XP = lambda i: X[:, 16 * b + 3 * i:16 * b + 3 * i + 48 * M - 47:48]
-                mm(EP[0:M, 0:256], T.o2k[:, 0:M], T.cep[:, 0:256], True, False, ["o2k", "cep0", "cep1"], ep, 256)
-                mid(EP[0:M, 0:256], HR(b), T.hb[:], [hr[b], "hb0", "hb1"], ep, 256)
-                if t > 0:
-                    mid(EP[0:M, 128:256], par2(STo, LUT + c0, b), T.rsp[:], [sto, "rsp"], ep, 128)
+                mm(E, HR(b), T.hb[:], True, False, [hr[b], "hb0", "hb1"], ep, 2 * KW)
+                mid(EN, T.o15[:, 0:M], T.cep[:], ["o15", "cep"], ep, KW)
                 for i0 in range(0, 16 - NA, PG):
-                    mms([(EP[0:M, i:256:16], XP(i), T.dx[:], False, False) for i in range(i0, min(16 - NA, i0 + PG))], xs[b] + ["dx"], [], [ep], 16)
+                    mms([(EI(i), XP(i), T.dx[:, 0:16], False, False) for i in range(i0, min(16 - NA, i0 + PG))], xs[b] + DX, [], [ep], 16)
                 for i in range(16 - NA):
-                    mid(EP[0:M, i:256:16], MX[:, 3 * M * i + b:3 * M * (i + 1):3], T.dmx[:], mxs[i] + ["dmx"], ep, 16)
+                    mid(EI(i), MX[:, 3 * M * i + b:3 * M * (i + 1):3], T.dx[:, 16:32], mxs[i] + ["dmx"], ep, 16)
                 for j0 in range(16 - NA, 16, YB):
                     nj = min(16, j0 + YB) - j0
-                    mms([(EP[0:M, j0 + j:256:16], MX[:, 3 * M * j0 + b * nj + j:3 * M * j0 + CW * nj:2 * nj], T.dx[:], False, False) for j in range(nj)],
-                        mxs[j0] + ["dx"], [], [ep], 16)
-                mm(EP[0:M, 128:256], par2(A, c0, b), T.ih[:], False, True, [a, "ih"], ep, 128)
-                op("s", lambda o_=T.gg[0:M, bs_], i_=EP[0:M, 0:128], b_=T.mc[0:M, 2:3]: s.activation(o_, i_, ACT.Relu, bias=b_), ["mb"], [r("gg%d" % b)], vc(128), [ep],
-                   alt=(lambda o_=T.gg[0:M, bs_], i_=EP[0:M, 0:128], b_=T.mc[0:M, 2:3]: v.tensor_scalar(o_, i_, b_, 0.0, ALU.add, ALU.max), vc(128)), onv=ONV["gg"])
-                scan(T.scp[0:M, bs_], T.rst[0:M, 0:128], EP[0:M, 128:256], ALU.add, ALU.min, ["rst"], [r("scp%d" % b)], 128, 1.0, [ep])
-            mm(KB[0:M, 0:256], T.o2k[:, 0:M], T.ck[:], True, False, ["o2k", "ck0", "ck1"], kb, 256)
-            for b in range(2):
-                if t > 0:
-                    mm(KB[0:M, b * 128:(b + 1) * 128], par2(STo, LUT + c0, b), T.rsk[:], False, False, [sto, "rsk"], kb, 128)
-                mm(KB[0:M, b * 128:(b + 1) * 128], par2(A, c0, b), T.ih[:], False, False, [a, "ih"], kb, 128)
-            mm(KB[0:M, 0:256], T.ibig[0:M, 0:M], T.gg[0:M, k0:k0 + 256], False, True, ["ibig", r("gg0"), r("gg1")], kb, 256)
-            scan(T.sck[0:M, k0:k0 + 256], T.rst[0:M, :], KB[0:M, 0:256], ALU.add, ALU.min, ["rst"], [r("sck")], 256, 1.0, [kb])
-            if last and notes:
-                ops[-1]["ord"].append(notes[-1])
-            KM, LL = T.km[:, 16 * c:16 * c + 16], T.ll[:, 128 * c:128 * c + 128]
-            tt(T.km[0:M, 16 * c:16 * c + 16], T.scp[0:M, k0 + 15:k0 + 256:16], T.sck[0:M, k0 + 15:k0 + 256:16], ALU.min, [r("sck"), r("scp0"), r("scp1")], [r("km")], 16)
-            mm(KB[:, 256:320], T.o2k[:], T.cz[:, 0:64], True, False, ["o2k", "cz"], kb, 64)
-            op("v", lambda o_=LL, w_=KM: v.tensor_tensor(o_, w_.indirect(T.bl[:, 0:8]), T.dm[:], ALU.mult), [r("km"), "bl", "dm"], [r("ll")], gat(128))
-            mm(KB[:, 256:320], LL, T.bs[:], False, True, [r("ll"), "bs0", "bs1"], kb, 64, 4.0)
-            Q = lambda i, j: T.qq[:, 112 * c + 16 * i:112 * c + 16 * j]
-            PR = lambda i, j: T.pr[:, 64 * c + 16 * i:64 * c + 16 * j]
-            LU = lambda i, j: T.lu[:, 96 * c + 16 * i:96 * c + 16 * j]
-            NM = T.nm[:, 48 * c:48 * c + 48]
-            ts(NM, KB[:, 272:320], -240.0 * 65536.0, None, ALU.is_ge, None, [], [r("nm")], 48, 1.0, [kb])
-            tt(Q(5, 7), KB[:, 256:288], T.cap[:], ALU.min, ["cap0", "cap1"], [r("ki")], 32, 1.0, [kb])
-            tt(PR(1, 4), NM, OF[:, 256:304], ALU.mult, [r("nm")], [r("pr")], 48, 1.0, [of])
-            cp(LU(5, 6), PR(3, 4), [r("pr")], [r("lz")], 16)
-            ts(Q(4, 5), Q(6, 7), 2047 if t == 0 else 4095, None, ALU.bitwise_and, None, [r("ki")], [r("bk")], 16)
-            ts(Q(3, 4), Q(6, 7), 3584, None, ALU.bitwise_and, None, [r("ki")], [r("gw0")], 16)
-            tt(Q(0, 3), PR(0, 3), Q(3, 6), ALU.add, [r("cc"), r("pr"), r("ki"), r("bk"), r("gw0")], [r("q3")], 48)
-            cp(LU(0, 5), Q(0, 5), [r("q3"), r("bk"), r("gw0")], [r("lu")], 80)
+                    mms([(EI(j0 + j), MX[:, 3 * M * j0 + b * nj + j:3 * M * j0 + CW * nj:2 * nj], T.dx[:, 0:16], False, False) for j in range(nj)],
+                        mxs[j0] + DX, [], [ep], 16)
+                for f, O in ((1, EF), (0, EN)):
+                    fs = slice(KW * f, KW * f + KW)
+                    calls = [(O, T.o15[:, 0:M], T.ck[:, fs], False, False)]
+                    if t > 0:
+                        calls.append((O, par2(T.sg, c0, b), T.rs[:, fs], False, False))
+                    rd = ["o15", "ck%d" % f] + ([r("sg"), "rs%d" % f] if t else [])
+                    if f:
+                        mms(calls, rd, [], [ep], KW)
+                    else:
+                        calls += [(EF, AB(b), T.iha[:], False, False), (EN, AB(b), T.iha[:], False, True)]
+                        mms([(O, L[:, 0:M], T.bn[:], False, False) for L in (T.ibig, T.ibn)] + calls, rd + ["ibig", "ibn", "bn", a, "iha"], [ep], [], KW)
+                s0 = 2 * KW * b
+                scan(SO[0:M, s0:s0 + 2 * KW], RST[0:M, s0:s0 + 2 * KW], E, ALU.max, ALU.min, [r("rst")], [r("so%d" % b)], 2 * KW, 1.0, [ep])
+                tt(T.km[0:M, 16 * c + 8 * b:16 * c + 8 * b + 8], SO[0:M, s0 + 15:s0 + KW:17], SO[0:M, s0 + KW + 15:s0 + 2 * KW:17], ALU.min, [r("so%d" % b)], [r("km%d" % b)], 8)
+                if last and notes and b:
+                    ops[-1]["ord"].append(notes[-1])
+            so = [r("so0"), r("so1")]
+            LA, LT = T.ll[:, 256 * c:256 * c + 128], T.ll[:, 256 * c + 128:256 * c + 256]
+            km = [r("km0"), r("km1")]
+            for o_, w_, at, rd, x in ((LA, SO[:], 0, so, "la"), (LT, KM, 8, km, "lt")):
+                op("v", lambda o_=o_, w_=w_, at=at: v.tensor_tensor(o_, w_.indirect(T.bl[:, at:at + 8]), T.dm[:], ALU.mult), rd + ["bl%d" % at, "dm"], [r(x)], gat(128))
+            z = 80 * c
+            lo = 16 if t == 0 else 0
+            rnd = lambda k0, k1, at: [(KB[:, k0:k1], L[:], T.czb[:, at + k0:at + k1], False, False) for L in (T.ibig, T.ibn)]
+            mm(KB[:, 0:80], T.ih[:], T.czh[:, 0:80], True, False, ["ih", "czh0"], "kb", 80)
+            mm(KB[:, lo:80], LA, T.bs[:, 128 + lo:208], False, False, [r("la"), "bs128", "bs160", "bs176", "bs192"], "kb", 80, 4.0)
+            mms(rnd(0, 80, 0) + [(KB[:, 0:80], T.ih[:], T.czh[:, 80:160], False, False)], ["ibig", "ibn", "czb0", "ih", "czh80"], ["kb"], [], 80)
+            mm(KB[:, 0:64], LT, T.bs[:, 0:64], False, False, [r("lt"), "bs0"], "kb", 64, 4.0)
+            mms(rnd(0, 64, 80), ["ibig", "ibn", "czb80"], ["kb"], [], 64)
+            mm(KB[:, 48:80], LA, T.bs[:, 208:240], False, False, [r("la"), "bs208", "bs224"], "kb", 32, 4.0)
+            mm(KB[:, 0:64], LT, T.bs[:, 64:128], False, False, [r("lt"), "bs1"], "kb", 64, 4.0)
+            mms([(KB[:, 16:80], T.ih[:], T.czc[:, z:z + 64], False, False)] + rnd(16, 80, 128) + [(KB[:, 16:32], T.ih[:], T.czc[:, z + 64:z + 80], False, True)],
+                ["ih", "ibig", "ibn", "czb144"] + ["czc%d" % (z + 16 * j) for j in range(5)], ["kb"], [], 64)
             lst = lambda i: T.lu[:, 96 * c + 16 * i:96 * c + 16 * i + NC]
-            lgw, liu, lbk = lst(0), lst(2), lst(4)
+            cp(T.lu[:, 96 * c:96 * c + 80], KB[:, 0:80], [], [r("lu")], 80, 1.0, ["kb"])
+            lbk, lgw, lz, lsp, liu = lst(0), lst(1), lst(2), lst(3), lst(4)
             rid, pid, _ = topo.addr(dst)
             msk = 0
             for e in topo.engines(core, dst)[:NE]:
                 msk |= 1 << e
             got = len(topo.engines(src, core)[:NE])
-            for f in range(NH):
-                fs = slice(c0 + f * PW, c0 + (f + 1) * PW)
-                part = lambda i: T.lu[:, 96 * c + 16 * i + f * PW // 16:96 * c + 16 * i + (f + 1) * PW // 16]
-                either(ONV["hz"], T.hz[:, fs], H[:, 0:h0 + CW].indirect(part(5)), ["hzero%d" % t, r("lz")] + ["h%d_%d_%d" % (t, e, x) for e in range(c + 1) for x in range(NH)],
-                       [r("hz%d" % f)], gat(PW), gat(PW))
-                op("v", lambda o_=T.yy[:, fs], l_=part(1), h_=T.hz[:, fs]: v.tensor_tensor(o_, T.tab[:, 0:8192].indirect(l_), h_, ALU.subtract),
-                   ["tab0", "tab1", "tab2", "sw0", "sw1", r("lu"), r("hz%d" % f)], [r("yy%d" % f)], gat(PW))
-                say = "say%d_%d_%d" % (t, c, f)
-                act(T["say%d" % t][:, fs], T.yy[:, fs], ACT.Abs, [r("yy%d" % f)], [say], vc(PW))
-                arr = "arr%d_%d_%d" % (t, c, f)
-                flight("g", lambda o_=T["h%d" % (t + 1)][:, h0 + f * PW:h0 + (f + 1) * PW], i_=T["say%d" % t][:, fs], a_=arr, pid=pid, rid=rid, msk=msk:
-                       g.remote_dma(o_, i_, T.sem[a_], T.sem["sent"], pid, rid, msk),
-                       [say], ["h%d_%d_%d" % (t + 1, c, f)], GI, RL + (FIRST if t + c + f == 0 else 0.0), RB, (arr, got, len(topo.engines(core, dst)[:NE])))
-            op("v", lambda o_=T.tt[:, cs], l_=lbk, a_=A[:, cs], w_=T.book[:, 0:2048 if t == 0 else 4096]: v.tensor_tensor(o_, w_.indirect(l_), a_, ALU.subtract),
+            either(ONV["hz"], T.hz[:, cs], H[:, 0:h0 + CW].indirect(lz), ["hzero%d" % t, r("lu")] + ["h%d_%d" % (t, e) for e in range(c + 1)], [r("hz")], gat(CW), gat(CW))
+            say = "say%d_%d" % (t, c)
+            tabs = ["tab0", "tab1", "tab2", "sw0", "sw1", r("lu")]
+            if YPE:
+                either(1 - ONV["hz"], T.yy[:, cs], T.tab[:, 0:8200].indirect(lsp), tabs, [r("yy")], gat(CW), gat(CW))
+                mm(KB[:, 256:256 + CW], T.ineg[:], T.hz[:, cs], True, False, ["ineg", r("hz")], "kb", CW)
+                mm(KB[:, 256:256 + CW], T.ib[:], T.yy[:, cs], False, True, ["ib", r("yy")], "kb", CW)
+                act(T["say%d" % t][:, cs], KB[:, 256:256 + CW], ACT.Abs, [], [say], vc(CW), ["kb"])
+            else:
+                op("v", lambda o_=T.yy[:, cs], l_=lsp, h_=T.hz[:, cs]: v.tensor_tensor(o_, T.tab[:, 0:8200].indirect(l_), h_, ALU.subtract),
+                   tabs + [r("hz")], [r("yy")], gat(CW))
+                act(T["say%d" % t][:, cs], T.yy[:, cs], ACT.Abs, [r("yy")], [say], vc(CW))
+            arr = "arr%d_%d" % (t, c)
+            flight("g", lambda o_=T["h%d" % (t + 1)][:, hs], i_=T["say%d" % t][:, cs], a_=arr, pid=pid, rid=rid, msk=msk:
+                   g.remote_dma(o_, i_, T.sem[a_], T.sem["sent"], pid, rid, msk),
+                   [say], ["h%d_%d" % (t + 1, c)], GI, RL + (FIRST if t + c == 0 else 0.0), RB, (arr, got, len(topo.engines(core, dst)[:NE])))
+            an, AN, both = "a%d_%d" % (t + 1, c), T["a%d" % (t + 1)], slice(2 * c0, 2 * c0 + 2 * CW)
+            op("v", lambda o_=A[:, 2 * c0:2 * c0 + 2 * CW:2], l_=lbk, a_=A[:, odd], w_=T.book[:, 0:2048 if t == 0 else 4096]: v.tensor_tensor(o_, w_.indirect(l_), a_, ALU.subtract),
                [r("lu"), a, "spare"] + ([] if t == 0 else gap), [r("tt")], gat(CW))
-            op("v", lambda o_=T.mm[:, cs], l_=liu, t_=T.tt[:, cs]: v.tensor_tensor(o_, T.ut[:].indirect(l_), t_, ALU.mult),
-               ["ut0", "ut1", "ut2", r("lu"), r("tt")], [r("mm")], gat(CW))
+            either(ONV["mk"], T.mk[:, odd], T.ut[:, 0:289].indirect(liu), ["ut0", "ut1", "ut2", "mkz", r("lu")], [r("mk")], gat(CW), gat(CW))
+            scan(AN[:, both], T.mk[:, both], A[:, both], ALU.mult, ALU.add, [r("mk"), r("tt"), a], [an], 2 * CW, 0.5)
             if last:
-                mm(OF[:, 0:CW], T.ih[:], A[:, cs], True, False, ["ih", a], of, CW)
-                mm(OF[:, 0:CW], T.ih[:], T.mm[:, cs], False, True, ["ih", r("mm")], of, CW)
-                either(ONV["af"], T.af[:, cs], OF[:, 0:CW], [], [r("af")], vc(CW), vc(CW), None, [of])
+                act(T.af[:, cs], AN[:, odd], ACT.Copy, [an], [r("af")], vc(CW) + 10.0)
                 dma("y", T.ys[:, cs], T.af[:, cs], [r("af")], [r("ys")], CW * 512)
-                dma("y", T.yh[:, cs], T["h%d" % STEPS][:, hs], ["h%d_%d_%d" % (STEPS, c, f) for f in range(NH)], [r("yh")], CW * 256)
+                dma("y", T.yh[:, cs], T["h%d" % STEPS][:, hs], ["h%d_%d" % (STEPS, c)], [r("yh")], CW * 256)
                 G2 = T["g2%d" % c]
                 g2 = ["g2%d_%d" % (c, e) for e in range(4)]
-                op("v", lambda w_=G2[:], l_=lgw, a_=A[:, cs]: v.tensor_copy(w_.indirect(l_), a_), [r("lu"), a], g2, 60.0 + CW * SC * CY)
+                op("v", lambda w_=G2[:], l_=lgw, a_=A[:, odd]: v.tensor_copy(w_.indirect(l_), a_), [r("lu"), a], g2, 60.0 + CW * SC * CY)
                 notes.append(len(ops) - 1)
                 for e in range(4):
                     dma("y" if e % 2 == 0 or c < NCH - 1 else "s", T.yg[:, e * 512 + c0:e * 512 + c0 + CW], G2[:, 16 + e * 512 + c0:16 + e * 512 + c0 + CW],
                         [g2[e]], ["yg%d_%d" % (c, e)], CW * 512)
             else:
-                an = "a%d_%d" % (t + 1, c)
-                dma("y", T["a%d" % (t + 1)][:, cs], A[:, cs], [a], [an], CW * 256)
-                sem = "d%d" % nd[0]
-                nd[0] += 1
-                flight("g", lambda o_=T["a%d" % (t + 1)][:, cs], i_=T.mm[:, cs]: g.dma_start(o_, i_, accum_op=ALU.add),
-                       [an, r("mm")], [an], 1300.0 + (1500.0 if t + c == 0 else 0.0), 2200.0, 240.0 + CW * 512 / RATE, (sem, 16))
-                either(ONV["st"], STn[:, LUT + c0:LUT + c0 + CW], STo[:].indirect(liu),
-                       ["stt%d" % (t % 2), "stz%d" % (t % 2), r("lu")] + ["st%d_%d" % (t % 2, e) for e in range(NCH)], ["st%d_%d" % ((t + 1) % 2, c)], gat(CW), gat(CW))
+                either(ONV["st"], T.sg[:, cs], T.st[:, 0:289].indirect(liu), ["st0", "st1", "st2", r("lu")], [r("sg")], gat(CW), gat(CW))
+                op("s", lambda i_=KM, o_=T.cnt[:, c:c + 1]: s.activation(T.mj[:], i_, ACT.Sign, bias=3839.0 * 128.0 + 1.0 / 32.0, accum_out=o_), km, ["mj", r("cnt")], vc(16) + 20.0)
         if not last:
             for c in range(NCH):
-                op("v", lambda l_=T.lu[:, 96 * c:96 * c + WIDTHS[c] // 16], a_=A[:, C0[c]:C0[c + 1]]: v.tensor_copy(T.book[:, 2032:6144].indirect(l_), a_),
+                op("v", lambda l_=T.lu[:, 96 * c + 16:96 * c + 16 + WIDTHS[c] // 16], a_=A[:, 2 * C0[c] + 1:2 * C0[c + 1]:2]: v.tensor_copy(T.book[:, 2032:6144].indirect(l_), a_),
                    ["lu_%d" % c, "a%d_%d" % (t, c)], gap + ["spare"], 60.0 + WIDTHS[c] * SC * CY)
                 notes.append(len(ops) - 1)
             if t == STEPS - 2:
                 for c in range(NCH):
                     for e in range(4):
-                        at = e * 512 + C0[c]
-                        pool_copy(T["g2%d" % c][:, 16 + at:16 + at + WIDTHS[c]], T.book[:, 2048 + at:2048 + at + WIDTHS[c]], gap, ["g2%d_%d" % (c, e)], WIDTHS[c])
-            for c in range(NCH):
-                mm(KB[:, 336:352], T.o2k[:], T.nm[:, 48 * c:48 * c + 16], c == 0, c == NCH - 1, ["o2k", "nm_%d" % c], kb, 16)
-            op("s", lambda i_=KB[:, 336:352]: s.activation(T.mj[:], i_, ACT.Identity, bias=-0.46875, scale=-1.0 / 2048.0, accum_out=T.mc[:, 0:1]),
-               [], ["mc"], vc(16) + 20.0, [kb])
-            ts(T.mc[:, 1:2], T.mc[:, 0:1], 201326592.0, -201326592.0, ALU.add, ALU.add, ["mc"], ["mr"], 1)
-            ts(T.mc[:, 2:3], T.mc[:, 0:1], T.mc[:, 1:2], -2048.0, ALU.subtract, ALU.mult, ["mc", "mr"], ["mb"], 1)
+                        at, CW = e * 512 + C0[c], WIDTHS[c]
+                        pool_copy(T["g2%d" % c][:, 16 + at:16 + at + CW], T.book[:, 2048 + at:2048 + at + CW], gap, ["g2%d_%d" % (c, e)], CW)
+            MC = UB[:, 32:33]
+            mm(MC, T.ih[:], T.czh[:, 192:193], True, False, ["ih", "czh176"], "ub", 1)
+            for x, L in (("onn", T.onn), ("onp", T.onp)):
+                for c in range(NCH):
+                    mm(MC, L[:], T.cnt[:, c:c + 1], False, False, [x, "cnt_%d" % c], "ub", 1, 4.0)
+                if x == "onn":
+                    mms([(MC, T.ibig[:], T.czb[:, 240:241], False, False), (MC, T.ibn[:], T.czb[:, 240:241], False, False)], ["ibig", "ibn", "czb224"], ["ub"], [], 1)
+            mm(MC, T.ih[:], T.thn[:, 0:1], False, True, ["ih", "thn"], "ub", 1)
+            ts(T.cep[:], T.iha[:], MC, 256.0, ALU.mult, ALU.mult, ["iha"], ["cep"], KW, 0.5, ["ub"])
     return ops
 
 
 def depend(ops):
     lw, rds = {}, {}
     for i, o in enumerate(ops):
-        d = set(lw[x] for x in o.get("gate", []))
+        d = set()
         for x in o["rd"]:
             if x in lw:
                 d.add(lw[x])
@@ -563,6 +597,166 @@ def rerun(oth, pre, seq, eng):
     return end
 
 
+def pattern(ops, others, pre, suc, eng):
+    m = len(ops)
+    zero, lat = [0.0] * m, [o["lat"] for o in ops]
+    kinds = sorted(set(o["kind"] for o in ops if o["kind"]))
+    members = {k: [i for i in range(m) if ops[i]["kind"] == k] for k in kinds}
+    soon = [0.0] * m
+    for i in range(m):
+        for j, lag, wait in pre[i]:
+            if ops[j]["at"] == ops[i]["at"] and ops[j]["kind"]:
+                soon[i] = max(soon[i], soon[j] + ops[j]["cost"] + lag + 200.0 * wait)
+    time = {k: soon[members[k][len(members[k]) // 2]] + LATE.get(k.rstrip("0123456789"), 0.0) for k in kinds}
+    time.update({k: x for k, x in PLAN.items() if k in time})
+    names = [k for k in time if k in PLAN or not k.startswith(("epp", "kbp", "ofp", "ubp"))]
+    for o in ops:
+        if o["kind"]:
+            time["at%d%d" % o["at"]] = PERIOD * o["at"][0] + LAM * o["at"][1]
+    names += 2 * [k for k in time if k.startswith("at")]
+    cls = [o["kind"] and o["kind"] + CLASS[o["at"][0]][o["at"][1]] for o in ops]
+    queue = {cls[i]: eng[i] for i in range(m) if cls[i] and ops[i]["alt"]}
+    at = [o["kind"] and "at%d%d" % o["at"] for o in ops]
+
+    def value(time, queue):
+        key = [time[a] + time[o["kind"]] if a else 1e9 for a, o in zip(at, ops)]
+        for i in range(m - 1, -1, -1):
+            if not ops[i]["kind"]:
+                key[i] = min([key[j] - lag - 200.0 for j, lag, wait in suc[i]] + [1e9]) - ops[i]["cost"]
+        for i in range(m):
+            for j, lag, wait in pre[i]:
+                if key[i] <= key[j]:
+                    key[i] = key[j] + 1e-3
+        e = [queue.get(k, x) for k, x in zip(cls, eng)]
+        t0, t1, end = place(ops, sorted(range(m), key=lambda i: key[i]), pre, (zero, lat), e)
+        if others:
+            seq = sorted(range(m), key=lambda i: t0[i])
+            end = (end + sum(wt * rerun(oth, opre, seq, e) for oth, opre, wt in others)) / (1.0 + sum(x[2] for x in others))
+        return end, key, e
+
+    rng = np.random.default_rng(SEED)
+    now = best = value(time, queue)
+    for x in range(TRIES):
+        nt, nq = dict(time), dict(queue)
+        u = rng.random(4)
+        if u[0] < 0.15:
+            for k in rng.choice(sorted(queue), 1 + int(u[1] * 2), replace=False):
+                nq[str(k)] = "v" if queue[str(k)] == "s" else "s"
+        else:
+            for k in rng.choice(names, 1 + int(u[1] * u[1] * 3), replace=False):
+                nt[str(k)] += float(rng.normal()) * (STEP[0] if u[2] < 0.5 else STEP[1])
+        new = value(nt, nq)
+        if new[0] < now[0] - WARM * (1.0 - x / TRIES) * math.log(u[3] + 1e-9):
+            now, time, queue = new, nt, nq
+            if now[0] < best[0]:
+                best = now
+                FOUND[:] = [now[0], time, queue]
+    return best[1], best[2]
+
+
+FOUND = []
+
+
+def spot(slots, t, cost):
+    lo, hi = 0, len(slots) >> 1
+    if hi and slots[-1] > t:
+        while lo < hi:
+            md = (lo + hi) >> 1
+            if slots[2 * md + 1] <= t:
+                lo = md + 1
+            else:
+                hi = md
+        x, n = 2 * lo, len(slots)
+        while x < n and slots[x] < t + cost - 1e-6:
+            if slots[x + 1] > t:
+                t = slots[x + 1]
+            x += 2
+        slots[x:x] = (t, t + cost)
+    else:
+        slots += (t, t + cost)
+    return t + cost
+
+
+def tighten(ops, others, pre, key, eng):
+    m = len(ops)
+    Q = "vspgyd"
+    eng = [Q.index(e) for e in eng]
+    W = []
+    for oth, opre, wt in [(ops, pre, 1.0)] + others:
+        hop = oth[0]["hop"][1]
+        W.append(([[(j, lag + (hop if wait else 0.0)) for j, lag, wait in x] for x in opre], [[o["alt"][1] if o["alt"] else o["cost"]] + [o["cost"]] * 5 for o in oth],
+                  [o["lat"] if o["eng"] == "d" else 0.0 for o in oth], wt))
+    total = sum(w[3] for w in W)
+    sucs = []
+    for w in W:
+        suc = [[] for i in range(m)]
+        for i in range(m):
+            for j, lag in w[0][i]:
+                suc[j].append((i, lag))
+        sucs.append(suc)
+    free = [i for i in range(m) if ops[i]["alt"] is not None]
+    ends = [i for i in range(m) if ops[i]["eng"] == "d"]
+    rng = np.random.default_rng(SEED)
+
+    def put(seq, before, cost, first, eng):
+        slots = [[] for e in Q]
+        fin = [0.0] * m
+        for i in seq:
+            t = first[i]
+            for j, lag in before[i]:
+                u = fin[j] + lag
+                if u > t:
+                    t = u
+            e = eng[i]
+            fin[i] = spot(slots[e], t, cost[i][e])
+        return fin
+
+    def run(w, seq, eng):
+        before, cost, lat, wt = w
+        fin, at = [0.0] * m, [0.0] * 6
+        for i in seq:
+            e = eng[i]
+            t = at[e]
+            for j, lag in before[i]:
+                u = fin[j] + lag
+                if u > t:
+                    t = u
+            fin[i] = at[e] = t + cost[i][e]
+        return max(fin[i] + lat[i] for i in ends)
+
+    zero = [0.0] * m
+    best, keep = None, None
+    seq = sorted(range(m), key=lambda i: key[i])
+    for x in range(ROUNDS):
+        k = x % len(W) if TURN else 0
+        before, cost, lat, wt = W[k]
+        fin = put(seq, before, cost, zero, eng)
+        t0 = [fin[i] - cost[i][eng[i]] for i in range(m)]
+        seq = np.argsort(t0, kind="stable").tolist()
+        end = sum(w[3] * (run(w, seq, eng) if w is not W[k] else max(fin[i] + lat[i] for i in ends)) for w in W) / total
+        if best is None or end < best[1]:
+            best = ([(i, Q[eng[i]], t0[i]) for i in seq], end)
+        if keep is None or end < keep[2] + SLACK * (1.0 - x / ROUNDS):
+            keep = (fin, eng, end)
+        fin, eng = np.array(keep[0]), list(keep[1])
+        lo = float(rng.random()) * (float(fin.max()) + WIDE) - WIDE
+        near = [i for i in free if lo < fin[i] < lo + WIDE]
+        for i in rng.choice(near, int(rng.integers(0, FLIP + 1))).tolist() if near else []:
+            eng[i] = 1 - eng[i] if rng.random() < (PV if eng[i] else 1.0) else eng[i]
+        back = (-fin + float(rng.choice(AMPS)) * rng.random(m) * ((fin > lo) & (fin < lo + WIDE))).tolist()
+        k = (x + 1) % len(W) if TURN else 0
+        suc = sucs[k]
+        for i in range(m - 1, -1, -1):
+            b = back[i]
+            for j, lag in suc[i]:
+                if back[j] >= b:
+                    b = back[j] + 1e-3
+            back[i] = b
+        fin = put(np.argsort(back, kind="stable").tolist(), suc, W[k][1], W[k][2], eng)
+        seq = np.argsort([-u for u in fin], kind="stable").tolist()
+    return best
+
+
 def schedule(ops, others):
     m = len(ops)
     pre = links(ops)
@@ -582,6 +776,10 @@ def schedule(ops, others):
     rng = np.random.default_rng(SEED)
     best, keep = None, None
     eng = ["v" if o["onv"] else o["eng"] for o in ops]
+    if TRIES:
+        key, eng = pattern(ops, others, pre, suc, eng)
+    if FAST:
+        return tighten(ops, others, pre, key, eng)
     for x in range(ROUNDS):
         t0, t1, end = place(ops, sorted(range(m), key=lambda i: (key[i], i)), pre, (zero, lat), eng)
         seq = sorted(range(m), key=lambda i: (t0[i], i))
@@ -754,7 +952,182 @@ def plan(g, core, T, topo):
     eng = [None] * len(ops)
     for i, e, _ in first:
         eng[i] = e
-    return polish([(ops, links(ops), 1.0)] + others, [x[0] for x in first], eng)
+    return refine([(ops, links(ops), 1.0)] + others, [x[0] for x in first], eng)
+
+
+def refine(worlds, seq, eng):
+    ops = worlds[0][0]
+    m = len(ops)
+    Q = "vspgyd"
+    eng = [Q.index(e) for e in eng]
+    up = [set(j for j, _, _ in worlds[0][1][i]) for i in range(m)]
+    free = [o["alt"] is not None for o in ops]
+    W = []
+    for oth, pre, wt in worlds:
+        hop = oth[0]["hop"][1]
+        quick = [[(j, lag + (hop if wait else 0.0)) for j, lag, wait in pre[i] if wait or lag or oth[j]["eng"] != oth[i]["eng"] or free[i] or free[j]] for i in range(m)]
+        suc = [[] for i in range(m)]
+        for i in range(m):
+            for j, lag in quick[i]:
+                suc[j].append((i, lag))
+        cost = [[o["alt"][1] if o["alt"] else o["cost"]] + [o["cost"]] * 5 for o in oth]
+        W.append((quick, suc, cost, [o["lat"] if o["eng"] == "d" else 0.0 for o in oth], wt))
+    total = sum(w[4] for w in W)
+
+    ends = [i for i in range(m) if ops[i]["eng"] == "d"]
+
+    def full(w, seq, eng, old=None, lo=0, hi=m):
+        pre, suc, cost, lat, wt = w
+        fin, why, tail = old[:3] if old else ([0.0] * m, [-1] * m, [0.0] * m)
+        prev, at = [-1] * 6, [0.0] * 6
+        for i in seq[:lo]:
+            prev[eng[i]] = i
+        at = [fin[i] if i >= 0 else 0.0 for i in prev]
+        for i in seq[lo:]:
+            e = eng[i]
+            t, y = at[e], -2 - prev[e]
+            for j, lag in pre[i]:
+                u = fin[j] + lag
+                if u > t:
+                    t, y = u, j
+            fin[i] = at[e] = t + cost[i][e]
+            why[i] = y
+            prev[e] = i
+        at = [0.0] * 6
+        for i in seq[:hi:-1]:
+            at[eng[i]] = tail[i]
+        for i in seq[hi::-1]:
+            e = eng[i]
+            t = at[e]
+            if lat[i] > t:
+                t = lat[i]
+            for j, lag in suc[i]:
+                u = tail[j] + lag
+                if u > t:
+                    t = u
+            tail[i] = at[e] = t + cost[i][e]
+        end = max(ends, key=lambda i: fin[i] + lat[i])
+        return fin, why, tail, end, fin[end] + lat[end]
+
+    def guess(w, st, win, neng, lo, hi):
+        pre, suc, cost, lat, wt = w
+        fin, tail = list(st[0]), st[2]
+        at = [0.0] * 6
+        for i in seq[max(0, lo - REACH):lo]:
+            at[eng[i]] = fin[i]
+        val = 0.0
+        for i in win:
+            e = neng[i]
+            t = at[e]
+            for j, lag in pre[i]:
+                u = fin[j] + lag
+                if u > t:
+                    t = u
+            fin[i] = at[e] = t = t + cost[i][e]
+            if t + lat[i] > val:
+                val = t + lat[i]
+        for i in seq[hi + 1:hi + 1 + REACH]:
+            e = eng[i]
+            t = at[e]
+            at[e] = 0.0
+            for j, lag in pre[i]:
+                if pos[j] <= hi:
+                    u = fin[j] + lag
+                    if u > t:
+                        t = u
+            if t + tail[i] > val:
+                val = t + tail[i]
+        return val
+
+    rng = np.random.default_rng(SEED)
+    draw = rng.random((MOVES, 4)).tolist()
+    state = [full(w, seq, eng) for w in W]
+    now = sum(w[4] * s[4] for w, s in zip(W, state)) / total
+    best = (now, list(seq), list(eng))
+    held, took = None, [0]
+    for x in range(MOVES):
+        d = draw[x]
+        if held is None:
+            took[0] += 1
+            if took[0] % RESORT == 0:
+                fin, cost = state[0][0], W[0][2]
+                seq = sorted(seq, key=lambda i: fin[i] - cost[i][eng[i]])
+            pos = [0] * m
+            for k, i in enumerate(seq):
+                pos[i] = k
+            held = []
+            for s in state:
+                i, why = s[3], s[1]
+                while i >= 0:
+                    j = why[i]
+                    if j <= -2:
+                        j = -2 - j
+                        held.append((j, i))
+                    i = j
+        j, i = held[int(d[0] * len(held))]
+        neng = eng
+        if d[1] < 0.25:
+            k = i if d[2] < 0.5 else j
+            if not free[k]:
+                continue
+            neng = list(eng)
+            neng[k] = 1 - eng[k]
+            lo = hi = pos[k]
+            if d[1] < 0.1:
+                near = [u for u in seq[max(0, lo - SPAN):lo + SPAN] if free[u] and eng[u] == neng[k]]
+                if not near:
+                    continue
+                u = near[int(d[1] * 10.0 * len(near))]
+                neng[u] = eng[k]
+                lo, hi = min(lo, pos[u]), max(lo, pos[u])
+            win = seq[lo:hi + 1]
+        else:
+            lo, hi = pos[j], pos[i]
+            more = int(d[2] * d[2] * 6)
+            if d[1] < 0.65:
+                k = lo - 1
+                while more > 0 and k >= 0:
+                    if eng[seq[k]] == eng[i]:
+                        lo, more = k, more - 1
+                    k -= 1
+                need, go, stay = set(up[i]), [i], []
+                for k in range(hi - 1, lo - 1, -1):
+                    if seq[k] in need:
+                        need |= up[seq[k]]
+                        go.append(seq[k])
+                    else:
+                        stay.append(seq[k])
+                win = go[::-1] + stay[::-1]
+            else:
+                k = hi + 1
+                while more > 0 and k < m:
+                    if eng[seq[k]] == eng[i]:
+                        hi, more = k, more - 1
+                    k += 1
+                late, go, stay = {j}, [j], []
+                for k in range(lo + 1, hi + 1):
+                    if up[seq[k]] & late:
+                        late.add(seq[k])
+                        go.append(seq[k])
+                    else:
+                        stay.append(seq[k])
+                win = stay + go
+            if win == seq[lo:hi + 1]:
+                continue
+        room = now - HEAT * (1.0 - x / MOVES) * math.log(d[3] + 1e-9)
+        if sum(w[4] * guess(w, s, win, neng, lo, hi) for w, s in zip(W, state)) / total <= room:
+            seq, eng, held = seq[:lo] + win + seq[hi + 1:], neng, None
+            state = [full(w, seq, eng, s, lo, hi) for w, s in zip(W, state)]
+            now = sum(w[4] * s[4] for w, s in zip(W, state)) / total
+            if now < best[0]:
+                best = (now, seq, eng)
+    now, seq, eng = best
+    state = [full(w, seq, eng) for w in W]
+    ENDS[:] = [s[4] for s in state]
+    return [(i, Q[eng[i]], state[0][0][i] - W[0][2][i][eng[i]]) for i in seq], now
+
+
+ENDS = []
 
 
 ORDER = {}

@@ -1,126 +1,88 @@
 import math
 import numpy as np
 import comms_topo
+from concourse.bass import DstId, RemoteDMATransfer
 from concourse.mybir import dt, AluOpType, AxisListType, ActivationFunctionType
 
 ALU = AluOpType
 ACT = ActivationFunctionType
 C, V, VX, STEPS = 512, 2048, 4096, 4
-WIDTHS = (256, 256)
-MARKS = (0.0, 0.5, 1.0)
-NA = 4
-YB = 4
-YPE = False
+NCH, CW, M = 2, 256, 128
+MARKS = (0, 64, 128)
+SHORT, ALONE = (0, 48, 96, 128), ()
+QUICK = ((3, 1),)
+HRG = False
 GPC = 2
+NA = 4
 PG = 4
 NE = 8
 KW = 8 * 17
 LUT = 296
 LAM = 1000.0
-ROUNDS = 3600
-PV = 0.7
-FLIP = 2
-SEED = 5
-SLACK = 120.0
-MOVES = 12000
-HEAT = 30.0
-TRIES = 0
-PLAN = {"off0": 500, "off1": 850, "hr0": 200, "hr1": 330, "x0": 810, "x1": 1200, "x2": 1540, "x3": 2270, "x4": 3200, "x5": 3000, "x6": 3950, "x7": 4700,
-        "mx0": 3930, "mx1": 5620, "ybp0": 3200, "ybp1": 3400, "xbp0": 5600, "xbp1": 5800, "ab0": 5420, "ab1": 6050, "rst0": 7000,
-        "epp0": 1000, "epp1": 5500, "epp2": 5700, "epp3": 6000, "epp4": 6600, "epp5": 1200, "epp6": 5550, "epp7": 5750, "epp8": 6050, "epp9": 6700,
-        "so0": 7300, "so1": 7650, "km0": 7600, "km1": 7900, "la0": 8100, "lt0": 8400, "lu0": 9430, "hz0": 9700, "yy0": 10300, "say0": 11200,
-        "h0": 11500, "hd0": 12500, "tt0": 12450, "mk0": 14000, "sg0": 14400, "a0": 14700, "mj0": 8200, "cep0": 9600, "gap0": 14150, "gap1": 21650, "g0": 23000}
-FAST = True
-TURN = False
-AMPS = (100.0, 400.0, 1000.0, 2500.0)
-WIDE = 6000.0
-FIXED = ()
-WARM = 60.0
-STEP = (300.0, 1500.0)
-CLASS = ("ab", "cc", "cc", "cd")
-PERIOD = 15000.0
-LATE = {"tt": 2000.0, "mk": 2000.0, "a": 2000.0, "sg": 2000.0, "gap": 6000.0}
-REACH = 150
-RESORT = 8
-SPAN = 40
+STAGES = ((6, 130.0), (16, 50.0))
+ROUNDS, WIDE, AMPS, FLIP, PV = 3500, 6000.0, (100.0, 400.0, 1000.0, 2500.0), 2, 0.7
+MOVES, HEAT, REACH, RESORT, SPAN = 35000, 12.0, 150, 8, 40
+SEED = 2
 
 
 def buffers():
     bf, hf, fl = "bfloat16", "float16", "float32"
-    NCH = len(WIDTHS)
-    b = {"book": ("sbuf", [128, 6144], "int32"), "ai": ("sbuf", [128, 512], "int32"),
-         "thi": ("sbuf", [128, 8], "int32"), "wi": ("sbuf", [128, 8], "int32"),
-         "pi": ("sbuf", [128, 8], "int32"), "pj": ("sbuf", [128, 8], "int32"),
-         "off": ("sbuf", [128, 512], "uint16"), "lu": ("sbuf", [128, 96 * NCH], "uint16"), "bl": ("sbuf", [128, 16], "uint16")}
+    b = {}
     for dtype, sizes in (
-            (bf, {"tab": 8208, "hz": 512, "yy": 512, "hr": 768, "sg": 512, "jj": 128, "jl": 256, "jh": 128, "jd": 128, "tk": 256,
-                  "jb": 16, "ib": 128, "i16": 128, "ibig": 128, "ibn": 128, "wblk": 128, "wneg": 128, "wc": 32, "bigc": 128,
-                  "czb": 256, "eq": KW, "hb": 2 * KW, "rs": 2 * KW, "dx": 32, "bn": KW, "dm": 128,
-                  "mk": 2 * C, "lt": 256, "ut": LUT, "st": LUT, "jm": KW, "jg": KW, "jx": KW, "ineg": 128}),
-            (hf, {"ih": 128, "ihn": 128, "o15": 128, "iha": KW, "ck": 2 * KW, "cep": KW, "czh": 208,
-                  "czc": 80 * NCH, "thn": 8}),
-            (fl, {"km": 16 * NCH, "af": 512, "ll": 256 * NCH, "bs": 240, "col": 16, "loc": 32, "mj": 16, "cnt": 8, "onp": 128, "onn": 128})):
+            ("int32", {"book": 6144, "ai": C, "thi": 8, "wi": 8, "pi": 8, "pj": 8}),
+            ("uint16", {"off": C, "lu": 64 * NCH, "bl": 16}),
+            (bf, {"tab": 8208, "yy": CW, "hr": 768, "sg": C, "mk": 2 * C, "jj": 128, "jl": 256, "jh": 128, "jd": 128, "tk": 256, "jb": 16, "jm": KW, "jg": KW, "jx": KW,
+                  "ib": 128, "ineg": 128, "i16": 128, "ibig": 128, "ibn": 128, "wblk": 128, "wneg": 128, "wc": 32, "bigc": 128, "czb": 160,
+                  "eq": KW, "hb": 2 * KW, "rs": 2 * KW, "dx": 32, "bn": KW, "dm": 128, "lt": 256, "ut": LUT, "st": LUT}),
+            (hf, {"ih": 128, "ihn": 128, "o15": 128, "iha": KW, "ck": 2 * KW, "cep": KW, "czh": 224, "czc": 32, "thn": 8}),
+            (fl, {"km": 16 * NCH, "af": C, "ll": 256 * NCH, "bs": 192, "col": 16, "loc": 32, "mj": 16, "cnt": 8, "onp": 128, "onn": 128})):
         for name, k in sizes.items():
             b[name] = ("sbuf", [128, k], dtype)
-    for i, w in enumerate(WIDTHS):
-        b["xg%d" % i] = ("sbuf", [128, 24 * w + 32], bf)
-        b["mx%d" % i] = ("sbuf", [128, 24 * w], bf)
+    for i in range(NCH):
+        b["xg%d" % i] = ("sbuf", [128, 24 * CW + 32], bf)
+        b["mx%d" % i] = ("sbuf", [128, 24 * CW], bf)
         b["g2%d" % i] = ("sbuf", [128, 4112], fl)
         b["so%d" % i] = ("sbuf", [128, 4 * KW], fl)
         b["rst%d" % i] = ("sbuf", [128, 4 * KW], fl)
     for i in range(STEPS):
-        b["say%d" % i] = ("sbuf", [128, 512], bf)
+        b["say%d" % i] = ("sbuf", [128, C], bf)
+        b["up%d" % i] = ("sbuf", [128, C], bf)
     for i in range(STEPS + 1):
         b["a%d" % i] = ("sbuf", [128, 2 * C], hf)
-        b["h%d" % i] = ("sbuf", [128, 16 + C], bf)
+        b["h%d" % i] = ("sbuf", [128, C], bf)
     for x in ("of0", "of1", "ep0", "ep1", "yb", "xb", "kb", "ub"):
         b[x] = ("psum", [128, 512], fl)
     return b
 
 
 SCRATCH = buffers()
-NDMA = 12 + 16 * len(WIDTHS)
-SEMAPHORES = ["cv", "cs", "cp", "cg", "sent"] + ["d%d" % _i for _i in range(NDMA)] + ["arr%d_%d" % (_t, _c) for _t in range(STEPS) for _c in range(len(WIDTHS))]
+SEMAPHORES = ["cv", "cs", "cp", "cg", "sent"] + ["d%d" % _i for _i in range(11 + 6 * NCH)] + ["arr%d_%d" % (_t, _c) for _t in range(STEPS) for _c in range(NCH)]
 
-PAR = (0.83, 0.43, 1.56, 3.8, (190.0, 200.0), 5.0, 1600.0, 350.0, 700.0, 300.0, (10.0, 0.0), 1400.0)
-FIRST = 2000.0
-ONV = {"hz": 1, "hr": 0, "af": 0, "st": 0, "k": 0, "cap": 0, "mk": 0}
-VG = {None: (), (0, 0): (1, 3)}
-OTHER = [((0.83 * 1.45, 0.43 * 1.45, 1.9, 5.0, (240.0, 250.0), 5.0, 1600.0, 350.0, 1200.0, 300.0, (10.0, 0.0), 2000.0), 0.7)]
-
-
-def cuts(lo, hi, n):
-    return [lo + 2 * ((hi - lo) // 2 * i // n) for i in range(n + 1)]
+TIMES = [((0.83, 0.43, 1.56, 3.8, 200.0, 700.0, 1400.0), 1.0),
+         ((0.83 * 1.45, 0.43 * 1.45, 1.9, 5.0, 250.0, 1200.0, 2000.0), 0.3),
+         ((0.83 * 1.2, 0.43 * 1.2, 1.1, 2.0, 300.0, 1500.0, 2500.0), 0.25)]
+FIX, SFIX, DL, RATE, GI, FIRST = 5.0, 10.0, 1600.0, 350.0, 300.0, 2000.0
+YBANK = "ub"
 
 
-def build(g, core, T, topo, par=None):
-    CY, PCY, GA, SC, HOP, FIX, DL, RATE, RL, GI, SFIX, RB = par or PAR
-    NCH, W0 = len(WIDTHS), WIDTHS[0]
-    C0 = [sum(WIDTHS[:c]) for c in range(NCH + 1)]
+def build(g, core, T, topo, par):
+    CY, PCY, GA, SC, HOP, RL, RB = par
     ops = []
     cores = list(T.cores)
     n = len(cores)
     rank = T.rank_of(core)
     v, s, p, y = g.vector, g.scalar, g.tensor, g.sync
-
-    now, step, seen = [0], [None], {}
-    GROUP = {"vmx": 16 - NA, "pof": 4, "pep": 4, "gg": 8}
+    now, nd = [0], [0]
 
     def op(eng, fn, rd, wr, cost, banks=(), lat=0.0, sem=None, alt=None, onv=0):
-        kind = None
-        if step[0] is not None:
-            name = eng + "".join(x for x in (list(wr) + list(banks))[0] if not x.isdigit() and x != "_")
-            seen[name, step[0], now[0]] = k = seen.get((name, step[0], now[0]), -1) + 1
-            kind = name[1:] + ("" if eng != "d" else "d") + ("" if eng != "p" else "p") + str(k // GROUP.get(name, 1))
-        if kind and alt and kind.rstrip("0123456789") in FIXED:
-            if onv:
-                eng, fn, cost = "v", alt[0], alt[1]
-            alt, onv = None, 0
-        ops.append({"kind": kind, "at": (step[0], now[0]), "onv": onv, "ord": [], "alt": alt, "c": now[0], "eng": eng, "fn": fn, "rd": list(rd), "wr": list(wr), "bk": list(banks),
-                    "cost": cost * (1.25 if eng == "g" and sem is None else 1.0) + (SFIX[0] + SFIX[1] * cost if eng == "s" and sem is None else 0.0), "lat": lat, "sem": sem, "hop": HOP})
+        ops.append({"onv": onv, "ord": [], "alt": alt, "c": now[0], "eng": eng, "fn": fn, "rd": list(rd), "wr": list(wr), "bk": list(banks),
+                    "cost": cost * (1.25 if eng == "g" and sem is None else 1.0) + (SFIX if eng == "s" and sem is None else 0.0), "lat": lat, "sem": sem, "hop": HOP})
 
     def vc(k, f=1.0):
         return max(64.0, k * f) * CY + FIX
+
+    def gat(k):
+        return 60.0 + k * GA * CY
 
     def ts(out, in0, s1, s2, o0, o1, rd, wr, k, f=1.0, banks=()):
         if o1 is None:
@@ -128,11 +90,11 @@ def build(g, core, T, topo, par=None):
         else:
             op("v", lambda: v.tensor_scalar(out, in0, s1, s2, o0, o1), rd, wr, vc(k, f), banks)
 
-    def tt(out, in0, in1, o, rd, wr, k, f=2.0, banks=()):
-        op("v", lambda: v.tensor_tensor(out, in0, in1, o), rd, wr, vc(k, f), banks)
+    def tt(out, in0, in1, o, rd, wr, cost):
+        op("v", lambda: v.tensor_tensor(out, in0, in1, o), rd, wr, cost)
 
-    def cp(out, in_, rd, wr, k, f=1.0, banks=()):
-        op("v", lambda: v.tensor_copy(out, in_), rd, wr, vc(k, f), banks)
+    def cp(out, in_, rd, wr, cost, banks=()):
+        op("v", lambda: v.tensor_copy(out, in_), rd, wr, cost, banks)
 
     def ms(ap, val, wr, k, f=1.0):
         op("v", lambda: v.memset(ap, val), [], wr, vc(k, f))
@@ -140,8 +102,8 @@ def build(g, core, T, topo, par=None):
     def scan(out, d0, d1, o0, o1, rd, wr, k, f=1.0, banks=()):
         op("v", lambda: v.tensor_tensor_scan(out, d0, d1, 0.0, o0, o1), rd, wr, vc(k, f), banks)
 
-    def act(out, in_, fn, rd, wr, cost, banks=()):
-        op("s", lambda: s.activation(out, in_, fn), rd, wr, cost, banks)
+    def act(out, in_, fn, rd, wr, cost, banks=(), bias=0.0, acc=None):
+        op("s", lambda: s.activation(out, in_, fn, bias=bias, accum_out=acc), rd, wr, cost, banks)
 
     def either(onv, out, in_, rd, wr, cost_s, cost_v, add=None, banks=(), mul=None):
         if mul is not None:
@@ -156,9 +118,6 @@ def build(g, core, T, topo, par=None):
     def mm(out, lhs, rhs, st, sp, rd, bank, k, f=1.0):
         op("p", lambda: p.matmul(out, lhs, rhs, st, sp), rd, [bank], max(64.0, k) * f * PCY)
 
-    def mid(out, lhs, rhs, rd, bank, k):
-        op("p", lambda: p.matmul(out, lhs, rhs, False, False), rd, [], max(64.0, k) * PCY, [bank])
-
     def mms(calls, rd, wr, banks, k):
         op("p", lambda: [p.matmul(*x) for x in calls][-1], rd, wr, len(calls) * max(64.0, k) * PCY, banks)
 
@@ -171,11 +130,6 @@ def build(g, core, T, topo, par=None):
     def sel(out, in_, pat, o, fill, base, cm, rd, wr, k):
         op("g", lambda: g.affine_select(out, in_, pat, o, fill, base, cm), rd, wr, 170.0 + 2 * k * CY)
 
-    def pool_copy(out, in_, rd, wr, k):
-        sel(out, in_, [[0, k]], ALU.is_ge, 0.0, 0, 0, rd, wr, k)
-
-    nd = [0]
-
     def flight(q, fn, rd, wr, cost, lat, busy, sem):
         op(q, fn, rd, wr, cost, lat=lat, sem=sem)
         op("d", None, rd, wr, busy, sem=sem)
@@ -186,16 +140,13 @@ def build(g, core, T, topo, par=None):
         e = y if q == "y" else s
         flight(q, lambda: e.dma_start(out, in_), rd, wr, 60.0, DL, 240.0 + nbytes / RATE, (sem, 16))
 
-    def gat(k):
-        return 60.0 + k * GA * CY
-
     dma("s", T.wi[:, 0:1], T.w[:], [], ["wi"], 512)
-    dma("y", T.h0[:, 16:16 + W0], T.heard[:, 0:W0], [], ["h0_0"], 256 * W0)
-    dma("s", T.ai[:, 0:W0], T.scroll[:, 0:W0], [], ["ai_0"], 512 * W0)
+    dma("y", T.h0[:, 0:CW], T.heard[:, 0:CW], [], ["h0_0"], 256 * CW)
+    dma("s", T.ai[:, 0:CW], T.scroll[:, 0:CW], [], ["ai_0"], 512 * CW)
     dma("y", T.tab[:, 2048:4104], T.cues[:, 2040:4096], [], ["tab1"], 1 << 19)
     dma("y", T.tab[:, 4104:6160], T.cues[:, 0:2056], [], ["tab0"], 1 << 19)
-    dma("y", T.h0[:, 16 + W0:16 + C], T.heard[:, W0:C], [], ["h0_%d" % c for c in range(1, NCH)], 256 * (C - W0))
-    dma("y", T.ai[:, W0:C], T.scroll[:, W0:C], [], ["ai_%d" % c for c in range(1, NCH)], 512 * (C - W0))
+    dma("y", T.h0[:, CW:C], T.heard[:, CW:C], [], ["h0_1"], 256 * CW)
+    dma("y", T.ai[:, CW:C], T.scroll[:, CW:C], [], ["ai_1"], 512 * CW)
     dma("y", T.thi[:, 0:1], T.th[:], [], ["thi"], 512)
     dma("y", T.tab[:, 6160:8200], T.cues[:, 2056:4096], [], ["tab2"], 1 << 19)
     dma("y", T.book[:, 0:2048], T.spare[:], [], ["spare"], 1 << 20)
@@ -212,87 +163,70 @@ def build(g, core, T, topo, par=None):
     io(T.jd[:], [[0, 8], [1, 8], [0, 2]], 0, 0, ["jd"], 128)
     io(T.jb[:, 0:8], [[17, 8]], 15, 0, ["jb"], 8)
     io(T.tk[:], [[1, 16], [-1, 16]], 0, 0, ["tk"], 256)
-    io(T.loc[:, 0:32], [[1024, 2], [16, 16]], 16 - 1024, 1, ["loc"], 32)
+    io(T.loc[:], [[16, 32]], 16, 1, ["loc"], 32)
     io(T.jg[:], [[1, 8], [0, 17]], 0, 0, ["jg"], KW)
     io(T.jx[:], [[16, 8], [1, 17]], 0, 0, ["jx"], KW)
     sel(T.jm[:], T.jg[:], [[0, 8], [-1, 17]], ALU.is_ge, -1.0, 15 - NA, 0, ["jg"], ["jm"], KW)
     col = lambda j: T.col[:, j:j + 1]
-    PF, LANE, GRP, P7, P8, P1, WF, L15, G16, PAR8, _, L17 = range(12)
-    cp(col(PF), T.pi[:, 0:1], ["pi"], ["pf"], 1)
+    PF, LANE, GRP, P7, P8, P1, WF, L15, G16, PAR8, THF, L17, PARW = range(13)
+    cp(col(PF), T.pi[:, 0:1], ["pi"], ["pf"], vc(1))
     for j, (o, k) in enumerate(((ALU.bitwise_and, 15), (ALU.arith_shift_right, 4), (ALU.bitwise_and, 7), (ALU.arith_shift_right, 3), (ALU.bitwise_and, 1))):
         ts(T.pj[:, j:j + 1], T.pi[:, 0:1], k, None, o, None, ["pi"], ["pj%d" % j], 1)
-    cp(T.col[:, 1:3], T.pj[:, 0:2], ["pj0", "pj1"], ["col"], 2)
-    cp(T.col[:, 3:6], T.pj[:, 2:5], ["pj2", "pj3", "pj4"], ["col2"], 3)
-    cp(col(WF), T.wi[:, 0:1], ["wi"], ["wf"], 1)
+    cp(T.col[:, 1:3], T.pj[:, 0:2], ["pj0", "pj1"], ["col"], vc(2))
+    cp(T.col[:, 3:6], T.pj[:, 2:5], ["pj2", "pj3", "pj4"], ["col2"], vc(3))
+    cp(col(WF), T.wi[:, 0:1], ["wi"], ["wf"], vc(1))
     ts(T.wblk[:], T.jh[:], col(GRP), col(WF), ALU.is_equal, ALU.mult, ["jh", "col", "wf"], ["wblk"], 128, 0.5)
     either(1, T.wneg[:], T.wblk[:], ["wblk"], ["wneg"], vc(128), vc(64), mul=-1.0)
     ts(T.ih[:], T.jj[:], col(PF), None, ALU.is_equal, None, ["jj", "pf"], ["ih"], 128, 0.5)
-    for name, k in (("ihn", -1.0), ("ib", 1.0), ("i16", -16.0), ("ibig", 2.0 ** 15), ("ibn", -2.0 ** 15)):
+    for name, k in (("ihn", -1.0), ("ib", 1.0), ("i16", -16.0), ("ibig", 2.0 ** 15), ("ibn", -2.0 ** 15), ("ineg", -1.0)):
         ts(T[name][:], T.jj[:], col(PF), k, ALU.is_equal, ALU.mult, ["jj", "pf"], [name], 128, 0.5)
     ms(T.bigc[:], 1.5 * 2.0 ** 20, ["bigc"], 128, 0.5)
     for c in range(NCH):
-        cp(T.a0[:, 2 * C0[c] + 1:2 * C0[c + 1]:2], T.ai[:, C0[c]:C0[c + 1]], ["ai_%d" % c], ["a0_%d" % c], WIDTHS[c])
+        cp(T.a0[:, 2 * c * CW + 1:2 * (c + 1) * CW:2], T.ai[:, c * CW:(c + 1) * CW], ["ai_%d" % c], ["a0_%d" % c], vc(CW))
     io(T.mk[:, 0::2], [[0, C]], 0, 0, ["mkz"], C)
-    either(ONV["k"], T.wc[:, 0:8], T.wblk[:, 0::16], ["wblk"], ["wc0"], vc(8), vc(8), mul=-65536.0)
-    either(ONV["k"], T.wc[:, 8:16], T.wblk[:, 0::16], ["wblk"], ["wc1"], vc(8), vc(8), mul=65536.0)
+    either(0, T.wc[:, 0:8], T.wblk[:, 0::16], ["wblk"], ["wc0"], vc(8), vc(8), mul=-65536.0)
+    either(0, T.wc[:, 8:16], T.wblk[:, 0::16], ["wblk"], ["wc1"], vc(8), vc(8), mul=65536.0)
     ts(T.wc[:, 16:24], T.jj[:, 0:8], col(GRP), 128.0, ALU.is_equal, ALU.mult, ["jj", "col"], ["wc2"], 8)
     ts(col(L15), col(LANE), -15.0, 1.0 / 16.0, ALU.add, ALU.mult, ["col"], ["l15"], 1)
+    ts(col(L17), col(L15), 17.0, None, ALU.mult, None, ["l15"], ["l17"], 1)
     ts(col(G16), col(GRP), -16.0, None, ALU.mult, None, ["col"], ["g16"], 1)
     ts(col(PAR8), col(P1), 8.0, None, ALU.mult, None, ["col2"], ["par8"], 1)
-    ts(col(12), col(P1), 2.0 * KW, None, ALU.mult, None, ["col2"], ["parw"], 1)
+    ts(col(PARW), col(P1), 2.0 * KW, None, ALU.mult, None, ["col2"], ["parw"], 1)
     ts(T.thn[:, 0:1], T.thi[:, 0:1], -2.0, 1023.0, ALU.mult, ALU.add, ["thi"], ["thn"], 1)
-    cp(T.col[:, 10:11], T.thn[:, 0:1], ["thn"], ["thf"], 1)
+    cp(col(THF), T.thn[:, 0:1], ["thn"], ["thf"], vc(1))
     DX = ["dx0", "dx1"]
     for f, k in enumerate((2.0 ** 20, 2.0 ** 11)):
         ts(T.hb[:, KW * f:KW * f + KW], T.jm[:], col(GRP), k, ALU.is_equal, ALU.mult, ["jm", "col"], ["hb%d" % f], KW, 0.5)
         ts(T.dx[:, 8 * f:8 * f + 8], T.jj[:, 0:8], col(GRP), k, ALU.is_equal, ALU.mult, ["jj", "col"], ["dx%d" % f], 8)
-    either(ONV["k"], T.dx[:, 16:32], T.dx[:, 0:16], DX, ["dmx"], vc(16), vc(16), mul=-2.0)
-    ts(T.ineg[:], T.jj[:], col(PF), -1.0, ALU.is_equal, ALU.mult, ["jj", "pf"], ["ineg"], 128, 0.5)
+    either(0, T.dx[:, 16:32], T.dx[:, 0:16], DX, ["dmx"], vc(16), vc(16), mul=-2.0)
     ts(T.eq[:], T.jg[:], col(GRP), -128.0, ALU.is_equal, ALU.mult, ["jg", "col"], ["eq"], KW, 0.5)
     sel(T.rs[:, KW:2 * KW], T.eq[:], [[16, 8], [1, 17]], ALU.not_equal, 15.0 * 128.0, 0, -1, ["eq"], ["rs1"], KW)
-    either(ONV["k"], T.rs[:, 0:KW], T.rs[:, KW:2 * KW], ["rs1"], ["rs0"], vc(KW), vc(KW, 0.5), mul=16.0)
+    either(0, T.rs[:, 0:KW], T.rs[:, KW:2 * KW], ["rs1"], ["rs0"], vc(KW), vc(KW, 0.5), mul=16.0)
     ts(T.iha[:], T.jx[:], col(PF), 0.0625, ALU.is_equal, ALU.mult, ["jx", "pf"], ["iha"], KW, 0.5)
-    ts(col(L17), col(L15), 17.0, None, ALU.mult, None, ["l15"], ["l17"], 1)
     for f, (j, x) in enumerate(((L17, "l17"), (L15, "l15"))):
         ts(T.ck[:, KW * f:KW * f + KW], T.iha[:], col(j), -30.0 / 256.0, ALU.mult, ALU.add, ["iha", x], ["ck%d" % f], KW, 0.5)
     ms(T.bn[:], 1.5 * 2.0 ** 38, ["bn"], KW, 0.5)
-    ts(T.cep[:], T.iha[:], T.col[:, 10:11], 256.0, ALU.mult, ALU.mult, ["iha", "thf"], ["cep"], KW, 0.5)
+    ts(T.cep[:], T.iha[:], col(THF), 256.0, ALU.mult, ALU.mult, ["iha", "thf"], ["cep"], KW, 0.5)
     ms(T.o15[:], 2.0 ** 15, ["o15"], 128, 0.5)
     io(T.onp[:], [[0, 128]], 1, 0, ["onp"], 128)
     io(T.onn[:], [[0, 128]], -1, 0, ["onn"], 128)
     ms(T.rst0[:], -1.0e9, ["rst_0"], 4 * KW)
-    for c in range(1, NCH):
-        either(ONV["k"], T["rst%d" % c][:], T.rst0[:], ["rst_0"], ["rst_%d" % c], vc(4 * KW), vc(4 * KW))
+    either(0, T.rst1[:], T.rst0[:], ["rst_0"], ["rst_1"], vc(4 * KW), vc(4 * KW))
     ts(T.dm[:], T.jd[:], col(P7), None, ALU.is_equal, None, ["jd", "col2"], ["dm"], 128, 0.5)
-    ts(T.bl[:, 0:8], T.jb[:, 0:8], col(12), None, ALU.add, None, ["jb", "parw"], ["bl0"], 8)
+    ts(T.bl[:, 0:8], T.jb[:, 0:8], col(PARW), None, ALU.add, None, ["jb", "parw"], ["bl0"], 8)
     ts(T.bl[:, 8:16], T.jj[:, 0:8], col(PAR8), None, ALU.add, None, ["jj", "par8"], ["bl8"], 8)
-    ts(T.bs[:, 0:64], T.jl[:, 0:64], col(P8), -16.0, ALU.is_equal, ALU.mult, ["jl", "col2"], ["bs0"], 64)
-    ms(T.bs[:, 32:48], 0.0, ["bs0"], 16)
-    either(ONV["k"], T.bs[:, 64:128], T.bs[:, 0:64], ["bs0"], ["bs1"], vc(64), vc(64), mul=-1.0)
-    for at, k, x in ((128, 32, -2.0 ** -21), (160, 16, -2.0 ** -22), (176, 16, 0.0), (192, 16, 2.0 ** -11), (208, 16, -2.0 ** -20), (224, 16, -2.0 ** -11)):
-        either(ONV["k"], T.bs[:, at:at + k], T.bs[:, 0:k], ["bs0"], ["bs%d" % at], vc(k), vc(k), mul=x)
-    for at, k, e, name in ((0, 144, 19, "czb0"), (32, 16, 18, "czb0"), (64, 16, 17, "czb0"), (144, 16, 17, "czb144"), (160, 48, 8, "czb144"),
-                           (208, 32, 36, "czb208"), (240, 16, 13, "czb224")):
-        ms(T.czb[:, at:at + k], 1.5 * 2.0 ** e, [name] + (["czb80"] if at == 0 else []), k, 0.5)
-    ms(T.czb[:, 112:128], 0.0, ["czb80"], 16)
-    for at, k, x, name in ((0, 64, 0.0, "czh0"), (64, 16, 128.0, "czh0"), (80, 64, 1023.5, "czh80"), (112, 16, 0.0, "czh80"), (144, 16, 32.0, "czh80"),
-                           (160, 32, 32768.0, "czh160"), (192, 16, -15.0, "czh176")):
-        ms(T.czh[:, at:at + k], x, [name], k, 0.5)
-    for c in range(NCH):
-        z = 80 * c
-        for at, x in ((0, -255.5), (32, 7.75), (48, -2047.0 / 4096.0)):
-            ms(T.czc[:, z + at:z + at + 16], x, ["czc%d" % (z + at)], 16)
-        for j in range(2):
-            at = z + 16 + 48 * j
-            ts(T.czc[:, at:at + 16], T.loc[:, 16 * j:16 * j + 16], col(G16), float(C0[c]), ALU.add, ALU.add, ["loc", "g16"], ["czc%d" % at], 16)
+    ts(T.bs[:, 0:48], T.jl[:, 0:48], col(P8), -16.0, ALU.is_equal, ALU.mult, ["jl", "col2"], ["bs0"], 48)
+    for at, k, x in ((48, 48, -1.0), (96, 32, -2.0 ** -21), (128, 16, 0.0), (144, 16, 2.0 ** -11), (160, 16, -2.0 ** -20), (176, 16, -2.0 ** -11)):
+        either(0, T.bs[:, at:at + k], T.bs[:, 0:k], ["bs0"], ["bs%d" % at], vc(k), vc(k), mul=x)
+    for at, k, e in ((0, 48, 19), (48, 32, 17), (80, 32, 8), (112, 32, 36), (144, 16, 13)):
+        ms(T.czb[:, at:at + k], 1.5 * 2.0 ** e, ["czb%d" % at], k, 0.5)
+    for at, k, x in ((0, 48, 0.0), (48, 16, 128.0), (64, 48, 1023.5), (112, 16, 32.0), (128, 16, -255.5), (144, 16, 7.75), (160, 16, -2047.0 / 4096.0),
+                     (176, 32, 32768.0), (208, 16, -15.0)):
+        ms(T.czh[:, at:at + k], x, ["czh%d" % at], k, 0.5)
+    ts(T.czc[:], T.loc[:], col(G16), None, ALU.add, None, ["loc", "g16"], ["czc"], 32)
     ms(T.hr[:], 0.0, ["hr%d_%d" % (c, b) for c in range(NCH) for b in range(2)], 768, 0.5)
-    ms(T.h0[:, 0:16], 0.0, ["hzero0"], 16)
-    for t in range(1, STEPS):
-        io(T["h%d" % t][:, 0:16], [[0, 16]], 0, 0, ["hzero%d" % t], 16)
-    ms(T.xg0[:, 32::3], 0.0, ["xr0"], 8 * W0, 0.5)
-    for c in range(1, NCH):
-        k = 8 * WIDTHS[c]
-        either(0, T["xg%d" % c][:, 32::3], T.xg0[:, 32:32 + 3 * k:3], ["xr0"], ["xr%d" % c], vc(k), vc(k, 0.5))
+    ms(T.xg0[:, 32::3], 0.0, ["xr0"], 8 * CW, 0.5)
+    either(0, T.xg1[:, 32::3], T.xg0[:, 32::3], ["xr0"], ["xr1"], vc(8 * CW), vc(8 * CW, 0.5))
     ms(T.ut[:, 0:16], 0.0, ["ut1"], 16)
     ms(T.ut[:, 16:40], 1.0, ["ut2"], 24)
     ts(T.lt[:], T.jl[:], col(LANE), None, ALU.is_lt, None, ["jl", "col"], ["lt"], 256, 0.5)
@@ -304,29 +238,23 @@ def build(g, core, T, topo, par=None):
     ts(T.st[:, 33:289], T.jl[:], col(LANE), None, ALU.is_ge, None, ["jl", "col", "st2"], ["st0"], 256, 0.5)
     ms(T.st[:, 48:289:16], 0.0, ["st0"], 16)
     for e in range(2):
-        pool_copy(T.tab[:, e:2048:2], T.tab[:, 4105 - e:6152:2], ["tab0"], ["sw%d" % e], 1024)
-    gap = ["gap"]
+        either(e, T.tab[:, e:2048:2], T.tab[:, 4105 - e:6152:2], ["tab0"], ["sw%d" % e], vc(1024), vc(512), -64.0)
 
-    notes, ny = [], [0]
     KB, UB = T.kb, T.ub
     for t in range(STEPS):
         last = t == STEPS - 1
-        H, A = T["h%d" % t], T["a%d" % t]
+        H, A, AN = T["h%d" % t], T["a%d" % t], T["a%d" % (t + 1)]
         dst = cores[(rank + 1 + t % (n - 1)) % n]
         src = cores[(rank - 1 - t % (n - 1)) % n]
         for c in range(NCH):
-            now[0], step[0] = c, t
-            c0, CW = C0[c], WIDTHS[c]
-            M, NC = CW // 2, CW // 16
+            now[0] = c
+            c0 = c * CW
             cs = slice(c0, c0 + CW)
-            h0 = 16 + c0
-            hs = slice(h0, h0 + CW)
-            hh, a = "h%d_%d" % (t, c), "a%d_%d" % (t, c)
-            X, MX, SO, RST = T["xg%d" % c], T["mx%d" % c], T["so%d" % c], T["rst%d" % c]
-            KM = T.km[:, 16 * c:16 * c + 16]
+            hh, a, an = "h%d_%d" % (t, c), "a%d_%d" % (t, c), "a%d_%d" % (t + 1, c)
+            X, MX, SO, RST, KM = T["xg%d" % c], T["mx%d" % c], T["so%d" % c], T["rst%d" % c], T.km[:, 16 * c:16 * c + 16]
             r = lambda name: "%s_%d" % (name, c)
-            par2 = lambda buf, at, b: buf[:, at + b:at + CW:2]
-            odd = slice(2 * c0 + 1, 2 * c0 + 2 * CW, 2)
+            par2 = lambda buf, b: buf[:, c0 + b:c0 + CW:2]
+            even, odd, both = slice(2 * c0, 2 * c0 + 2 * CW, 2), slice(2 * c0 + 1, 2 * c0 + 2 * CW, 2), slice(2 * c0, 2 * c0 + 2 * CW)
             AB = lambda b: A[:, 2 * c0 + 1 + 2 * b:2 * c0 + 2 * CW:4]
             r0 = 3 * c0 // 2
             HR = lambda b: T.hr[:, r0 + b:r0 + 3 * M:3]
@@ -336,174 +264,155 @@ def build(g, core, T, topo, par=None):
                 O = T[of][:, 0:M]
                 if t == 0:
                     mm(O, T.ihn[:], AB(b), True, False, ["ihn", a], of, M)
-                    mm(O, T.wneg[:], par2(H, h0, b), False, False, ["wneg", hh], of, M)
-                    mm(O, T.ibig[:], T.bigc[:, 0:M], False, False, ["ibig", "bigc"], of, M)
+                    mm(O, T.wneg[:], par2(H, b), False, False, ["wneg", hh], of, M)
+                    mm(O, T.ibig[:], T.bigc[:], False, False, ["ibig", "bigc"], of, M)
                 else:
-                    mm(O, T.ibig[:], T.bigc[:, 0:M], True, False, ["ibig", "bigc"], of, M)
-                    mm(O, T.wneg[:], par2(H, h0, b), False, False, ["wneg", hh], of, M)
-                mm(O, T.ibn[:], T.bigc[:, 0:M], False, False, ["ibn", "bigc"], of, M)
-                mm(O, T.wblk[:], par2(H, h0, b), False, False, ["wblk", hh], of, M)
+                    mm(O, T.ibig[:], T.bigc[:], True, False, ["ibig", "bigc"], of, M)
+                    mm(O, T.wneg[:], par2(H, b), False, False, ["wneg", hh], of, M)
+                mm(O, T.ibn[:], T.bigc[:], False, False, ["ibn", "bigc"], of, M)
+                mm(O, T.wblk[:], par2(H, b), False, False, ["wblk", hh], of, M)
                 mm(O, T.ih[:], AB(b), False, True, ["ih", a], of, M)
                 ts(T.off[:, c0 + M * b:c0 + M * b + M], O, 2056.0, None, ALU.add, None, [], [r("off%d" % b)], M, 1.0, [of])
-            for b in range(2):
-                either(ONV["hr"], HR(b), par2(H, h0, b), [hh], [hr[b]], vc(M), vc(M, 0.5), 32.0 if b else None)
-            CP = T.of1[0:M, 128:160]
-            half = lambda b: T.of1[0:M, 128 + 16 * b:136 + 16 * b]
-            calls = [(CP, T.ih[:, 0:M], T.czh[:, 160:192], True, False)] + [(half(b), par2(H, h0, b), T.wc[:, 0:8], False, False) for b in range(2)]
-            calls += [(CP, T.ibig[:, 0:M], T.czb[:, 208:240], False, False), (CP, T.ibn[:, 0:M], T.czb[:, 208:240], False, False)]
-            calls += [(half(b), par2(H, h0, b), T.wc[:, 8:16], False, b == 1 and t == 0) for b in range(2)]
+            if HRG:
+                sel(HR(0), par2(H, 0), [[0, M]], ALU.is_ge, 0.0, 0, 0, [hh], [hr[0]], M)
+            else:
+                either(0, HR(0), par2(H, 0), [hh], [hr[0]], vc(M), vc(M, 0.5))
+            either(0, HR(1), par2(H, 1), [hh], [hr[1]], vc(M), vc(M, 0.5), 32.0)
+            CP = T.of1[:, 128:160]
+            half = lambda b: T.of1[:, 128 + 16 * b:136 + 16 * b]
+            calls = [(CP, T.ih[:], T.czh[:, 176:208], True, False)] + [(half(b), par2(H, b), T.wc[:, 0:8], False, False) for b in range(2)]
+            calls += [(CP, L[:], T.czb[:, 112:144], False, False) for L in (T.ibig, T.ibn)]
+            calls += [(half(b), par2(H, b), T.wc[:, 8:16], False, b == 1 and t == 0) for b in range(2)]
             if t > 0:
-                calls += [(half(b), par2(T.sg, c0, b), T.wc[:, 16:24], False, b == 1) for b in range(2)]
-            mms(calls, ["ih", "czh160", hh, "wc0", "wc1", "wc2", "ibig", "ibn", "czb208"] + ([r("sg")] if t else []), ["of1"], [], 16)
-            either(ONV["cap"], RST[0:M, 0::17], CP, [], [r("rst")], vc(16), vc(16), 2.0 ** 28 - 4032.0, ["of1"])
+                calls += [(half(b), par2(T.sg, b), T.wc[:, 16:24], False, b == 1) for b in range(2)]
+            mms(calls, ["ih", "czh176", hh, "wc0", "wc1", "wc2", "ibig", "ibn", "czb112"] + ([r("sg")] if t else []), ["of1"], [], 16)
+            either(0, RST[:, 0::17], CP, [], [r("rst")], vc(16), vc(16), 2.0 ** 28 - 4032.0, ["of1"])
             xs = [[], []]
-            mxs = [[] for i in range(16)]
+            mxs = [[] for i in range(16 - NA)]
+            abs_ = []
             wide = 4112 if t == 0 else 6152
-            for e in range(len(MARKS) - 1):
-                u0, u1 = 2 * round(MARKS[e] * M / 2), 2 * round(MARKS[e + 1] * M / 2)
-                cut = []
-                calls = cuts(u0, u1, GPC)
-                for w0, w1 in zip(calls, calls[1:]):
-                    for b in range(2):
-                        x = "x%d_%d_%d" % (c, b, w0)
-                        onv = len(xs[0]) + len(xs[1]) in VG.get((t, c), VG[None])
-                        xs[b].append(x)
-                        cut.append(x)
+            j0 = 16 - NA
+            marks, gpc = (SHORT, 1) if (t, c) in ALONE else (MARKS, GPC)
+            for e in range(len(marks) - 1):
+                u0, u1 = marks[e], marks[e + 1]
+                cut = [[], []]
+                for b in range(2):
+                    for w in range(gpc):
+                        w0, w1 = u0 + (u1 - u0) * w // gpc, u0 + (u1 - u0) * (w + 1) // gpc
+                        cut[b].append("x%d_%d_%d" % (c, b, w0))
                         k = (w1 - w0) * 16
-                        either(onv, X[:, 16 * b + 48 * w0:16 * b + 48 * w1:3], T.tab[:, 2048:2048 + wide].indirect(T.off[:, c0 + M * b + w0:c0 + M * b + w1]),
-                               ["tab0", "tab1", r("off%d" % b)] + (["tab2"] if t else []), [x], gat(k), gat(k), 32.0 if b else None)
-                for i in range(16 - NA):
+                        either(b if (t, c) in ALONE else t + c + e == 0 and w == 1, X[:, 16 * b + 48 * w0:16 * b + 48 * w1:3], T.tab[:, 2048:2048 + wide].indirect(T.off[:, c0 + M * b + w0:c0 + M * b + w1]),
+                               ["tab0", "tab1", r("off%d" % b)] + (["tab2"] if t else []), cut[b][-1:], gat(k), gat(k), 32.0 if b else None)
+                    xs[b] += cut[b]
+                for i in range(j0):
                     mxs[i].append("mx%d_%d_%d" % (c, i, e))
                     k = 3 * (u1 - u0)
                     scan(MX[:, 3 * M * i + 3 * u0:3 * M * i + 3 * u1], X[:, 3 * i + 48 * u0:3 * i + 48 * u0 + 16 * k - 15:16], T.hr[:, r0 + 3 * u0:r0 + 3 * u1],
-                         ALU.max, ALU.min, cut + ["xr%d" % c] + hr, [mxs[i][e]], k, 0.5)
-                for j0 in range(16 - NA, 16, YB):
-                    nj = min(16, j0 + YB) - j0
-                    yb = ("yb", "xb")[ny[0] % 2]
-                    ny[0] += 1
-                    k = (u1 - u0) * 2 * nj
-                    for b in range(2):
-                        calls = []
-                        for j in range(nj):
-                            o_ = T[yb][:, b * nj + j:k:2 * nj]
-                            x0 = 16 * b + 3 * (j0 + j)
-                            calls.append((o_, T.ineg[:], T.hr[:, r0 + b + 3 * u0:r0 + 3 * u1:3], True, False))
-                            calls.append((o_, T.ib[:], X[:, x0 + 48 * u0:x0 + 48 * u1 - 47:48], False, True))
-                        mms(calls, ["ineg", "ib", hr[b]] + [x for x in cut if x in xs[b]], [yb], [], u1 - u0)
-                    m0 = 3 * M * j0 + 2 * nj * u0
-                    mxr = "ab%d_%d_%d" % (c, j0, e)
-                    act(MX[:, m0:m0 + k], T[yb][:, 0:k], ACT.Abs, [], [mxr], vc(k), [yb])
-                    for j in range(nj):
-                        mxs[j0 + j].append(mxr)
+                         ALU.max, ALU.min, cut[0] + cut[1] + ["xr%d" % c] + hr, [mxs[i][e]], k, 0.5)
+                yb = ("yb", "xb")[e % 2]
+                k = (u1 - u0) * 2 * NA
+                for b in range(2):
+                    calls = []
+                    for j in range(NA):
+                        o_ = T[yb][:, b * NA + j:k:2 * NA]
+                        x0 = 16 * b + 3 * (j0 + j)
+                        calls.append((o_, T.ineg[:], T.hr[:, r0 + b + 3 * u0:r0 + 3 * u1:3], True, False))
+                        calls.append((o_, T.ib[:], X[:, x0 + 48 * u0:x0 + 48 * u1 - 47:48], False, True))
+                    mms(calls, ["ineg", "ib", hr[b]] + cut[b], [yb], [], u1 - u0)
+                m0 = 3 * M * j0 + 2 * NA * u0
+                abs_.append("ab%d_%d" % (c, e))
+                act(MX[:, m0:m0 + k], T[yb][:, 0:k], ACT.Abs, [], abs_[-1:], vc(k), [yb])
             for b in range(2):
                 ep = "ep%d" % b
                 EP = T[ep]
-                E, EN, EF = EP[0:M, 0:2 * KW], EP[0:M, 0:KW], EP[0:M, KW:2 * KW]
-                EI = lambda i: EP[0:M, i:2 * KW:17]
+                E, EN, EF = EP[:, 0:2 * KW], EP[:, 0:KW], EP[:, KW:2 * KW]
+                EI = lambda i: EP[:, i:2 * KW:17]
                 XP = lambda i: X[:, 16 * b + 3 * i:16 * b + 3 * i + 48 * M - 47:48]
                 mm(E, HR(b), T.hb[:], True, False, [hr[b], "hb0", "hb1"], ep, 2 * KW)
-                mid(EN, T.o15[:, 0:M], T.cep[:], ["o15", "cep"], ep, KW)
-                for i0 in range(0, 16 - NA, PG):
-                    mms([(EI(i), XP(i), T.dx[:, 0:16], False, False) for i in range(i0, min(16 - NA, i0 + PG))], xs[b] + DX, [], [ep], 16)
-                for i in range(16 - NA):
-                    mid(EI(i), MX[:, 3 * M * i + b:3 * M * (i + 1):3], T.dx[:, 16:32], mxs[i] + ["dmx"], ep, 16)
-                for j0 in range(16 - NA, 16, YB):
-                    nj = min(16, j0 + YB) - j0
-                    mms([(EI(j0 + j), MX[:, 3 * M * j0 + b * nj + j:3 * M * j0 + CW * nj:2 * nj], T.dx[:, 0:16], False, False) for j in range(nj)],
-                        mxs[j0] + DX, [], [ep], 16)
+                mms([(EN, T.o15[:], T.cep[:], False, False)], ["o15", "cep"], [], [ep], KW)
+                for i0 in range(0, j0, PG):
+                    mms([(EI(i), XP(i), T.dx[:, 0:16], False, False) for i in range(i0, min(j0, i0 + PG))], xs[b] + DX, [], [ep], 16)
+                for i in range(j0):
+                    mms([(EI(i), MX[:, 3 * M * i + b:3 * M * (i + 1):3], T.dx[:, 16:32], False, False)], mxs[i] + ["dmx"], [], [ep], 16)
+                mms([(EI(j0 + j), MX[:, 3 * M * j0 + b * NA + j:3 * M * j0 + CW * NA:2 * NA], T.dx[:, 0:16], False, False) for j in range(NA)], abs_ + DX, [], [ep], 16)
                 for f, O in ((1, EF), (0, EN)):
                     fs = slice(KW * f, KW * f + KW)
-                    calls = [(O, T.o15[:, 0:M], T.ck[:, fs], False, False)]
-                    if t > 0:
-                        calls.append((O, par2(T.sg, c0, b), T.rs[:, fs], False, False))
+                    calls = [(O, T.o15[:], T.ck[:, fs], False, False)] + ([(O, par2(T.sg, b), T.rs[:, fs], False, False)] if t else [])
                     rd = ["o15", "ck%d" % f] + ([r("sg"), "rs%d" % f] if t else [])
                     if f:
                         mms(calls, rd, [], [ep], KW)
                     else:
                         calls += [(EF, AB(b), T.iha[:], False, False), (EN, AB(b), T.iha[:], False, True)]
-                        mms([(O, L[:, 0:M], T.bn[:], False, False) for L in (T.ibig, T.ibn)] + calls, rd + ["ibig", "ibn", "bn", a, "iha"], [ep], [], KW)
+                        mms([(O, L[:], T.bn[:], False, False) for L in (T.ibig, T.ibn)] + calls, rd + ["ibig", "ibn", "bn", a, "iha"], [ep], [], KW)
                 s0 = 2 * KW * b
-                scan(SO[0:M, s0:s0 + 2 * KW], RST[0:M, s0:s0 + 2 * KW], E, ALU.max, ALU.min, [r("rst")], [r("so%d" % b)], 2 * KW, 1.0, [ep])
-                tt(T.km[0:M, 16 * c + 8 * b:16 * c + 8 * b + 8], SO[0:M, s0 + 15:s0 + KW:17], SO[0:M, s0 + KW + 15:s0 + 2 * KW:17], ALU.min, [r("so%d" % b)], [r("km%d" % b)], 8)
-                if last and notes and b:
-                    ops[-1]["ord"].append(notes[-1])
-            so = [r("so0"), r("so1")]
+                scan(SO[:, s0:s0 + 2 * KW], RST[:, s0:s0 + 2 * KW], E, ALU.max, ALU.min, [r("rst")], [r("so%d" % b)], 2 * KW, 1.0, [ep])
+                tt(T.km[:, 16 * c + 8 * b:16 * c + 8 * b + 8], SO[:, s0 + 15:s0 + KW:17], SO[:, s0 + KW + 15:s0 + 2 * KW:17], ALU.min, [r("so%d" % b)], [r("km%d" % b)], vc(16))
+            so, km = [r("so0"), r("so1")], [r("km0"), r("km1")]
             LA, LT = T.ll[:, 256 * c:256 * c + 128], T.ll[:, 256 * c + 128:256 * c + 256]
-            km = [r("km0"), r("km1")]
-            for o_, w_, at, rd, x in ((LA, SO[:], 0, so, "la"), (LT, KM, 8, km, "lt")):
-                op("v", lambda o_=o_, w_=w_, at=at: v.tensor_tensor(o_, w_.indirect(T.bl[:, at:at + 8]), T.dm[:], ALU.mult), rd + ["bl%d" % at, "dm"], [r(x)], gat(128))
-            z = 80 * c
+            tt(LA, SO[:].indirect(T.bl[:, 0:8]), T.dm[:], ALU.mult, so + ["bl0", "dm"], [r("la")], gat(128))
+            tt(LT, KM.indirect(T.bl[:, 8:16]), T.dm[:], ALU.mult, km + ["bl8", "dm"], [r("lt")], gat(128))
             lo = 16 if t == 0 else 0
             rnd = lambda k0, k1, at: [(KB[:, k0:k1], L[:], T.czb[:, at + k0:at + k1], False, False) for L in (T.ibig, T.ibn)]
-            mm(KB[:, 0:80], T.ih[:], T.czh[:, 0:80], True, False, ["ih", "czh0"], "kb", 80)
-            mm(KB[:, lo:80], LA, T.bs[:, 128 + lo:208], False, False, [r("la"), "bs128", "bs160", "bs176", "bs192"], "kb", 80, 4.0)
-            mms(rnd(0, 80, 0) + [(KB[:, 0:80], T.ih[:], T.czh[:, 80:160], False, False)], ["ibig", "ibn", "czb0", "ih", "czh80"], ["kb"], [], 80)
-            mm(KB[:, 0:64], LT, T.bs[:, 0:64], False, False, [r("lt"), "bs0"], "kb", 64, 4.0)
-            mms(rnd(0, 64, 80), ["ibig", "ibn", "czb80"], ["kb"], [], 64)
-            mm(KB[:, 48:80], LA, T.bs[:, 208:240], False, False, [r("la"), "bs208", "bs224"], "kb", 32, 4.0)
-            mm(KB[:, 0:64], LT, T.bs[:, 64:128], False, False, [r("lt"), "bs1"], "kb", 64, 4.0)
-            mms([(KB[:, 16:80], T.ih[:], T.czc[:, z:z + 64], False, False)] + rnd(16, 80, 128) + [(KB[:, 16:32], T.ih[:], T.czc[:, z + 64:z + 80], False, True)],
-                ["ih", "ibig", "ibn", "czb144"] + ["czc%d" % (z + 16 * j) for j in range(5)], ["kb"], [], 64)
-            lst = lambda i: T.lu[:, 96 * c + 16 * i:96 * c + 16 * i + NC]
-            cp(T.lu[:, 96 * c:96 * c + 80], KB[:, 0:80], [], [r("lu")], 80, 1.0, ["kb"])
-            lbk, lgw, lz, lsp, liu = lst(0), lst(1), lst(2), lst(3), lst(4)
-            rid, pid, _ = topo.addr(dst)
-            msk = 0
-            for e in topo.engines(core, dst)[:NE]:
-                msk |= 1 << e
-            got = len(topo.engines(src, core)[:NE])
-            either(ONV["hz"], T.hz[:, cs], H[:, 0:h0 + CW].indirect(lz), ["hzero%d" % t, r("lu")] + ["h%d_%d" % (t, e) for e in range(c + 1)], [r("hz")], gat(CW), gat(CW))
-            say = "say%d_%d" % (t, c)
-            tabs = ["tab0", "tab1", "tab2", "sw0", "sw1", r("lu")]
-            if YPE:
-                either(1 - ONV["hz"], T.yy[:, cs], T.tab[:, 0:8200].indirect(lsp), tabs, [r("yy")], gat(CW), gat(CW))
-                mm(KB[:, 256:256 + CW], T.ineg[:], T.hz[:, cs], True, False, ["ineg", r("hz")], "kb", CW)
-                mm(KB[:, 256:256 + CW], T.ib[:], T.yy[:, cs], False, True, ["ib", r("yy")], "kb", CW)
-                act(T["say%d" % t][:, cs], KB[:, 256:256 + CW], ACT.Abs, [], [say], vc(CW), ["kb"])
+            mm(KB[:, 0:64], T.ih[:], T.czh[:, 0:64], True, False, ["ih", "czh0", "czh48"], "kb", 64)
+            mm(KB[:, lo:64], LA, T.bs[:, 96 + lo:160], False, False, [r("la"), "bs96", "bs128", "bs144"], "kb", 64, 4.0)
+            mms(rnd(0, 64, 0) + [(KB[:, 0:64], T.ih[:], T.czh[:, 64:128], False, False)], ["ibig", "ibn", "czb0", "czb48", "ih", "czh64", "czh112"], ["kb"], [], 64)
+            mm(KB[:, 0:48], LT, T.bs[:, 0:48], False, False, [r("lt"), "bs0"], "kb", 64, 4.0)
+            mms(rnd(0, 48, 0), ["ibig", "ibn", "czb0"], ["kb"], [], 64)
+            mm(KB[:, 32:64], LA, T.bs[:, 160:192], False, False, [r("la"), "bs160", "bs176"], "kb", 32, 4.0)
+            mm(KB[:, 0:48], LT, T.bs[:, 48:96], False, False, [r("lt"), "bs48"], "kb", 64, 4.0)
+            mms([(KB[:, 16:64], T.ih[:], T.czh[:, 128:176], False, False)] + rnd(16, 64, 48) + [(KB[:, 16:32], T.ih[:], T.czc[:, 16 * c:16 * c + 16], False, True)],
+                ["ih", "ibig", "ibn", "czb48", "czb80", "czh128", "czh144", "czh160", "czc"], ["kb"], [], 64)
+            cp(T.lu[:, 64 * c:64 * c + 64], KB[:, 0:64], [], [r("lu")], vc(64), ["kb"])
+            lbk, lgw, lsp, liu = [T.lu[:, 64 * c + 16 * i:64 * c + 16 * i + 16] for i in range(4)]
+            UP, SAY, YY = T["up%d" % t][:, cs], T["say%d" % t][:, cs], T[YBANK][:, 256:256 + CW]
+            up, say, arr = "up%d_%d" % (t, c), "say%d_%d" % (t, c), "arr%d_%d" % (t, c)
+            cue, tabs = T.tab[:, 0:8200].indirect(lsp), ["tab0", "tab1", "tab2", "sw0", "sw1", r("lu")]
+            either((t, c) not in QUICK, UP, cue, tabs, [up], gat(CW), gat(CW), 64.0)
+            if (t, c) in QUICK:
+                tt(T.yy[:], cue, H[:, cs], ALU.subtract, tabs + [hh], ["yy"], gat(CW))
+                act(SAY, T.yy[:], ACT.Abs, ["yy"], [say], vc(CW))
             else:
-                op("v", lambda o_=T.yy[:, cs], l_=lsp, h_=T.hz[:, cs]: v.tensor_tensor(o_, T.tab[:, 0:8200].indirect(l_), h_, ALU.subtract),
-                   tabs + [r("hz")], [r("yy")], gat(CW))
-                act(T["say%d" % t][:, cs], T.yy[:, cs], ACT.Abs, [r("yy")], [say], vc(CW))
-            arr = "arr%d_%d" % (t, c)
-            flight("g", lambda o_=T["h%d" % (t + 1)][:, hs], i_=T["say%d" % t][:, cs], a_=arr, pid=pid, rid=rid, msk=msk:
-                   g.remote_dma(o_, i_, T.sem[a_], T.sem["sent"], pid, rid, msk),
-                   [say], ["h%d_%d" % (t + 1, c)], GI, RL + (FIRST if t + c == 0 else 0.0), RB, (arr, got, len(topo.engines(core, dst)[:NE])))
-            an, AN, both = "a%d_%d" % (t + 1, c), T["a%d" % (t + 1)], slice(2 * c0, 2 * c0 + 2 * CW)
-            op("v", lambda o_=A[:, 2 * c0:2 * c0 + 2 * CW:2], l_=lbk, a_=A[:, odd], w_=T.book[:, 0:2048 if t == 0 else 4096]: v.tensor_tensor(o_, w_.indirect(l_), a_, ALU.subtract),
-               [r("lu"), a, "spare"] + ([] if t == 0 else gap), [r("tt")], gat(CW))
-            either(ONV["mk"], T.mk[:, odd], T.ut[:, 0:289].indirect(liu), ["ut0", "ut1", "ut2", "mkz", r("lu")], [r("mk")], gat(CW), gat(CW))
+                mm(YY, T.ineg[:], H[:, cs], True, False, ["ineg", hh], YBANK, CW)
+                mm(YY, T.ib[:], UP, False, True, ["ib", up], YBANK, CW)
+                act(SAY, YY, ACT.Abs, [], [say], vc(CW), [YBANK], -64.0)
+            rid, pid, _ = topo.addr(dst)
+            use = topo.engines(core, dst)[:NE]
+            send = RemoteDMATransfer(dst_ids=[DstId(rid=rid, pnc=pid)], dma_engine_mask=sum(1 << e for e in use), remote_sem=T.sem[arr],
+                                     srcs=[SAY, UP], dsts=[T["h%d" % (t + 1)][:, cs]], alu_op=3)
+            flight("g", lambda x=send: g.remote_dma_fused([x], local_sem=T.sem["sent"]), [say, up], ["h%d_%d" % (t + 1, c)],
+                   GI, RL + (FIRST if t + c == 0 else 0.0), RB, (arr, len(topo.engines(src, core)[:NE]), len(use)))
+            tt(A[:, even], T.book[:, 0:2048 if t == 0 else 4096].indirect(lbk), A[:, odd], ALU.subtract, [r("lu"), "spare", a] + (["gap"] if t else []), [r("tt")], gat(CW))
+            either(0, T.mk[:, odd], T.ut[:, 0:289].indirect(liu), ["ut0", "ut1", "ut2", "mkz", r("lu")], [r("mk")], gat(CW), gat(CW))
             scan(AN[:, both], T.mk[:, both], A[:, both], ALU.mult, ALU.add, [r("mk"), r("tt"), a], [an], 2 * CW, 0.5)
             if last:
                 act(T.af[:, cs], AN[:, odd], ACT.Copy, [an], [r("af")], vc(CW) + 10.0)
                 dma("y", T.ys[:, cs], T.af[:, cs], [r("af")], [r("ys")], CW * 512)
-                dma("y", T.yh[:, cs], T["h%d" % STEPS][:, hs], ["h%d_%d" % (STEPS, c)], [r("yh")], CW * 256)
+                dma("y", T.yh[:, cs], T["h%d" % STEPS][:, cs], ["h%d_%d" % (STEPS, c)], [r("yh")], CW * 256)
                 G2 = T["g2%d" % c]
                 g2 = ["g2%d_%d" % (c, e) for e in range(4)]
-                op("v", lambda w_=G2[:], l_=lgw, a_=A[:, odd]: v.tensor_copy(w_.indirect(l_), a_), [r("lu"), a], g2, 60.0 + CW * SC * CY)
-                notes.append(len(ops) - 1)
+                cp(G2[:].indirect(lgw), A[:, odd], [r("lu"), a], g2, 60.0 + CW * SC * CY)
                 for e in range(4):
                     dma("y" if e % 2 == 0 or c < NCH - 1 else "s", T.yg[:, e * 512 + c0:e * 512 + c0 + CW], G2[:, 16 + e * 512 + c0:16 + e * 512 + c0 + CW],
                         [g2[e]], ["yg%d_%d" % (c, e)], CW * 512)
             else:
-                either(ONV["st"], T.sg[:, cs], T.st[:, 0:289].indirect(liu), ["st0", "st1", "st2", r("lu")], [r("sg")], gat(CW), gat(CW))
-                op("s", lambda i_=KM, o_=T.cnt[:, c:c + 1]: s.activation(T.mj[:], i_, ACT.Sign, bias=3839.0 * 128.0 + 1.0 / 32.0, accum_out=o_), km, ["mj", r("cnt")], vc(16) + 20.0)
+                either(0, T.sg[:, cs], T.st[:, 0:289].indirect(liu), ["st0", "st1", "st2", r("lu")], [r("sg")], gat(CW), gat(CW))
+                act(T.mj[:], KM, ACT.Sign, km, ["mj", r("cnt")], vc(16) + 20.0, (), 3839.0 * 128.0 + 1.0 / 32.0, T.cnt[:, c:c + 1])
         if not last:
             for c in range(NCH):
-                op("v", lambda l_=T.lu[:, 96 * c + 16:96 * c + 16 + WIDTHS[c] // 16], a_=A[:, 2 * C0[c] + 1:2 * C0[c + 1]:2]: v.tensor_copy(T.book[:, 2032:6144].indirect(l_), a_),
-                   ["lu_%d" % c, "a%d_%d" % (t, c)], gap + ["spare"], 60.0 + WIDTHS[c] * SC * CY)
-                notes.append(len(ops) - 1)
+                cp(T.book[:, 2032:6144].indirect(T.lu[:, 64 * c + 16:64 * c + 32]), A[:, 2 * c * CW + 1:2 * (c + 1) * CW:2],
+                   ["lu_%d" % c, "a%d_%d" % (t, c)], ["gap", "spare"], 60.0 + CW * SC * CY)
             if t == STEPS - 2:
                 for c in range(NCH):
                     for e in range(4):
-                        at, CW = e * 512 + C0[c], WIDTHS[c]
-                        pool_copy(T["g2%d" % c][:, 16 + at:16 + at + CW], T.book[:, 2048 + at:2048 + at + CW], gap, ["g2%d_%d" % (c, e)], CW)
+                        at = e * 512 + c * CW
+                        sel(T["g2%d" % c][:, 16 + at:16 + at + CW], T.book[:, 2048 + at:2048 + at + CW], [[0, CW]], ALU.is_ge, 0.0, 0, 0, ["gap"], ["g2%d_%d" % (c, e)], CW)
             MC = UB[:, 32:33]
-            mm(MC, T.ih[:], T.czh[:, 192:193], True, False, ["ih", "czh176"], "ub", 1)
-            for x, L in (("onn", T.onn), ("onp", T.onp)):
+            mm(MC, T.ih[:], T.czh[:, 208:209], True, False, ["ih", "czh208"], "ub", 1)
+            for x in ("onn", "onp"):
                 for c in range(NCH):
-                    mm(MC, L[:], T.cnt[:, c:c + 1], False, False, [x, "cnt_%d" % c], "ub", 1, 4.0)
+                    mm(MC, T[x][:], T.cnt[:, c:c + 1], False, False, [x, "cnt_%d" % c], "ub", 1, 4.0)
                 if x == "onn":
-                    mms([(MC, T.ibig[:], T.czb[:, 240:241], False, False), (MC, T.ibn[:], T.czb[:, 240:241], False, False)], ["ibig", "ibn", "czb224"], ["ub"], [], 1)
+                    mms([(MC, L[:], T.czb[:, 144:145], False, False) for L in (T.ibig, T.ibn)], ["ibig", "ibn", "czb144"], ["ub"], [], 1)
             mm(MC, T.ih[:], T.thn[:, 0:1], False, True, ["ih", "thn"], "ub", 1)
             ts(T.cep[:], T.iha[:], MC, 256.0, ALU.mult, ALU.mult, ["iha"], ["cep"], KW, 0.5, ["ub"])
     return ops
@@ -535,126 +444,27 @@ def depend(ops):
             rds[x] = []
 
 
-def place(ops, seq, before, tail, eng):
-    slots = {e: ([], []) for e in "vspgyd"}
-    m = len(ops)
-    t0, t1 = [0.0] * m, [0.0] * m
-    end = 0.0
-    near, far = ops[0]["hop"]
-    for i in seq:
-        o = ops[i]
-        rdy = tail[0][i]
-        e = eng[i]
-        for j, lag, wait in before[i]:
-            u = t1[j] + lag
-            if wait:
-                u += near if eng[j] == e else far
-            if u > rdy:
-                rdy = u
-        cost = o["cost"] if e == o["eng"] else o["alt"][1]
-        st, en = slots[e]
-        x, hi = 0, len(en)
-        while x < hi:
-            md = (x + hi) >> 1
-            if en[md] <= rdy:
-                x = md + 1
-            else:
-                hi = md
-        t = rdy
-        while x < len(st) and st[x] < t + cost - 1e-6:
-            t = max(t, en[x])
-            x += 1
-        st.insert(x, t)
-        en.insert(x, t + cost)
-        t0[i], t1[i] = t, t + cost
-        end = max(end, t + cost + tail[1][i])
-    return t0, t1, end
+Q = "vspgyd"
 
 
-def links(ops):
-    return [[(j, ops[j]["lat"], o["eng"] != "d" and not ops[j]["eng"] == o["eng"] == "p") for j in o["dep"]] + [(j, 0.0, False) for j in o["ord"]] for o in ops]
-
-
-def rerun(oth, pre, seq, eng):
-    fin = [0.0] * len(oth)
-    free = {e: 0.0 for e in "vspgyd"}
-    end = 0.0
-    near, far = oth[0]["hop"]
-    for i in seq:
-        e = eng[i]
-        t = free[e]
-        for j, lag, wait in pre[i]:
-            u = fin[j] + lag
-            if wait:
-                u += near if eng[j] == e else far
-            if u > t:
-                t = u
-        o = oth[i]
-        t += o["cost"] if e == o["eng"] else o["alt"][1]
-        fin[i] = free[e] = t
-        if t + o["lat"] > end:
-            end = t + o["lat"]
-    return end
-
-
-def pattern(ops, others, pre, suc, eng):
-    m = len(ops)
-    zero, lat = [0.0] * m, [o["lat"] for o in ops]
-    kinds = sorted(set(o["kind"] for o in ops if o["kind"]))
-    members = {k: [i for i in range(m) if ops[i]["kind"] == k] for k in kinds}
-    soon = [0.0] * m
-    for i in range(m):
-        for j, lag, wait in pre[i]:
-            if ops[j]["at"] == ops[i]["at"] and ops[j]["kind"]:
-                soon[i] = max(soon[i], soon[j] + ops[j]["cost"] + lag + 200.0 * wait)
-    time = {k: soon[members[k][len(members[k]) // 2]] + LATE.get(k.rstrip("0123456789"), 0.0) for k in kinds}
-    time.update({k: x for k, x in PLAN.items() if k in time})
-    names = [k for k in time if k in PLAN or not k.startswith(("epp", "kbp", "ofp", "ubp"))]
-    for o in ops:
-        if o["kind"]:
-            time["at%d%d" % o["at"]] = PERIOD * o["at"][0] + LAM * o["at"][1]
-    names += 2 * [k for k in time if k.startswith("at")]
-    cls = [o["kind"] and o["kind"] + CLASS[o["at"][0]][o["at"][1]] for o in ops]
-    queue = {cls[i]: eng[i] for i in range(m) if cls[i] and ops[i]["alt"]}
-    at = [o["kind"] and "at%d%d" % o["at"] for o in ops]
-
-    def value(time, queue):
-        key = [time[a] + time[o["kind"]] if a else 1e9 for a, o in zip(at, ops)]
-        for i in range(m - 1, -1, -1):
-            if not ops[i]["kind"]:
-                key[i] = min([key[j] - lag - 200.0 for j, lag, wait in suc[i]] + [1e9]) - ops[i]["cost"]
-        for i in range(m):
-            for j, lag, wait in pre[i]:
-                if key[i] <= key[j]:
-                    key[i] = key[j] + 1e-3
-        e = [queue.get(k, x) for k, x in zip(cls, eng)]
-        t0, t1, end = place(ops, sorted(range(m), key=lambda i: key[i]), pre, (zero, lat), e)
-        if others:
-            seq = sorted(range(m), key=lambda i: t0[i])
-            end = (end + sum(wt * rerun(oth, opre, seq, e) for oth, opre, wt in others)) / (1.0 + sum(x[2] for x in others))
-        return end, key, e
-
-    rng = np.random.default_rng(SEED)
-    now = best = value(time, queue)
-    for x in range(TRIES):
-        nt, nq = dict(time), dict(queue)
-        u = rng.random(4)
-        if u[0] < 0.15:
-            for k in rng.choice(sorted(queue), 1 + int(u[1] * 2), replace=False):
-                nq[str(k)] = "v" if queue[str(k)] == "s" else "s"
-        else:
-            for k in rng.choice(names, 1 + int(u[1] * u[1] * 3), replace=False):
-                nt[str(k)] += float(rng.normal()) * (STEP[0] if u[2] < 0.5 else STEP[1])
-        new = value(nt, nq)
-        if new[0] < now[0] - WARM * (1.0 - x / TRIES) * math.log(u[3] + 1e-9):
-            now, time, queue = new, nt, nq
-            if now[0] < best[0]:
-                best = now
-                FOUND[:] = [now[0], time, queue]
-    return best[1], best[2]
-
-
-FOUND = []
+def world(ops, weight):
+    depend(ops)
+    pre = [[(j, ops[j]["lat"] + (o["hop"] if o["eng"] != "d" and not ops[j]["eng"] == o["eng"] == "p" else 0.0)) for j in o["dep"]] + [(j, 0.0) for j in o["ord"]] for o in ops]
+    above = []
+    for i, x in enumerate(pre):
+        far = 0
+        for j, lag in x:
+            far |= above[j]
+        pre[i] = [(j, lag) for j, lag in x if ops[j]["lat"] or not far >> j & 1]
+        for j, lag in x:
+            far |= 1 << j
+        above.append(far)
+    suc = [[] for o in ops]
+    for i, x in enumerate(pre):
+        for j, lag in x:
+            suc[j].append((i, lag))
+    cost = [[o["alt"][1] if o["alt"] else o["cost"]] + [o["cost"]] * 5 for o in ops]
+    return pre, suc, cost, [o["lat"] if o["eng"] == "d" else 0.0 for o in ops], weight
 
 
 def spot(slots, t, cost):
@@ -677,28 +487,39 @@ def spot(slots, t, cost):
     return t + cost
 
 
-def tighten(ops, others, pre, key, eng):
+def run(w, seq, eng):
+    pre, suc, cost, lat, wt = w
+    fin, at, end = [0.0] * len(seq), [0.0] * 6, 0.0
+    for i in seq:
+        e = eng[i]
+        t = at[e]
+        for j, lag in pre[i]:
+            u = fin[j] + lag
+            if u > t:
+                t = u
+        fin[i] = at[e] = t = t + cost[i][e]
+        if t + lat[i] > end:
+            end = t + lat[i]
+    return end
+
+
+def tighten(ops, W, start, seed, slack):
     m = len(ops)
-    Q = "vspgyd"
-    eng = [Q.index(e) for e in eng]
-    W = []
-    for oth, opre, wt in [(ops, pre, 1.0)] + others:
-        hop = oth[0]["hop"][1]
-        W.append(([[(j, lag + (hop if wait else 0.0)) for j, lag, wait in x] for x in opre], [[o["alt"][1] if o["alt"] else o["cost"]] + [o["cost"]] * 5 for o in oth],
-                  [o["lat"] if o["eng"] == "d" else 0.0 for o in oth], wt))
-    total = sum(w[3] for w in W)
-    sucs = []
-    for w in W:
-        suc = [[] for i in range(m)]
-        for i in range(m):
-            for j, lag in w[0][i]:
-                suc[j].append((i, lag))
-        sucs.append(suc)
+    pre, suc, cost, lat, wt = W[0]
+    total = sum(w[4] for w in W)
+    eng = [0 if o["onv"] else Q.index(o["eng"]) for o in ops]
+    rank = [0.0] * m
+    for i in range(m - 1, -1, -1):
+        rank[i] = ops[i]["cost"] + max([lag + rank[j] for j, lag in suc[i]] + [lat[i]])
+    key = [LAM * ops[i]["c"] - rank[i] for i in range(m)]
+    for i in range(m):
+        for j, lag in pre[i]:
+            key[i] = max(key[i], key[j] + 1e-3)
     free = [i for i in range(m) if ops[i]["alt"] is not None]
     ends = [i for i in range(m) if ops[i]["eng"] == "d"]
-    rng = np.random.default_rng(SEED)
+    rng = np.random.default_rng(seed)
 
-    def put(seq, before, cost, first, eng):
+    def put(seq, before, first, eng):
         slots = [[] for e in Q]
         fin = [0.0] * m
         for i in seq:
@@ -711,275 +532,47 @@ def tighten(ops, others, pre, key, eng):
             fin[i] = spot(slots[e], t, cost[i][e])
         return fin
 
-    def run(w, seq, eng):
-        before, cost, lat, wt = w
-        fin, at = [0.0] * m, [0.0] * 6
-        for i in seq:
-            e = eng[i]
-            t = at[e]
-            for j, lag in before[i]:
-                u = fin[j] + lag
-                if u > t:
-                    t = u
-            fin[i] = at[e] = t + cost[i][e]
-        return max(fin[i] + lat[i] for i in ends)
-
     zero = [0.0] * m
     best, keep = None, None
-    seq = sorted(range(m), key=lambda i: key[i])
+    seq, eng = start or (sorted(range(m), key=lambda i: key[i]), eng)
     for x in range(ROUNDS):
-        k = x % len(W) if TURN else 0
-        before, cost, lat, wt = W[k]
-        fin = put(seq, before, cost, zero, eng)
-        t0 = [fin[i] - cost[i][eng[i]] for i in range(m)]
-        seq = np.argsort(t0, kind="stable").tolist()
-        end = sum(w[3] * (run(w, seq, eng) if w is not W[k] else max(fin[i] + lat[i] for i in ends)) for w in W) / total
-        if best is None or end < best[1]:
-            best = ([(i, Q[eng[i]], t0[i]) for i in seq], end)
-        if keep is None or end < keep[2] + SLACK * (1.0 - x / ROUNDS):
-            keep = (fin, eng, end)
+        fin = put(seq, pre, zero, eng)
+        own = max(fin[i] + lat[i] for i in ends)
+        if keep is None or own < keep[3] + 1000.0:
+            seq = np.argsort([fin[i] - cost[i][eng[i]] for i in range(m)], kind="stable").tolist()
+            end = (own * wt + sum(w[4] * run(w, seq, eng) for w in W[1:])) / total
+            if best is None or end < best[2]:
+                best = (seq, eng, end)
+            if keep is None or end < keep[2] + slack * (1.0 - x / ROUNDS):
+                keep = (fin, eng, end, own)
         fin, eng = np.array(keep[0]), list(keep[1])
         lo = float(rng.random()) * (float(fin.max()) + WIDE) - WIDE
         near = [i for i in free if lo < fin[i] < lo + WIDE]
         for i in rng.choice(near, int(rng.integers(0, FLIP + 1))).tolist() if near else []:
             eng[i] = 1 - eng[i] if rng.random() < (PV if eng[i] else 1.0) else eng[i]
         back = (-fin + float(rng.choice(AMPS)) * rng.random(m) * ((fin > lo) & (fin < lo + WIDE))).tolist()
-        k = (x + 1) % len(W) if TURN else 0
-        suc = sucs[k]
         for i in range(m - 1, -1, -1):
             b = back[i]
             for j, lag in suc[i]:
                 if back[j] >= b:
                     b = back[j] + 1e-3
             back[i] = b
-        fin = put(np.argsort(back, kind="stable").tolist(), suc, W[k][1], W[k][2], eng)
+        fin = put(np.argsort(back, kind="stable").tolist(), suc, lat, eng)
         seq = np.argsort([-u for u in fin], kind="stable").tolist()
-    return best
+    return best[0], best[1]
 
 
-def schedule(ops, others):
+def refine(ops, W, seq, eng):
     m = len(ops)
-    pre = links(ops)
-    suc = [[] for _ in range(m)]
-    for i in range(m):
-        for j, lag, wait in pre[i]:
-            suc[j].append((i, lag, wait))
-    rank = [0.0] * m
-    for i in range(m - 1, -1, -1):
-        rank[i] = ops[i]["cost"] + max([lag + 120.0 * wait + rank[x] for x, lag, wait in suc[i]] + [ops[i]["lat"]])
-    key = [LAM * ops[i]["c"] - rank[i] for i in range(m)]
-    for i in range(m):
-        for j, lag, wait in pre[i]:
-            key[i] = max(key[i], key[j] + 1e-3)
-    zero, lat = [0.0] * m, [o["lat"] for o in ops]
-    free = [i for i in range(m) if ops[i]["alt"] is not None]
-    rng = np.random.default_rng(SEED)
-    best, keep = None, None
-    eng = ["v" if o["onv"] else o["eng"] for o in ops]
-    if TRIES:
-        key, eng = pattern(ops, others, pre, suc, eng)
-    if FAST:
-        return tighten(ops, others, pre, key, eng)
-    for x in range(ROUNDS):
-        t0, t1, end = place(ops, sorted(range(m), key=lambda i: (key[i], i)), pre, (zero, lat), eng)
-        seq = sorted(range(m), key=lambda i: (t0[i], i))
-        weight = 1.0
-        for oth, opre, wt in others:
-            end += wt * rerun(oth, opre, seq, eng)
-            weight += wt
-        end /= weight
-        if best is None or end < best[1]:
-            best = ([(i, eng[i], t0[i]) for i in seq], end)
-        if keep is None or end < keep[2] + SLACK * (1.0 - x / ROUNDS):
-            keep = (t1, eng, end)
-        t1, eng = keep[0], list(keep[1])
-        for i in rng.choice(free, int(rng.integers(0, FLIP + 1))):
-            eng[int(i)] = "v" if (rng.random() < PV) != bool(ops[int(i)]["onv"]) else "s"
-        lo = float(rng.random()) * t1[seq[-1]]
-        amp = float(rng.choice([0.0, 200.0, 600.0, 1500.0]))
-        back = [-t1[i] + (amp * float(u) if lo < t1[i] < lo + 12000.0 else 0.0) for i, u in enumerate(rng.random(m))]
-        for i in range(m - 1, -1, -1):
-            for j, lag, wait in suc[i]:
-                back[i] = max(back[i], back[j] + 1e-3)
-        b0, b1, _ = place(ops, sorted(range(m), key=lambda i: (back[i], -i)), suc, (lat, zero), eng)
-        key = [-b1[i] for i in range(m)]
-    return best
-
-
-def times(ops, pre, seq, eng, fin, why, start):
-    near, far = ops[0]["hop"]
-    prev = {e: -1 for e in "vspgy"}
-    left = 5
-    for x in range(start - 1, -1, -1):
-        e = eng[seq[x]]
-        if e != "d" and prev[e] < 0:
-            prev[e] = seq[x]
-            left -= 1
-            if left == 0:
-                break
-    busy = sorted((fin[i] - ops[i]["cost"], fin[i], i) for i in seq[:start] if eng[i] == "d")
-    for x in range(start, len(seq)):
-        i = seq[x]
-        e = eng[i]
-        if e == "d":
-            t, w = max((fin[j] + lag, j) for j, lag, wait in pre[i])
-            cost = ops[i]["cost"]
-            k = 0
-            while k < len(busy) and busy[k][0] < t + cost:
-                if busy[k][1] > t:
-                    t, w = busy[k][1], busy[k][2]
-                k += 1
-            busy.insert(k, (t, t + cost, i))
-            fin[i], why[i] = t + cost, w
-            continue
-        w = prev[e]
-        t = fin[w] if w >= 0 else 0.0
-        w = -2 - w
-        for j, lag, wait in pre[i]:
-            u = fin[j] + lag
-            if wait:
-                u += near if eng[j] == e else far
-            if u > t:
-                t, w = u, j
-        o = ops[i]
-        fin[i] = t + (o["cost"] if e == o["eng"] else o["alt"][1])
-        why[i] = w
-        prev[e] = i
-
-
-def polish(worlds, seq, eng):
-    ops, pre = worlds[0][0], worlds[0][1]
-    m = len(ops)
-    up = [set(j for j, _, _ in pre[i]) for i in range(m)]
-    ends = [i for i in range(m) if ops[i]["eng"] == "d"]
-    rng = np.random.default_rng(SEED)
-    draw = rng.random((MOVES, 5))
-    total = sum(w[2] for w in worlds)
-
-    def value(fins):
-        return sum(w[2] * max(f[i] + w[0][i]["lat"] for i in ends) for w, f in zip(worlds, fins)) / total
-
-    fins, whys = [[0.0] * m for w in worlds], [[-1] * m for w in worlds]
-    for w, f, y in zip(worlds, fins, whys):
-        times(w[0], w[1], seq, eng, f, y, 0)
-    now = value(fins)
-    best = (now, list(seq), list(eng))
-    held = None
-    for x in range(MOVES):
-        d = draw[x]
-        if held is None:
-            pos = {i: k for k, i in enumerate(seq)}
-            held = []
-            for w, f, y in zip(worlds, fins, whys):
-                i = max(ends, key=lambda i: f[i] + w[0][i]["lat"])
-                while i >= 0:
-                    j = y[i]
-                    if j <= -2:
-                        j = -2 - j
-                        held.append((j, i))
-                    i = j
-        j, i = held[int(d[0] * len(held))]
-        new, neng = seq, eng
-        if d[1] < 0.25:
-            k = i if d[2] < 0.5 else j
-            if ops[k]["alt"] is None:
-                continue
-            neng = list(eng)
-            neng[k] = "v" if eng[k] == "s" else "s"
-            lo = pos[k]
-        else:
-            lo, hi = pos[j], pos[i]
-            if d[1] < 0.65:
-                more = int(d[2] * d[2] * 6)
-                k = lo - 1
-                while more > 0 and k >= 0:
-                    if eng[seq[k]] == eng[i]:
-                        lo, more = k, more - 1
-                    k -= 1
-                need, go, stay = set(up[i]), [i], []
-                for k in range(hi - 1, lo - 1, -1):
-                    if seq[k] in need:
-                        need |= up[seq[k]]
-                        go.append(seq[k])
-                    else:
-                        stay.append(seq[k])
-                new = seq[:lo] + go[::-1] + stay[::-1] + seq[hi + 1:]
-            else:
-                more = int(d[2] * d[2] * 6)
-                k = hi + 1
-                while more > 0 and k < m:
-                    if eng[seq[k]] == eng[i]:
-                        hi, more = k, more - 1
-                    k += 1
-                late, go, stay = {j}, [j], []
-                for k in range(lo + 1, hi + 1):
-                    if up[seq[k]] & late:
-                        late.add(seq[k])
-                        go.append(seq[k])
-                    else:
-                        stay.append(seq[k])
-                new = seq[:lo] + stay + go + seq[hi + 1:]
-            if new == seq:
-                continue
-        room = -HEAT * (1.0 - x / MOVES) * np.log(d[3] + 1e-9) * total
-        nf, ny, more = [], [], 0.0
-        for w, f, y in zip(worlds, fins, whys):
-            nf.append(list(f))
-            ny.append(list(y))
-            times(w[0], w[1], new, neng, nf[-1], ny[-1], lo)
-            more += w[2] * (max(nf[-1][i] for i in ends) - max(f[i] for i in ends))
-            if more > room + 400.0:
-                break
-        if more <= room:
-            val = value(nf)
-            seq, eng, fins, whys, now, held = new, neng, nf, ny, val, None
-            if now < best[0]:
-                best = (now, list(seq), list(eng))
-    now, seq, eng = best
-    times(ops, pre, seq, eng, fins[0], whys[0], 0)
-    return [(i, eng[i], fins[0][i] - (ops[i]["cost"] if eng[i] == ops[i]["eng"] else ops[i]["alt"][1])) for i in seq], now
-
-
-def plan(g, core, T, topo):
-    ops = build(g, core, T, topo)
-    depend(ops)
-    others = []
-    for par, wt in OTHER:
-        oth = build(g, core, T, topo, par)
-        depend(oth)
-        others.append((oth, links(oth), wt))
-    first = schedule(ops, others)[0]
-    eng = [None] * len(ops)
-    for i, e, _ in first:
-        eng[i] = e
-    return refine([(ops, links(ops), 1.0)] + others, [x[0] for x in first], eng)
-
-
-def refine(worlds, seq, eng):
-    ops = worlds[0][0]
-    m = len(ops)
-    Q = "vspgyd"
-    eng = [Q.index(e) for e in eng]
-    up = [set(j for j, _, _ in worlds[0][1][i]) for i in range(m)]
+    up = [set(j for j, _ in W[0][0][i]) for i in range(m)]
     free = [o["alt"] is not None for o in ops]
-    W = []
-    for oth, pre, wt in worlds:
-        hop = oth[0]["hop"][1]
-        quick = [[(j, lag + (hop if wait else 0.0)) for j, lag, wait in pre[i] if wait or lag or oth[j]["eng"] != oth[i]["eng"] or free[i] or free[j]] for i in range(m)]
-        suc = [[] for i in range(m)]
-        for i in range(m):
-            for j, lag in quick[i]:
-                suc[j].append((i, lag))
-        cost = [[o["alt"][1] if o["alt"] else o["cost"]] + [o["cost"]] * 5 for o in oth]
-        W.append((quick, suc, cost, [o["lat"] if o["eng"] == "d" else 0.0 for o in oth], wt))
     total = sum(w[4] for w in W)
-
     ends = [i for i in range(m) if ops[i]["eng"] == "d"]
 
     def full(w, seq, eng, old=None, lo=0, hi=m):
         pre, suc, cost, lat, wt = w
         fin, why, tail = old[:3] if old else ([0.0] * m, [-1] * m, [0.0] * m)
-        prev, at = [-1] * 6, [0.0] * 6
+        prev = [-1] * 6
         for i in seq[:lo]:
             prev[eng[i]] = i
         at = [fin[i] if i >= 0 else 0.0 for i in prev]
@@ -998,9 +591,7 @@ def refine(worlds, seq, eng):
             at[eng[i]] = tail[i]
         for i in seq[hi::-1]:
             e = eng[i]
-            t = at[e]
-            if lat[i] > t:
-                t = lat[i]
+            t = max(at[e], lat[i])
             for j, lag in suc[i]:
                 u = tail[j] + lag
                 if u > t:
@@ -1039,17 +630,16 @@ def refine(worlds, seq, eng):
                 val = t + tail[i]
         return val
 
-    rng = np.random.default_rng(SEED)
-    draw = rng.random((MOVES, 4)).tolist()
+    draw = np.random.default_rng(SEED).random((MOVES, 4)).tolist()
     state = [full(w, seq, eng) for w in W]
     now = sum(w[4] * s[4] for w, s in zip(W, state)) / total
-    best = (now, list(seq), list(eng))
-    held, took = None, [0]
+    best = (now, seq, eng)
+    held, took = None, 0
     for x in range(MOVES):
         d = draw[x]
         if held is None:
-            took[0] += 1
-            if took[0] % RESORT == 0:
+            took += 1
+            if took % RESORT == 0:
                 fin, cost = state[0][0], W[0][2]
                 seq = sorted(seq, key=lambda i: fin[i] - cost[i][eng[i]])
             pos = [0] * m
@@ -1121,29 +711,32 @@ def refine(worlds, seq, eng):
             now = sum(w[4] * s[4] for w, s in zip(W, state)) / total
             if now < best[0]:
                 best = (now, seq, eng)
-    now, seq, eng = best
-    state = [full(w, seq, eng) for w in W]
-    ENDS[:] = [s[4] for s in state]
-    return [(i, Q[eng[i]], state[0][0][i] - W[0][2][i][eng[i]]) for i in seq], now
+    return best[1], best[2]
 
 
-ENDS = []
+def plan(g, core, T, topo):
+    lists = [build(g, core, T, topo, par) for par, wt in TIMES]
+    W = [world(x, wt) for x, (par, wt) in zip(lists, TIMES)]
+    order = None
+    for seed, slack in STAGES:
+        order = tighten(lists[0], W, order, seed, slack)
+    return refine(lists[0], W, order[0], order[1])
 
 
-ORDER = {}
+ORDER = []
 
 
 def rank_program(g, core, T, topo):
     if T.rank_of(core) is None:
         return
-    if "o" not in ORDER:
-        ORDER["o"] = plan(g, core, T, topo)[0]
-    ops = build(g, core, T, topo)
+    if not ORDER:
+        ORDER.extend(plan(g, core, T, topo))
+    ops = build(g, core, T, topo, TIMES[0][0])
     depend(ops)
-    order = [x[0] for x in ORDER["o"] if x[1] != "d"]
-    for i, e, _ in ORDER["o"]:
-        if ops[i]["eng"] != e:
-            ops[i]["eng"], ops[i]["fn"] = e, ops[i]["alt"][0]
+    order = [i for i in ORDER[0] if ops[i]["eng"] != "d"]
+    for o, e in zip(ops, ORDER[1]):
+        if o["eng"] != Q[e]:
+            o["eng"], o["fn"] = Q[e], o["alt"][0]
     pos = {i: x for x, i in enumerate(order)}
     queue = {"v": g.vector, "s": g.scalar, "p": g.tensor, "g": g, "y": g.sync}
     seen = {}

import math
import numpy as np
import comms_topo
from concourse.bass import DstId, RemoteDMATransfer
from concourse.mybir import dt, AluOpType, AxisListType, ActivationFunctionType

ALU = AluOpType
ACT = ActivationFunctionType
C, V, VX, STEPS = 512, 2048, 4096, 4
NCH, CW, M = 2, 256, 128
MARKS = (0, 64, 128)
SHORT, ALONE = (0, 48, 96, 128), ()
QUICK = ((3, 1),)
HRG = False
GPC = 2
NA = 4
PG = 4
NE = 8
KW = 8 * 17
LUT = 296
LAM = 1000.0
STAGES = ((6, 130.0), (16, 50.0))
ROUNDS, WIDE, AMPS, FLIP, PV = 3500, 6000.0, (100.0, 400.0, 1000.0, 2500.0), 2, 0.7
MOVES, HEAT, REACH, RESORT, SPAN = 35000, 12.0, 150, 8, 40
SEED = 2


def buffers():
    bf, hf, fl = "bfloat16", "float16", "float32"
    b = {}
    for dtype, sizes in (
            ("int32", {"book": 6144, "ai": C, "thi": 8, "wi": 8, "pi": 8, "pj": 8}),
            ("uint16", {"off": C, "lu": 64 * NCH, "bl": 16}),
            (bf, {"tab": 8208, "yy": CW, "hr": 768, "sg": C, "mk": 2 * C, "jj": 128, "jl": 256, "jh": 128, "jd": 128, "tk": 256, "jb": 16, "jm": KW, "jg": KW, "jx": KW,
                  "ib": 128, "ineg": 128, "i16": 128, "ibig": 128, "ibn": 128, "wblk": 128, "wneg": 128, "wc": 32, "bigc": 128, "czb": 160,
                  "eq": KW, "hb": 2 * KW, "rs": 2 * KW, "dx": 32, "bn": KW, "dm": 128, "lt": 256, "ut": LUT, "st": LUT}),
            (hf, {"ih": 128, "ihn": 128, "o15": 128, "iha": KW, "ck": 2 * KW, "cep": KW, "czh": 224, "czc": 32, "thn": 8}),
            (fl, {"km": 16 * NCH, "af": C, "ll": 256 * NCH, "bs": 192, "col": 16, "loc": 32, "mj": 16, "cnt": 8, "onp": 128, "onn": 128})):
        for name, k in sizes.items():
            b[name] = ("sbuf", [128, k], dtype)
    for i in range(NCH):
        b["xg%d" % i] = ("sbuf", [128, 24 * CW + 32], bf)
        b["mx%d" % i] = ("sbuf", [128, 24 * CW], bf)
        b["g2%d" % i] = ("sbuf", [128, 4112], fl)
        b["so%d" % i] = ("sbuf", [128, 4 * KW], fl)
        b["rst%d" % i] = ("sbuf", [128, 4 * KW], fl)
    for i in range(STEPS):
        b["say%d" % i] = ("sbuf", [128, C], bf)
        b["up%d" % i] = ("sbuf", [128, C], bf)
    for i in range(STEPS + 1):
        b["a%d" % i] = ("sbuf", [128, 2 * C], hf)
        b["h%d" % i] = ("sbuf", [128, C], bf)
    for x in ("of0", "of1", "ep0", "ep1", "yb", "xb", "kb", "ub"):
        b[x] = ("psum", [128, 512], fl)
    return b


SCRATCH = buffers()
SEMAPHORES = ["cv", "cs", "cp", "cg", "sent"] + ["d%d" % _i for _i in range(11 + 6 * NCH)] + ["arr%d_%d" % (_t, _c) for _t in range(STEPS) for _c in range(NCH)]

TIMES = [((0.83, 0.43, 1.56, 3.8, 200.0, 700.0, 1400.0), 1.0),
         ((0.83 * 1.45, 0.43 * 1.45, 1.9, 5.0, 250.0, 1200.0, 2000.0), 0.3),
         ((0.83 * 1.2, 0.43 * 1.2, 1.1, 2.0, 300.0, 1500.0, 2500.0), 0.25)]
FIX, SFIX, DL, RATE, GI, FIRST = 5.0, 10.0, 1600.0, 350.0, 300.0, 2000.0
YBANK = "ub"


def build(g, core, T, topo, par):
    CY, PCY, GA, SC, HOP, RL, RB = par
    ops = []
    cores = list(T.cores)
    n = len(cores)
    rank = T.rank_of(core)
    v, s, p, y = g.vector, g.scalar, g.tensor, g.sync
    now, nd = [0], [0]

    def op(eng, fn, rd, wr, cost, banks=(), lat=0.0, sem=None, alt=None, onv=0):
        ops.append({"onv": onv, "ord": [], "alt": alt, "c": now[0], "eng": eng, "fn": fn, "rd": list(rd), "wr": list(wr), "bk": list(banks),
                    "cost": cost * (1.25 if eng == "g" and sem is None else 1.0) + (SFIX if eng == "s" and sem is None else 0.0), "lat": lat, "sem": sem, "hop": HOP})

    def vc(k, f=1.0):
        return max(64.0, k * f) * CY + FIX

    def gat(k):
        return 60.0 + k * GA * CY

    def ts(out, in0, s1, s2, o0, o1, rd, wr, k, f=1.0, banks=()):
        if o1 is None:
            op("v", lambda: v.tensor_scalar(out, in0, s1, None, o0), rd, wr, vc(k, f), banks)
        else:
            op("v", lambda: v.tensor_scalar(out, in0, s1, s2, o0, o1), rd, wr, vc(k, f), banks)

    def tt(out, in0, in1, o, rd, wr, cost):
        op("v", lambda: v.tensor_tensor(out, in0, in1, o), rd, wr, cost)

    def cp(out, in_, rd, wr, cost, banks=()):
        op("v", lambda: v.tensor_copy(out, in_), rd, wr, cost, banks)

    def ms(ap, val, wr, k, f=1.0):
        op("v", lambda: v.memset(ap, val), [], wr, vc(k, f))

    def scan(out, d0, d1, o0, o1, rd, wr, k, f=1.0, banks=()):
        op("v", lambda: v.tensor_tensor_scan(out, d0, d1, 0.0, o0, o1), rd, wr, vc(k, f), banks)

    def act(out, in_, fn, rd, wr, cost, banks=(), bias=0.0, acc=None):
        op("s", lambda: s.activation(out, in_, fn, bias=bias, accum_out=acc), rd, wr, cost, banks)

    def either(onv, out, in_, rd, wr, cost_s, cost_v, add=None, banks=(), mul=None):
        if mul is not None:
            op("s", lambda: s.activation(out, in_, ACT.Identity, scale=mul), rd, wr, cost_s, banks,
               alt=(lambda: v.tensor_scalar(out, in_, mul, None, ALU.mult), cost_v), onv=onv)
        elif add is None:
            op("s", lambda: s.activation(out, in_, ACT.Copy), rd, wr, cost_s, banks, alt=(lambda: v.tensor_copy(out, in_), cost_v), onv=onv)
        else:
            op("s", lambda: s.activation(out, in_, ACT.Identity, bias=add), rd, wr, cost_s, banks,
               alt=(lambda: v.tensor_scalar(out, in_, add, None, ALU.add), cost_v), onv=onv)

    def mm(out, lhs, rhs, st, sp, rd, bank, k, f=1.0):
        op("p", lambda: p.matmul(out, lhs, rhs, st, sp), rd, [bank], max(64.0, k) * f * PCY)

    def mms(calls, rd, wr, banks, k):
        op("p", lambda: [p.matmul(*x) for x in calls][-1], rd, wr, len(calls) * max(64.0, k) * PCY, banks)

    def io(out, pat, base, cm, wr, k, flt=True):
        if flt:
            op("g", lambda: g.iota(out, pat, base, cm, allow_small_or_imprecise_dtypes=True), [], wr, 130.0 + 2 * k * CY)
        else:
            op("g", lambda: g.iota(out, pat, base, cm), [], wr, 130.0 + 2 * k * CY)

    def sel(out, in_, pat, o, fill, base, cm, rd, wr, k):
        op("g", lambda: g.affine_select(out, in_, pat, o, fill, base, cm), rd, wr, 170.0 + 2 * k * CY)

    def flight(q, fn, rd, wr, cost, lat, busy, sem):
        op(q, fn, rd, wr, cost, lat=lat, sem=sem)
        op("d", None, rd, wr, busy, sem=sem)

    def dma(q, out, in_, rd, wr, nbytes):
        sem = "d%d" % nd[0]
        nd[0] += 1
        e = y if q == "y" else s
        flight(q, lambda: e.dma_start(out, in_), rd, wr, 60.0, DL, 240.0 + nbytes / RATE, (sem, 16))

    dma("s", T.wi[:, 0:1], T.w[:], [], ["wi"], 512)
    dma("y", T.h0[:, 0:CW], T.heard[:, 0:CW], [], ["h0_0"], 256 * CW)
    dma("s", T.ai[:, 0:CW], T.scroll[:, 0:CW], [], ["ai_0"], 512 * CW)
    dma("y", T.tab[:, 2048:4104], T.cues[:, 2040:4096], [], ["tab1"], 1 << 19)
    dma("y", T.tab[:, 4104:6160], T.cues[:, 0:2056], [], ["tab0"], 1 << 19)
    dma("y", T.h0[:, CW:C], T.heard[:, CW:C], [], ["h0_1"], 256 * CW)
    dma("y", T.ai[:, CW:C], T.scroll[:, CW:C], [], ["ai_1"], 512 * CW)
    dma("y", T.thi[:, 0:1], T.th[:], [], ["thi"], 512)
    dma("y", T.tab[:, 6160:8200], T.cues[:, 2056:4096], [], ["tab2"], 1 << 19)
    dma("y", T.book[:, 0:2048], T.spare[:], [], ["spare"], 1 << 20)
    dma("y", T.book[:, 2048:4096], T.spare[:], [], ["gap"], 1 << 20)
    for i, j in ((2, 0), (3, 1), (4, 3), (5, 4), (6, 5), (7, 6), (8, 7), (9, 8), (10, 9)):
        ops[2 * i]["ord"].append(2 * j)
    for i in range(1, 11):
        ops[2 * i + 1]["ord"].append(2 * i - 1)

    io(T.pi[:, 0:1], [[0, 1]], 0, 1, ["pi"], 1, False)
    io(T.jh[:], [[1, 8], [0, 16]], 0, 0, ["jh"], 128)
    io(T.jj[:], [[1, 128]], 0, 0, ["jj"], 128)
    io(T.jl[:], [[0, 16], [1, 16]], 0, 0, ["jl"], 256)
    io(T.jd[:], [[0, 8], [1, 8], [0, 2]], 0, 0, ["jd"], 128)
    io(T.jb[:, 0:8], [[17, 8]], 15, 0, ["jb"], 8)
    io(T.tk[:], [[1, 16], [-1, 16]], 0, 0, ["tk"], 256)
    io(T.loc[:], [[16, 32]], 16, 1, ["loc"], 32)
    io(T.jg[:], [[1, 8], [0, 17]], 0, 0, ["jg"], KW)
    io(T.jx[:], [[16, 8], [1, 17]], 0, 0, ["jx"], KW)
    sel(T.jm[:], T.jg[:], [[0, 8], [-1, 17]], ALU.is_ge, -1.0, 15 - NA, 0, ["jg"], ["jm"], KW)
    col = lambda j: T.col[:, j:j + 1]
    PF, LANE, GRP, P7, P8, P1, WF, L15, G16, PAR8, THF, L17, PARW = range(13)
    cp(col(PF), T.pi[:, 0:1], ["pi"], ["pf"], vc(1))
    for j, (o, k) in enumerate(((ALU.bitwise_and, 15), (ALU.arith_shift_right, 4), (ALU.bitwise_and, 7), (ALU.arith_shift_right, 3), (ALU.bitwise_and, 1))):
        ts(T.pj[:, j:j + 1], T.pi[:, 0:1], k, None, o, None, ["pi"], ["pj%d" % j], 1)
    cp(T.col[:, 1:3], T.pj[:, 0:2], ["pj0", "pj1"], ["col"], vc(2))
    cp(T.col[:, 3:6], T.pj[:, 2:5], ["pj2", "pj3", "pj4"], ["col2"], vc(3))
    cp(col(WF), T.wi[:, 0:1], ["wi"], ["wf"], vc(1))
    ts(T.wblk[:], T.jh[:], col(GRP), col(WF), ALU.is_equal, ALU.mult, ["jh", "col", "wf"], ["wblk"], 128, 0.5)
    either(1, T.wneg[:], T.wblk[:], ["wblk"], ["wneg"], vc(128), vc(64), mul=-1.0)
    ts(T.ih[:], T.jj[:], col(PF), None, ALU.is_equal, None, ["jj", "pf"], ["ih"], 128, 0.5)
    for name, k in (("ihn", -1.0), ("ib", 1.0), ("i16", -16.0), ("ibig", 2.0 ** 15), ("ibn", -2.0 ** 15), ("ineg", -1.0)):
        ts(T[name][:], T.jj[:], col(PF), k, ALU.is_equal, ALU.mult, ["jj", "pf"], [name], 128, 0.5)
    ms(T.bigc[:], 1.5 * 2.0 ** 20, ["bigc"], 128, 0.5)
    for c in range(NCH):
        cp(T.a0[:, 2 * c * CW + 1:2 * (c + 1) * CW:2], T.ai[:, c * CW:(c + 1) * CW], ["ai_%d" % c], ["a0_%d" % c], vc(CW))
    io(T.mk[:, 0::2], [[0, C]], 0, 0, ["mkz"], C)
    either(0, T.wc[:, 0:8], T.wblk[:, 0::16], ["wblk"], ["wc0"], vc(8), vc(8), mul=-65536.0)
    either(0, T.wc[:, 8:16], T.wblk[:, 0::16], ["wblk"], ["wc1"], vc(8), vc(8), mul=65536.0)
    ts(T.wc[:, 16:24], T.jj[:, 0:8], col(GRP), 128.0, ALU.is_equal, ALU.mult, ["jj", "col"], ["wc2"], 8)
    ts(col(L15), col(LANE), -15.0, 1.0 / 16.0, ALU.add, ALU.mult, ["col"], ["l15"], 1)
    ts(col(L17), col(L15), 17.0, None, ALU.mult, None, ["l15"], ["l17"], 1)
    ts(col(G16), col(GRP), -16.0, None, ALU.mult, None, ["col"], ["g16"], 1)
    ts(col(PAR8), col(P1), 8.0, None, ALU.mult, None, ["col2"], ["par8"], 1)
    ts(col(PARW), col(P1), 2.0 * KW, None, ALU.mult, None, ["col2"], ["parw"], 1)
    ts(T.thn[:, 0:1], T.thi[:, 0:1], -2.0, 1023.0, ALU.mult, ALU.add, ["thi"], ["thn"], 1)
    cp(col(THF), T.thn[:, 0:1], ["thn"], ["thf"], vc(1))
    DX = ["dx0", "dx1"]
    for f, k in enumerate((2.0 ** 20, 2.0 ** 11)):
        ts(T.hb[:, KW * f:KW * f + KW], T.jm[:], col(GRP), k, ALU.is_equal, ALU.mult, ["jm", "col"], ["hb%d" % f], KW, 0.5)
        ts(T.dx[:, 8 * f:8 * f + 8], T.jj[:, 0:8], col(GRP), k, ALU.is_equal, ALU.mult, ["jj", "col"], ["dx%d" % f], 8)
    either(0, T.dx[:, 16:32], T.dx[:, 0:16], DX, ["dmx"], vc(16), vc(16), mul=-2.0)
    ts(T.eq[:], T.jg[:], col(GRP), -128.0, ALU.is_equal, ALU.mult, ["jg", "col"], ["eq"], KW, 0.5)
    sel(T.rs[:, KW:2 * KW], T.eq[:], [[16, 8], [1, 17]], ALU.not_equal, 15.0 * 128.0, 0, -1, ["eq"], ["rs1"], KW)
    either(0, T.rs[:, 0:KW], T.rs[:, KW:2 * KW], ["rs1"], ["rs0"], vc(KW), vc(KW, 0.5), mul=16.0)
    ts(T.iha[:], T.jx[:], col(PF), 0.0625, ALU.is_equal, ALU.mult, ["jx", "pf"], ["iha"], KW, 0.5)
    for f, (j, x) in enumerate(((L17, "l17"), (L15, "l15"))):
        ts(T.ck[:, KW * f:KW * f + KW], T.iha[:], col(j), -30.0 / 256.0, ALU.mult, ALU.add, ["iha", x], ["ck%d" % f], KW, 0.5)
    ms(T.bn[:], 1.5 * 2.0 ** 38, ["bn"], KW, 0.5)
    ts(T.cep[:], T.iha[:], col(THF), 256.0, ALU.mult, ALU.mult, ["iha", "thf"], ["cep"], KW, 0.5)
    ms(T.o15[:], 2.0 ** 15, ["o15"], 128, 0.5)
    io(T.onp[:], [[0, 128]], 1, 0, ["onp"], 128)
    io(T.onn[:], [[0, 128]], -1, 0, ["onn"], 128)
    ms(T.rst0[:], -1.0e9, ["rst_0"], 4 * KW)
    either(0, T.rst1[:], T.rst0[:], ["rst_0"], ["rst_1"], vc(4 * KW), vc(4 * KW))
    ts(T.dm[:], T.jd[:], col(P7), None, ALU.is_equal, None, ["jd", "col2"], ["dm"], 128, 0.5)
    ts(T.bl[:, 0:8], T.jb[:, 0:8], col(PARW), None, ALU.add, None, ["jb", "parw"], ["bl0"], 8)
    ts(T.bl[:, 8:16], T.jj[:, 0:8], col(PAR8), None, ALU.add, None, ["jj", "par8"], ["bl8"], 8)
    ts(T.bs[:, 0:48], T.jl[:, 0:48], col(P8), -16.0, ALU.is_equal, ALU.mult, ["jl", "col2"], ["bs0"], 48)
    for at, k, x in ((48, 48, -1.0), (96, 32, -2.0 ** -21), (128, 16, 0.0), (144, 16, 2.0 ** -11), (160, 16, -2.0 ** -20), (176, 16, -2.0 ** -11)):
        either(0, T.bs[:, at:at + k], T.bs[:, 0:k], ["bs0"], ["bs%d" % at], vc(k), vc(k), mul=x)
    for at, k, e in ((0, 48, 19), (48, 32, 17), (80, 32, 8), (112, 32, 36), (144, 16, 13)):
        ms(T.czb[:, at:at + k], 1.5 * 2.0 ** e, ["czb%d" % at], k, 0.5)
    for at, k, x in ((0, 48, 0.0), (48, 16, 128.0), (64, 48, 1023.5), (112, 16, 32.0), (128, 16, -255.5), (144, 16, 7.75), (160, 16, -2047.0 / 4096.0),
                     (176, 32, 32768.0), (208, 16, -15.0)):
        ms(T.czh[:, at:at + k], x, ["czh%d" % at], k, 0.5)
    ts(T.czc[:], T.loc[:], col(G16), None, ALU.add, None, ["loc", "g16"], ["czc"], 32)
    ms(T.hr[:], 0.0, ["hr%d_%d" % (c, b) for c in range(NCH) for b in range(2)], 768, 0.5)
    ms(T.xg0[:, 32::3], 0.0, ["xr0"], 8 * CW, 0.5)
    either(0, T.xg1[:, 32::3], T.xg0[:, 32::3], ["xr0"], ["xr1"], vc(8 * CW), vc(8 * CW, 0.5))
    ms(T.ut[:, 0:16], 0.0, ["ut1"], 16)
    ms(T.ut[:, 16:40], 1.0, ["ut2"], 24)
    ts(T.lt[:], T.jl[:], col(LANE), None, ALU.is_lt, None, ["jl", "col"], ["lt"], 256, 0.5)
    mm(T.kb[:, 0:256], T.ib[:], T.tk[:], True, False, ["ib", "tk"], "kb", 256)
    mm(T.kb[:, 0:256], T.i16[:], T.lt[:], False, True, ["i16", "lt"], "kb", 256)
    ts(T.ut[:, 33:289], T.kb[:, 0:256], col(LANE), 0.0, ALU.add, ALU.is_ge, ["col", "ut2"], ["ut0"], 256, 1.0, ["kb"])
    ts(T.st[:, 0:16], T.jl[:, 0:16], col(LANE), 1.0, ALU.is_gt, ALU.add, ["jl", "col"], ["st1"], 16)
    ms(T.st[:, 16:40], 0.0, ["st2"], 24)
    ts(T.st[:, 33:289], T.jl[:], col(LANE), None, ALU.is_ge, None, ["jl", "col", "st2"], ["st0"], 256, 0.5)
    ms(T.st[:, 48:289:16], 0.0, ["st0"], 16)
    for e in range(2):
        either(e, T.tab[:, e:2048:2], T.tab[:, 4105 - e:6152:2], ["tab0"], ["sw%d" % e], vc(1024), vc(512), -64.0)

    KB, UB = T.kb, T.ub
    for t in range(STEPS):
        last = t == STEPS - 1
        H, A, AN = T["h%d" % t], T["a%d" % t], T["a%d" % (t + 1)]
        dst = cores[(rank + 1 + t % (n - 1)) % n]
        src = cores[(rank - 1 - t % (n - 1)) % n]
        for c in range(NCH):
            now[0] = c
            c0 = c * CW
            cs = slice(c0, c0 + CW)
            hh, a, an = "h%d_%d" % (t, c), "a%d_%d" % (t, c), "a%d_%d" % (t + 1, c)
            X, MX, SO, RST, KM = T["xg%d" % c], T["mx%d" % c], T["so%d" % c], T["rst%d" % c], T.km[:, 16 * c:16 * c + 16]
            r = lambda name: "%s_%d" % (name, c)
            par2 = lambda buf, b: buf[:, c0 + b:c0 + CW:2]
            even, odd, both = slice(2 * c0, 2 * c0 + 2 * CW, 2), slice(2 * c0 + 1, 2 * c0 + 2 * CW, 2), slice(2 * c0, 2 * c0 + 2 * CW)
            AB = lambda b: A[:, 2 * c0 + 1 + 2 * b:2 * c0 + 2 * CW:4]
            r0 = 3 * c0 // 2
            HR = lambda b: T.hr[:, r0 + b:r0 + 3 * M:3]
            hr = ["hr%d_%d" % (c, b) for b in range(2)]
            for b in range(2):
                of = "of%d" % b
                O = T[of][:, 0:M]
                if t == 0:
                    mm(O, T.ihn[:], AB(b), True, False, ["ihn", a], of, M)
                    mm(O, T.wneg[:], par2(H, b), False, False, ["wneg", hh], of, M)
                    mm(O, T.ibig[:], T.bigc[:], False, False, ["ibig", "bigc"], of, M)
                else:
                    mm(O, T.ibig[:], T.bigc[:], True, False, ["ibig", "bigc"], of, M)
                    mm(O, T.wneg[:], par2(H, b), False, False, ["wneg", hh], of, M)
                mm(O, T.ibn[:], T.bigc[:], False, False, ["ibn", "bigc"], of, M)
                mm(O, T.wblk[:], par2(H, b), False, False, ["wblk", hh], of, M)
                mm(O, T.ih[:], AB(b), False, True, ["ih", a], of, M)
                ts(T.off[:, c0 + M * b:c0 + M * b + M], O, 2056.0, None, ALU.add, None, [], [r("off%d" % b)], M, 1.0, [of])
            if HRG:
                sel(HR(0), par2(H, 0), [[0, M]], ALU.is_ge, 0.0, 0, 0, [hh], [hr[0]], M)
            else:
                either(0, HR(0), par2(H, 0), [hh], [hr[0]], vc(M), vc(M, 0.5))
            either(0, HR(1), par2(H, 1), [hh], [hr[1]], vc(M), vc(M, 0.5), 32.0)
            CP = T.of1[:, 128:160]
            half = lambda b: T.of1[:, 128 + 16 * b:136 + 16 * b]
            calls = [(CP, T.ih[:], T.czh[:, 176:208], True, False)] + [(half(b), par2(H, b), T.wc[:, 0:8], False, False) for b in range(2)]
            calls += [(CP, L[:], T.czb[:, 112:144], False, False) for L in (T.ibig, T.ibn)]
            calls += [(half(b), par2(H, b), T.wc[:, 8:16], False, b == 1 and t == 0) for b in range(2)]
            if t > 0:
                calls += [(half(b), par2(T.sg, b), T.wc[:, 16:24], False, b == 1) for b in range(2)]
            mms(calls, ["ih", "czh176", hh, "wc0", "wc1", "wc2", "ibig", "ibn", "czb112"] + ([r("sg")] if t else []), ["of1"], [], 16)
            either(0, RST[:, 0::17], CP, [], [r("rst")], vc(16), vc(16), 2.0 ** 28 - 4032.0, ["of1"])
            xs = [[], []]
            mxs = [[] for i in range(16 - NA)]
            abs_ = []
            wide = 4112 if t == 0 else 6152
            j0 = 16 - NA
            marks, gpc = (SHORT, 1) if (t, c) in ALONE else (MARKS, GPC)
            for e in range(len(marks) - 1):
                u0, u1 = marks[e], marks[e + 1]
                cut = [[], []]
                for b in range(2):
                    for w in range(gpc):
                        w0, w1 = u0 + (u1 - u0) * w // gpc, u0 + (u1 - u0) * (w + 1) // gpc
                        cut[b].append("x%d_%d_%d" % (c, b, w0))
                        k = (w1 - w0) * 16
                        either(b if (t, c) in ALONE else t + c + e == 0 and w == 1, X[:, 16 * b + 48 * w0:16 * b + 48 * w1:3], T.tab[:, 2048:2048 + wide].indirect(T.off[:, c0 + M * b + w0:c0 + M * b + w1]),
                               ["tab0", "tab1", r("off%d" % b)] + (["tab2"] if t else []), cut[b][-1:], gat(k), gat(k), 32.0 if b else None)
                    xs[b] += cut[b]
                for i in range(j0):
                    mxs[i].append("mx%d_%d_%d" % (c, i, e))
                    k = 3 * (u1 - u0)
                    scan(MX[:, 3 * M * i + 3 * u0:3 * M * i + 3 * u1], X[:, 3 * i + 48 * u0:3 * i + 48 * u0 + 16 * k - 15:16], T.hr[:, r0 + 3 * u0:r0 + 3 * u1],
                         ALU.max, ALU.min, cut[0] + cut[1] + ["xr%d" % c] + hr, [mxs[i][e]], k, 0.5)
                yb = ("yb", "xb")[e % 2]
                k = (u1 - u0) * 2 * NA
                for b in range(2):
                    calls = []
                    for j in range(NA):
                        o_ = T[yb][:, b * NA + j:k:2 * NA]
                        x0 = 16 * b + 3 * (j0 + j)
                        calls.append((o_, T.ineg[:], T.hr[:, r0 + b + 3 * u0:r0 + 3 * u1:3], True, False))
                        calls.append((o_, T.ib[:], X[:, x0 + 48 * u0:x0 + 48 * u1 - 47:48], False, True))
                    mms(calls, ["ineg", "ib", hr[b]] + cut[b], [yb], [], u1 - u0)
                m0 = 3 * M * j0 + 2 * NA * u0
                abs_.append("ab%d_%d" % (c, e))
                act(MX[:, m0:m0 + k], T[yb][:, 0:k], ACT.Abs, [], abs_[-1:], vc(k), [yb])
            for b in range(2):
                ep = "ep%d" % b
                EP = T[ep]
                E, EN, EF = EP[:, 0:2 * KW], EP[:, 0:KW], EP[:, KW:2 * KW]
                EI = lambda i: EP[:, i:2 * KW:17]
                XP = lambda i: X[:, 16 * b + 3 * i:16 * b + 3 * i + 48 * M - 47:48]
                mm(E, HR(b), T.hb[:], True, False, [hr[b], "hb0", "hb1"], ep, 2 * KW)
                mms([(EN, T.o15[:], T.cep[:], False, False)], ["o15", "cep"], [], [ep], KW)
                for i0 in range(0, j0, PG):
                    mms([(EI(i), XP(i), T.dx[:, 0:16], False, False) for i in range(i0, min(j0, i0 + PG))], xs[b] + DX, [], [ep], 16)
                for i in range(j0):
                    mms([(EI(i), MX[:, 3 * M * i + b:3 * M * (i + 1):3], T.dx[:, 16:32], False, False)], mxs[i] + ["dmx"], [], [ep], 16)
                mms([(EI(j0 + j), MX[:, 3 * M * j0 + b * NA + j:3 * M * j0 + CW * NA:2 * NA], T.dx[:, 0:16], False, False) for j in range(NA)], abs_ + DX, [], [ep], 16)
                for f, O in ((1, EF), (0, EN)):
                    fs = slice(KW * f, KW * f + KW)
                    calls = [(O, T.o15[:], T.ck[:, fs], False, False)] + ([(O, par2(T.sg, b), T.rs[:, fs], False, False)] if t else [])
                    rd = ["o15", "ck%d" % f] + ([r("sg"), "rs%d" % f] if t else [])
                    if f:
                        mms(calls, rd, [], [ep], KW)
                    else:
                        calls += [(EF, AB(b), T.iha[:], False, False), (EN, AB(b), T.iha[:], False, True)]
                        mms([(O, L[:], T.bn[:], False, False) for L in (T.ibig, T.ibn)] + calls, rd + ["ibig", "ibn", "bn", a, "iha"], [ep], [], KW)
                s0 = 2 * KW * b
                scan(SO[:, s0:s0 + 2 * KW], RST[:, s0:s0 + 2 * KW], E, ALU.max, ALU.min, [r("rst")], [r("so%d" % b)], 2 * KW, 1.0, [ep])
                tt(T.km[:, 16 * c + 8 * b:16 * c + 8 * b + 8], SO[:, s0 + 15:s0 + KW:17], SO[:, s0 + KW + 15:s0 + 2 * KW:17], ALU.min, [r("so%d" % b)], [r("km%d" % b)], vc(16))
            so, km = [r("so0"), r("so1")], [r("km0"), r("km1")]
            LA, LT = T.ll[:, 256 * c:256 * c + 128], T.ll[:, 256 * c + 128:256 * c + 256]
            tt(LA, SO[:].indirect(T.bl[:, 0:8]), T.dm[:], ALU.mult, so + ["bl0", "dm"], [r("la")], gat(128))
            tt(LT, KM.indirect(T.bl[:, 8:16]), T.dm[:], ALU.mult, km + ["bl8", "dm"], [r("lt")], gat(128))
            lo = 16 if t == 0 else 0
            rnd = lambda k0, k1, at: [(KB[:, k0:k1], L[:], T.czb[:, at + k0:at + k1], False, False) for L in (T.ibig, T.ibn)]
            mm(KB[:, 0:64], T.ih[:], T.czh[:, 0:64], True, False, ["ih", "czh0", "czh48"], "kb", 64)
            mm(KB[:, lo:64], LA, T.bs[:, 96 + lo:160], False, False, [r("la"), "bs96", "bs128", "bs144"], "kb", 64, 4.0)
            mms(rnd(0, 64, 0) + [(KB[:, 0:64], T.ih[:], T.czh[:, 64:128], False, False)], ["ibig", "ibn", "czb0", "czb48", "ih", "czh64", "czh112"], ["kb"], [], 64)
            mm(KB[:, 0:48], LT, T.bs[:, 0:48], False, False, [r("lt"), "bs0"], "kb", 64, 4.0)
            mms(rnd(0, 48, 0), ["ibig", "ibn", "czb0"], ["kb"], [], 64)
            mm(KB[:, 32:64], LA, T.bs[:, 160:192], False, False, [r("la"), "bs160", "bs176"], "kb", 32, 4.0)
            mm(KB[:, 0:48], LT, T.bs[:, 48:96], False, False, [r("lt"), "bs48"], "kb", 64, 4.0)
            mms([(KB[:, 16:64], T.ih[:], T.czh[:, 128:176], False, False)] + rnd(16, 64, 48) + [(KB[:, 16:32], T.ih[:], T.czc[:, 16 * c:16 * c + 16], False, True)],
                ["ih", "ibig", "ibn", "czb48", "czb80", "czh128", "czh144", "czh160", "czc"], ["kb"], [], 64)
            cp(T.lu[:, 64 * c:64 * c + 64], KB[:, 0:64], [], [r("lu")], vc(64), ["kb"])
            lbk, lgw, lsp, liu = [T.lu[:, 64 * c + 16 * i:64 * c + 16 * i + 16] for i in range(4)]
            UP, SAY, YY = T["up%d" % t][:, cs], T["say%d" % t][:, cs], T[YBANK][:, 256:256 + CW]
            up, say, arr = "up%d_%d" % (t, c), "say%d_%d" % (t, c), "arr%d_%d" % (t, c)
            cue, tabs = T.tab[:, 0:8200].indirect(lsp), ["tab0", "tab1", "tab2", "sw0", "sw1", r("lu")]
            either((t, c) not in QUICK, UP, cue, tabs, [up], gat(CW), gat(CW), 64.0)
            if (t, c) in QUICK:
                tt(T.yy[:], cue, H[:, cs], ALU.subtract, tabs + [hh], ["yy"], gat(CW))
                act(SAY, T.yy[:], ACT.Abs, ["yy"], [say], vc(CW))
            else:
                mm(YY, T.ineg[:], H[:, cs], True, False, ["ineg", hh], YBANK, CW)
                mm(YY, T.ib[:], UP, False, True, ["ib", up], YBANK, CW)
                act(SAY, YY, ACT.Abs, [], [say], vc(CW), [YBANK], -64.0)
            rid, pid, _ = topo.addr(dst)
            use = topo.engines(core, dst)[:NE]
            send = RemoteDMATransfer(dst_ids=[DstId(rid=rid, pnc=pid)], dma_engine_mask=sum(1 << e for e in use), remote_sem=T.sem[arr],
                                     srcs=[SAY, UP], dsts=[T["h%d" % (t + 1)][:, cs]], alu_op=3)
            flight("g", lambda x=send: g.remote_dma_fused([x], local_sem=T.sem["sent"]), [say, up], ["h%d_%d" % (t + 1, c)],
                   GI, RL + (FIRST if t + c == 0 else 0.0), RB, (arr, len(topo.engines(src, core)[:NE]), len(use)))
            tt(A[:, even], T.book[:, 0:2048 if t == 0 else 4096].indirect(lbk), A[:, odd], ALU.subtract, [r("lu"), "spare", a] + (["gap"] if t else []), [r("tt")], gat(CW))
            either(0, T.mk[:, odd], T.ut[:, 0:289].indirect(liu), ["ut0", "ut1", "ut2", "mkz", r("lu")], [r("mk")], gat(CW), gat(CW))
            scan(AN[:, both], T.mk[:, both], A[:, both], ALU.mult, ALU.add, [r("mk"), r("tt"), a], [an], 2 * CW, 0.5)
            if last:
                act(T.af[:, cs], AN[:, odd], ACT.Copy, [an], [r("af")], vc(CW) + 10.0)
                dma("y", T.ys[:, cs], T.af[:, cs], [r("af")], [r("ys")], CW * 512)
                dma("y", T.yh[:, cs], T["h%d" % STEPS][:, cs], ["h%d_%d" % (STEPS, c)], [r("yh")], CW * 256)
                G2 = T["g2%d" % c]
                g2 = ["g2%d_%d" % (c, e) for e in range(4)]
                cp(G2[:].indirect(lgw), A[:, odd], [r("lu"), a], g2, 60.0 + CW * SC * CY)
                for e in range(4):
                    dma("y" if e % 2 == 0 or c < NCH - 1 else "s", T.yg[:, e * 512 + c0:e * 512 + c0 + CW], G2[:, 16 + e * 512 + c0:16 + e * 512 + c0 + CW],
                        [g2[e]], ["yg%d_%d" % (c, e)], CW * 512)
            else:
                either(0, T.sg[:, cs], T.st[:, 0:289].indirect(liu), ["st0", "st1", "st2", r("lu")], [r("sg")], gat(CW), gat(CW))
                act(T.mj[:], KM, ACT.Sign, km, ["mj", r("cnt")], vc(16) + 20.0, (), 3839.0 * 128.0 + 1.0 / 32.0, T.cnt[:, c:c + 1])
        if not last:
            for c in range(NCH):
                cp(T.book[:, 2032:6144].indirect(T.lu[:, 64 * c + 16:64 * c + 32]), A[:, 2 * c * CW + 1:2 * (c + 1) * CW:2],
                   ["lu_%d" % c, "a%d_%d" % (t, c)], ["gap", "spare"], 60.0 + CW * SC * CY)
            if t == STEPS - 2:
                for c in range(NCH):
                    for e in range(4):
                        at = e * 512 + c * CW
                        sel(T["g2%d" % c][:, 16 + at:16 + at + CW], T.book[:, 2048 + at:2048 + at + CW], [[0, CW]], ALU.is_ge, 0.0, 0, 0, ["gap"], ["g2%d_%d" % (c, e)], CW)
            MC = UB[:, 32:33]
            mm(MC, T.ih[:], T.czh[:, 208:209], True, False, ["ih", "czh208"], "ub", 1)
            for x in ("onn", "onp"):
                for c in range(NCH):
                    mm(MC, T[x][:], T.cnt[:, c:c + 1], False, False, [x, "cnt_%d" % c], "ub", 1, 4.0)
                if x == "onn":
                    mms([(MC, L[:], T.czb[:, 144:145], False, False) for L in (T.ibig, T.ibn)], ["ibig", "ibn", "czb144"], ["ub"], [], 1)
            mm(MC, T.ih[:], T.thn[:, 0:1], False, True, ["ih", "thn"], "ub", 1)
            ts(T.cep[:], T.iha[:], MC, 256.0, ALU.mult, ALU.mult, ["iha"], ["cep"], KW, 0.5, ["ub"])
    return ops


def depend(ops):
    lw, rds = {}, {}
    for i, o in enumerate(ops):
        d = set()
        for x in o["rd"]:
            if x in lw:
                d.add(lw[x])
        for x in o["bk"]:
            if x in lw:
                d.add(lw[x])
            for j in rds.get(x, []):
                if ops[j]["eng"] != o["eng"] or o["alt"] is not None or ops[j]["alt"] is not None:
                    d.add(j)
        for x in o["wr"]:
            if x in lw:
                d.add(lw[x])
            d.update(rds.get(x, []))
        d.discard(i)
        o["dep"] = sorted(d)
        for x in o["rd"] + o["bk"]:
            rds.setdefault(x, []).append(i)
        for x in o["wr"]:
            lw[x] = i
            rds[x] = []


Q = "vspgyd"


def world(ops, weight):
    depend(ops)
    pre = [[(j, ops[j]["lat"] + (o["hop"] if o["eng"] != "d" and not ops[j]["eng"] == o["eng"] == "p" else 0.0)) for j in o["dep"]] + [(j, 0.0) for j in o["ord"]] for o in ops]
    above = []
    for i, x in enumerate(pre):
        far = 0
        for j, lag in x:
            far |= above[j]
        pre[i] = [(j, lag) for j, lag in x if ops[j]["lat"] or not far >> j & 1]
        for j, lag in x:
            far |= 1 << j
        above.append(far)
    suc = [[] for o in ops]
    for i, x in enumerate(pre):
        for j, lag in x:
            suc[j].append((i, lag))
    cost = [[o["alt"][1] if o["alt"] else o["cost"]] + [o["cost"]] * 5 for o in ops]
    return pre, suc, cost, [o["lat"] if o["eng"] == "d" else 0.0 for o in ops], weight


def spot(slots, t, cost):
    lo, hi = 0, len(slots) >> 1
    if hi and slots[-1] > t:
        while lo < hi:
            md = (lo + hi) >> 1
            if slots[2 * md + 1] <= t:
                lo = md + 1
            else:
                hi = md
        x, n = 2 * lo, len(slots)
        while x < n and slots[x] < t + cost - 1e-6:
            if slots[x + 1] > t:
                t = slots[x + 1]
            x += 2
        slots[x:x] = (t, t + cost)
    else:
        slots += (t, t + cost)
    return t + cost


def run(w, seq, eng):
    pre, suc, cost, lat, wt = w
    fin, at, end = [0.0] * len(seq), [0.0] * 6, 0.0
    for i in seq:
        e = eng[i]
        t = at[e]
        for j, lag in pre[i]:
            u = fin[j] + lag
            if u > t:
                t = u
        fin[i] = at[e] = t = t + cost[i][e]
        if t + lat[i] > end:
            end = t + lat[i]
    return end


def tighten(ops, W, start, seed, slack):
    m = len(ops)
    pre, suc, cost, lat, wt = W[0]
    total = sum(w[4] for w in W)
    eng = [0 if o["onv"] else Q.index(o["eng"]) for o in ops]
    rank = [0.0] * m
    for i in range(m - 1, -1, -1):
        rank[i] = ops[i]["cost"] + max([lag + rank[j] for j, lag in suc[i]] + [lat[i]])
    key = [LAM * ops[i]["c"] - rank[i] for i in range(m)]
    for i in range(m):
        for j, lag in pre[i]:
            key[i] = max(key[i], key[j] + 1e-3)
    free = [i for i in range(m) if ops[i]["alt"] is not None]
    ends = [i for i in range(m) if ops[i]["eng"] == "d"]
    rng = np.random.default_rng(seed)

    def put(seq, before, first, eng):
        slots = [[] for e in Q]
        fin = [0.0] * m
        for i in seq:
            t = first[i]
            for j, lag in before[i]:
                u = fin[j] + lag
                if u > t:
                    t = u
            e = eng[i]
            fin[i] = spot(slots[e], t, cost[i][e])
        return fin

    zero = [0.0] * m
    best, keep = None, None
    seq, eng = start or (sorted(range(m), key=lambda i: key[i]), eng)
    for x in range(ROUNDS):
        fin = put(seq, pre, zero, eng)
        own = max(fin[i] + lat[i] for i in ends)
        if keep is None or own < keep[3] + 1000.0:
            seq = np.argsort([fin[i] - cost[i][eng[i]] for i in range(m)], kind="stable").tolist()
            end = (own * wt + sum(w[4] * run(w, seq, eng) for w in W[1:])) / total
            if best is None or end < best[2]:
                best = (seq, eng, end)
            if keep is None or end < keep[2] + slack * (1.0 - x / ROUNDS):
                keep = (fin, eng, end, own)
        fin, eng = np.array(keep[0]), list(keep[1])
        lo = float(rng.random()) * (float(fin.max()) + WIDE) - WIDE
        near = [i for i in free if lo < fin[i] < lo + WIDE]
        for i in rng.choice(near, int(rng.integers(0, FLIP + 1))).tolist() if near else []:
            eng[i] = 1 - eng[i] if rng.random() < (PV if eng[i] else 1.0) else eng[i]
        back = (-fin + float(rng.choice(AMPS)) * rng.random(m) * ((fin > lo) & (fin < lo + WIDE))).tolist()
        for i in range(m - 1, -1, -1):
            b = back[i]
            for j, lag in suc[i]:
                if back[j] >= b:
                    b = back[j] + 1e-3
            back[i] = b
        fin = put(np.argsort(back, kind="stable").tolist(), suc, lat, eng)
        seq = np.argsort([-u for u in fin], kind="stable").tolist()
    return best[0], best[1]


def refine(ops, W, seq, eng):
    m = len(ops)
    up = [set(j for j, _ in W[0][0][i]) for i in range(m)]
    free = [o["alt"] is not None for o in ops]
    total = sum(w[4] for w in W)
    ends = [i for i in range(m) if ops[i]["eng"] == "d"]

    def full(w, seq, eng, old=None, lo=0, hi=m):
        pre, suc, cost, lat, wt = w
        fin, why, tail = old[:3] if old else ([0.0] * m, [-1] * m, [0.0] * m)
        prev = [-1] * 6
        for i in seq[:lo]:
            prev[eng[i]] = i
        at = [fin[i] if i >= 0 else 0.0 for i in prev]
        for i in seq[lo:]:
            e = eng[i]
            t, y = at[e], -2 - prev[e]
            for j, lag in pre[i]:
                u = fin[j] + lag
                if u > t:
                    t, y = u, j
            fin[i] = at[e] = t + cost[i][e]
            why[i] = y
            prev[e] = i
        at = [0.0] * 6
        for i in seq[:hi:-1]:
            at[eng[i]] = tail[i]
        for i in seq[hi::-1]:
            e = eng[i]
            t = max(at[e], lat[i])
            for j, lag in suc[i]:
                u = tail[j] + lag
                if u > t:
                    t = u
            tail[i] = at[e] = t + cost[i][e]
        end = max(ends, key=lambda i: fin[i] + lat[i])
        return fin, why, tail, end, fin[end] + lat[end]

    def guess(w, st, win, neng, lo, hi):
        pre, suc, cost, lat, wt = w
        fin, tail = list(st[0]), st[2]
        at = [0.0] * 6
        for i in seq[max(0, lo - REACH):lo]:
            at[eng[i]] = fin[i]
        val = 0.0
        for i in win:
            e = neng[i]
            t = at[e]
            for j, lag in pre[i]:
                u = fin[j] + lag
                if u > t:
                    t = u
            fin[i] = at[e] = t = t + cost[i][e]
            if t + lat[i] > val:
                val = t + lat[i]
        for i in seq[hi + 1:hi + 1 + REACH]:
            e = eng[i]
            t = at[e]
            at[e] = 0.0
            for j, lag in pre[i]:
                if pos[j] <= hi:
                    u = fin[j] + lag
                    if u > t:
                        t = u
            if t + tail[i] > val:
                val = t + tail[i]
        return val

    draw = np.random.default_rng(SEED).random((MOVES, 4)).tolist()
    state = [full(w, seq, eng) for w in W]
    now = sum(w[4] * s[4] for w, s in zip(W, state)) / total
    best = (now, seq, eng)
    held, took = None, 0
    for x in range(MOVES):
        d = draw[x]
        if held is None:
            took += 1
            if took % RESORT == 0:
                fin, cost = state[0][0], W[0][2]
                seq = sorted(seq, key=lambda i: fin[i] - cost[i][eng[i]])
            pos = [0] * m
            for k, i in enumerate(seq):
                pos[i] = k
            held = []
            for s in state:
                i, why = s[3], s[1]
                while i >= 0:
                    j = why[i]
                    if j <= -2:
                        j = -2 - j
                        held.append((j, i))
                    i = j
        j, i = held[int(d[0] * len(held))]
        neng = eng
        if d[1] < 0.25:
            k = i if d[2] < 0.5 else j
            if not free[k]:
                continue
            neng = list(eng)
            neng[k] = 1 - eng[k]
            lo = hi = pos[k]
            if d[1] < 0.1:
                near = [u for u in seq[max(0, lo - SPAN):lo + SPAN] if free[u] and eng[u] == neng[k]]
                if not near:
                    continue
                u = near[int(d[1] * 10.0 * len(near))]
                neng[u] = eng[k]
                lo, hi = min(lo, pos[u]), max(lo, pos[u])
            win = seq[lo:hi + 1]
        else:
            lo, hi = pos[j], pos[i]
            more = int(d[2] * d[2] * 6)
            if d[1] < 0.65:
                k = lo - 1
                while more > 0 and k >= 0:
                    if eng[seq[k]] == eng[i]:
                        lo, more = k, more - 1
                    k -= 1
                need, go, stay = set(up[i]), [i], []
                for k in range(hi - 1, lo - 1, -1):
                    if seq[k] in need:
                        need |= up[seq[k]]
                        go.append(seq[k])
                    else:
                        stay.append(seq[k])
                win = go[::-1] + stay[::-1]
            else:
                k = hi + 1
                while more > 0 and k < m:
                    if eng[seq[k]] == eng[i]:
                        hi, more = k, more - 1
                    k += 1
                late, go, stay = {j}, [j], []
                for k in range(lo + 1, hi + 1):
                    if up[seq[k]] & late:
                        late.add(seq[k])
                        go.append(seq[k])
                    else:
                        stay.append(seq[k])
                win = stay + go
            if win == seq[lo:hi + 1]:
                continue
        room = now - HEAT * (1.0 - x / MOVES) * math.log(d[3] + 1e-9)
        if sum(w[4] * guess(w, s, win, neng, lo, hi) for w, s in zip(W, state)) / total <= room:
            seq, eng, held = seq[:lo] + win + seq[hi + 1:], neng, None
            state = [full(w, seq, eng, s, lo, hi) for w, s in zip(W, state)]
            now = sum(w[4] * s[4] for w, s in zip(W, state)) / total
            if now < best[0]:
                best = (now, seq, eng)
    return best[1], best[2]


def plan(g, core, T, topo):
    lists = [build(g, core, T, topo, par) for par, wt in TIMES]
    W = [world(x, wt) for x, (par, wt) in zip(lists, TIMES)]
    order = None
    for seed, slack in STAGES:
        order = tighten(lists[0], W, order, seed, slack)
    return refine(lists[0], W, order[0], order[1])


ORDER = []


def rank_program(g, core, T, topo):
    if T.rank_of(core) is None:
        return
    if not ORDER:
        ORDER.extend(plan(g, core, T, topo))
    ops = build(g, core, T, topo, TIMES[0][0])
    depend(ops)
    order = [i for i in ORDER[0] if ops[i]["eng"] != "d"]
    for o, e in zip(ops, ORDER[1]):
        if o["eng"] != Q[e]:
            o["eng"], o["fn"] = Q[e], o["alt"][0]
    pos = {i: x for x, i in enumerate(order)}
    queue = {"v": g.vector, "s": g.scalar, "p": g.tensor, "g": g, "y": g.sync}
    seen = {}
    for i in order:
        o = ops[i]
        need = {}
        o["w"] = []
        for j in o["dep"]:
            d = ops[j]
            if d["sem"] is not None:
                if (o["eng"], d["sem"][0]) not in seen:
                    seen[(o["eng"], d["sem"][0])] = 1
                    o["w"].append(j)
            elif not (d["eng"] == "p" and o["eng"] == "p"):
                if d["eng"] not in need or pos[j] > pos[need[d["eng"]]]:
                    need[d["eng"]] = j
        for e, j in need.items():
            if pos[j] > seen.get((o["eng"], e), -1):
                seen[(o["eng"], e)] = pos[j]
                ops[j]["inc"] = True
                o["w"].append(j)
    count = {e: 0 for e in "vspg"}
    for i in order:
        o = ops[i]
        if o.get("inc"):
            count[o["eng"]] += 1
            o["n"] = count[o["eng"]]
    sent = 0
    for i in order:
        o = ops[i]
        qu = queue[o["eng"]]
        for j in o["w"]:
            d = ops[j]
            if d["sem"] is not None:
                qu.wait_ge(T.sem[d["sem"][0]], d["sem"][1])
            else:
                qu.wait_ge(T.sem["c" + d["eng"]], d["n"])
        ins = o["fn"]()
        if o["sem"] is not None:
            if len(o["sem"]) == 3:
                sent += o["sem"][2]
            else:
                ins.then_inc(T.sem[o["sem"][0]], 16)
        elif o.get("inc"):
            ins.then_inc(T.sem["c" + o["eng"]], 1)
    g.wait_ge(T.sem["sent"], sent)
    waited = set(x[1] for x in seen)
    for o in ops:
        if o["sem"] is not None and o["sem"][0] not in waited:
            g.wait_ge(T.sem[o["sem"][0]], o["sem"][1])
